import numpy as np
import ml_dtypes


def mxq(x, axis, fmt="e4m3"):
    dtype, down = {"e4m3": (ml_dtypes.float8_e4m3fn, 7), "e5m2": (ml_dtypes.float8_e5m2, 14)}[fmt]
    v = np.moveaxis(np.asarray(x, np.float32).astype(ml_dtypes.bfloat16).astype(np.float64), axis, -1)
    blocks = v.reshape(v.shape[:-1] + (-1, 32))
    amax = np.abs(blocks).max(-1, keepdims=True)
    byte = np.maximum(np.where(amax > 0, np.frexp(amax)[1] - 1 + 127, 0) - down, 1)
    scale = np.exp2(byte - 127.0)
    codes = (blocks / scale).astype(np.float32).astype(dtype).astype(np.float64)
    return np.moveaxis((codes * scale).reshape(v.shape), -1, axis)


WIDE = False


def mx_kscale(k):
    if not WIDE:
        return np.ones(k)
    levels = np.array([30, -30])
    if k % 512:
        return np.exp2(np.random.permutation(np.resize(levels, k // 32))).repeat(32)
    a = np.empty((k // 512, 16))
    for p in range(k // 512):
        a[p, :8] = np.random.permutation(np.resize(levels, 8))
        for g in range(8):
            far = levels[np.abs(levels - a[p, g]) >= 10]
            a[p, g + 8] = far[np.random.randint(len(far))]
    return np.exp2(a.ravel()).repeat(32)


def f64(x):
    return np.asarray(x).astype(np.float64)


def striped(idx):
    return np.tile(idx.reshape(-1, 16).T, (8, 1)).astype(np.uint16)


def unstriped(offs):
    return offs[:16].T.reshape(-1).astype(np.int64)


def bf(x):
    return np.asarray(x, np.float32).astype(ml_dtypes.bfloat16)


E2M1 = np.array([0.0, 0.5, 1.0, 1.5, 2.0, 3.0, 4.0, 6.0, -0.0, -0.5, -1.0, -1.5, -2.0, -3.0, -4.0, -6.0])


def pack_weight(w, fmt):
    k, n = w.shape
    w = f64(bf(w)).reshape(k // 32, 32, n)
    amax = np.abs(w).max(1)
    if fmt in ("e4m3", "e5m2"):
        byte = np.frexp(amax)[1] - 1 + 127 - (7 if fmt == "e4m3" else 14)
    else:
        mant, ex = np.frexp(amax / 6.0)
        byte = np.where(mant > 0.5, ex, ex - 1) + 127
    byte = np.clip(np.where(amax > 0, byte, 1), 1, 254)
    scaled = (w * np.exp2(127.0 - byte)[:, None, :]).reshape(k, n).astype(np.float32)
    by_word = np.ascontiguousarray(scaled.reshape(k // 512, 128, 4, n).transpose(0, 1, 3, 2))
    if fmt in ("e4m3", "e5m2"):
        words = by_word.astype(ml_dtypes.float8_e4m3fn if fmt == "e4m3" else ml_dtypes.float8_e5m2).view(np.uint8)
    else:
        c = by_word.astype(ml_dtypes.float4_e2m1fn).view(np.uint8) & 0xF
        words = c[..., 0::2] | (c[..., 1::2] << 4)
    return np.ascontiguousarray(words), np.ascontiguousarray(byte.astype(np.uint8).reshape(k // 512, 16, n))


def unpack_weight(words, scales, fmt):
    g, p, n, _ = words.shape
    if fmt in ("e4m3", "e5m2"):
        vals = np.ascontiguousarray(words).view(ml_dtypes.float8_e4m3fn if fmt == "e4m3" else ml_dtypes.float8_e5m2).astype(np.float64)
    else:
        nib = np.empty((g, p, n, 4), np.uint8)
        nib[..., 0::2] = words & 0xF
        nib[..., 1::2] = words >> 4
        vals = E2M1[nib]
    vals = vals * np.repeat(np.exp2(scales.astype(np.float64) - 127.0), 8, axis=1)[..., None]
    return vals.transpose(0, 1, 3, 2).reshape(g * 512, n)


K, H, N, T, S, T2 = 1024, 1024, 512, 2048, 1024, 2048

def setup_inputs():
    n = np.random.standard_normal
    s = mx_kscale(K)[:, None]
    u = mx_kscale(H)[:, None]
    tab_words, tab_scales = pack_weight(n((K, T)) * np.exp(1.0 * n((1, T))) * s, "e5m2")
    w1_words, w1_scales = pack_weight(n((K, H)) / np.sqrt(K) / s * u.T, "e4m3")
    return {
        "tab_words": tab_words,
        "tab_scales": tab_scales,
        "offs": striped(np.random.permutation(T)[:S]),
        "w1_words": w1_words,
        "w1_scales": w1_scales,
        "sT": np.tanh(n((H, T))).astype(np.float32),
        "w2": (1.5 * n((H, N)) / np.sqrt(H) / u).astype(np.float32),
        "wgo": np.exp(0.3 * n((128, S))).astype(np.float32),
        "offs2": striped(np.random.permutation(T2)[:S]),
    }

def reference(tab_words, tab_scales, offs, w1_words, w1_scales, sT, w2, wgo, offs2):
    v = unpack_weight(tab_words, tab_scales, "e5m2")[:, unstriped(offs)]
    w1 = unpack_weight(w1_words, w1_scales, "e4m3")
    b = w1.T @ v
    saved = f64(sT)[:, unstriped(offs)]
    h = b * ((1.0 - saved) * (1.0 + saved))
    y = mxq(f64(w2), 0, "e4m3").T @ mxq(h, 0, "e4m3")
    m = np.log1p(y * y)
    out = np.zeros((N, T2))
    out[:, unstriped(offs2)] = np.tile(f64(wgo), (N // 128, 1)) * m
    return out

@@ -1,0 +1,269 @@
+from contextlib import ExitStack
+
+import concourse.mybir as mybir
+
+K, H, N, T, S, T2 = 1024, 1024, 512, 2048, 1024, 2048
+FLOPS = 2 * K * H * S + 2 * H * N * S
+
+F32 = mybir.dt.float32
+BF16 = mybir.dt.bfloat16
+I32 = mybir.dt.int32
+U32 = mybir.dt.uint32
+U16 = mybir.dt.uint16
+U8 = mybir.dt.uint8
+E4M3X4 = mybir.dt.float8_e4m3fn_x4
+E5M2X4 = mybir.dt.float8_e5m2_x4
+ALU = mybir.AluOpType
+ACT = mybir.ActivationFunctionType
+
+P = 128
+PACK = 4
+PASS = P * PACK
+HALF = 512
+LIST_COLS = HALF // 16
+
+
+def tile_list_hit_sensitivity_map_kernel(
+    tc, tab_words, tab_scales, offs, w1_words, w1_scales, sT, w2, wgo, offs2, out
+):
+    nc = tc.nc
+    with ExitStack() as ctx:
+        keep = ctx.enter_context(tc.tile_pool(name="keep", bufs=1))
+        ring = ctx.enter_context(tc.tile_pool(name="ring", bufs=2))
+        psum1 = ctx.enter_context(tc.psum_pool(name="psum1", bufs=5))
+        psum2 = ctx.enter_context(tc.psum_pool(name="psum2", bufs=3))
+
+        def held(shape, dtype, name, tag=""):
+            return keep.tile(shape, dtype, name=name, tag=tag or name, align_bytes=64)
+
+        idx = keep.tile([P, S // 16], U16, name="idx")
+        idx2 = keep.tile([P, S // 16], U16, name="idx2")
+        tab_bytes = held([P, T], U8, name="tab_bytes")
+        w1_bytes_raw = held([P, 2, H // 4], I32, name="w1_bytes_raw")
+        v_planes = held([P, 2 * S // 4], I32, name="v_planes")
+        pages = [held([P, T2], F32, name="page0")]
+
+        nc.vector.memset(tab_bytes[:].bitcast(I32)[32:64, :], 0)
+        nc.vector.memset(tab_bytes[:].bitcast(I32)[64:128, :], 0)
+        nc.vector.memset(w1_bytes_raw[:], 0)
+        nc.vector.memset(v_planes[:], 0)
+        nc.vector.memset(pages[0][:], 0.0)
+
+        def rows_of(x, b, t):
+            return x[PASS * b : PASS * (b + 1), :].rearrange("(g t i) c -> t g i c", t=PACK, i=8)[t]
+
+        saved = {}
+        w2_raw = {}
+
+        def load_saved(u, after):
+            saved[u] = held([P, T], F32, name="saved%d" % u, tag=after)
+            nc.sync.dma_start(out=saved[u][:], in_=rows_of(sT, u // PACK, u % PACK))
+
+        def load_w2(b, after):
+            w2_raw[b] = held([P, PACK, N], F32, name="w2_raw%d" % b, tag=after)
+            for t in range(PACK):
+                nc.sync.dma_start(out=w2_raw[b][:, t, :], in_=rows_of(w2, b, t))
+
+        nc.sync.dma_start(idx[:], offs)
+        nc.sync.dma_start(
+            out=tab_bytes[:].bitcast(I32)[0:32, :], in_=tab_scales.rearrange("a q t -> (a q) t").bitcast(I32)
+        )
+        tab = [held([P, T], I32, name="tab%d" % a) for a in range(2)]
+        for a in range(2):
+            nc.sync.dma_start(out=tab[a][:], in_=tab_words[a].rearrange("p t i -> p (t i)").bitcast(I32))
+        nc.sync.dma_start(idx2[:], offs2)
+        for q in range(4):
+            nc.gpsimd.dma_start(
+                out=w1_bytes_raw[32 * q : 32 * q + 4, :, :],
+                in_=w1_scales[:, 4 * q : 4 * q + 4, :].bitcast(I32).rearrange("a r c -> r a c"),
+            )
+        load_saved(0, "saved0")
+        load_saved(1, "saved1")
+
+        v_bytes = held([P, S], U8, name="v_bytes")
+        nc.vector.tensor_copy(v_bytes[:], tab_bytes[:].indirect(idx[:]))
+        for a in range(2):
+            for q in range(4):
+                nc.scalar.dma_start(
+                    out=v_planes[32 * q : 32 * q + 4, S // 4 * a : S // 4 * (a + 1)],
+                    in_=v_bytes[:].bitcast(I32)[16 * a + 4 * q : 16 * a + 4 * q + 4, :],
+                )
+        v_scale = [v_planes[:].bitcast(U8)[:, S * a : S * (a + 1)] for a in range(2)]
+        v_words = [held([P, S], U32, name="v_words%d" % a) for a in range(2)]
+        for a in range(2):
+            nc.vector.tensor_copy(v_words[a][:], tab[a][:].bitcast(U32).indirect(idx[:]))
+
+        load_saved(2, "tab0")
+        w1_raw = held([P, 2, H], I32, name="w1_raw", tag="tab1")
+        nc.sync.dma_start(out=w1_raw[:], in_=w1_words.rearrange("a p c i -> p a (c i)").bitcast(I32))
+
+        w1_cols = held([P, 2 * H], I32, name="w1_cols")
+
+        def order_w1():
+            w1_bytes = held([P, 2 * H // 4], I32, name="w1_bytes", tag="saved0")
+            nc.vector.tensor_copy(
+                out=w1_bytes[:].rearrange("p (ab t g i) -> p ab t g i", ab=4, t=PACK, i=2),
+                in_=w1_bytes_raw[:].rearrange("p a (b g t i) -> p (a b) t g i", b=2, t=PACK, i=2),
+            )
+            nc.vector.tensor_copy(
+                out=w1_cols[:].rearrange("p (ab t g i) -> p ab t g i", ab=4, t=PACK, i=8),
+                in_=w1_raw[:].rearrange("p a (b g t i) -> p (a b) t g i", b=2, t=PACK, i=8),
+            )
+            return w1_bytes
+
+        squares = {}
+        h_rows = {}
+        h_codes = {}
+        h_scale = {}
+        w2_codes = {}
+        w2_scale = {}
+
+        def pick(u, halves, picked=None):
+            lo, hi = halves[0], halves[-1] + 1
+            if picked is None:
+                picked = held([P, HALF * len(halves)], F32, name="picked%d%d" % (u, lo))[:]
+            nc.vector.tensor_copy(picked, saved[u][:].indirect(idx[:, LIST_COLS * lo : LIST_COLS * hi]))
+            nc.scalar.activation(picked, picked, ACT.Square)
+            for j in halves:
+                squares[u, j] = picked[:, HALF * (j - lo) : HALF * (j - lo + 1)]
+
+        def back(u, j):
+            b, t = divmod(u, PACK)
+            acc = psum1.tile([P, HALF], F32, name="acc1")
+            for a in range(2):
+                cols = slice(H * a + P * u, H * a + P * (u + 1))
+                nc.tensor.matmul_mx(
+                    out=acc[:],
+                    lhsT=w1_cols[:, cols].bitcast(E4M3X4),
+                    lhsT_scale=w1_bytes[:].bitcast(U8)[:, cols],
+                    rhs=v_words[a][:, HALF * j : HALF * (j + 1)].bitcast(E5M2X4),
+                    rhs_scale=v_scale[a][:, HALF * j : HALF * (j + 1)],
+                    start=(a == 0),
+                    stop=(a == 1),
+                )
+            if t == 0:
+                tag = "h_rows10" if b == 1 else "h_rows0%d" % j
+                h_rows[b, j] = held([P, PACK, HALF], BF16, name="h_rows%d%d" % (b, j), tag=tag)
+            nc.vector.scalar_tensor_tensor(
+                out=h_rows[b, j][:, t, :], in0=squares[u, j], scalar=1.0, in1=acc[:], op0=ALU.subtract, op1=ALU.mult
+            )
+
+        def weave(rows, name, after=None):
+            woven = held([P, HALF, PACK], BF16, name=name + "_woven", tag=after or name + "_woven")
+            nc.scalar.copy(
+                out=woven[:].rearrange("p (c i) t -> p c t i", i=4),
+                in_=rows[:].rearrange("p t (c i) -> p c t i", i=4),
+            )
+            return woven
+
+        def quantise(woven, name):
+            codes = held([P, HALF], U32, name=name + "_codes")
+            scale = held([P, HALF], U8, name=name + "_scale")
+            nc.vector.quantize_mx(
+                out=codes[:].bitcast(E4M3X4), scales=scale[:], in_=woven[:].rearrange("p c t -> p (c t)")
+            )
+            return codes, scale
+
+        logs = [held([P, S], F32, name="logs%d" % n) for n in range(4)]
+
+        def forward(n, j):
+            acc = psum2.tile([P, HALF], F32, name="acc2")
+            cols = slice(P * n, P * (n + 1))
+            for b in range(2):
+                nc.tensor.matmul_mx(
+                    out=acc[:],
+                    lhsT=w2_codes[b][:, cols].bitcast(E4M3X4),
+                    lhsT_scale=w2_scale[b][:, cols],
+                    rhs=h_codes[b, j][:].bitcast(E4M3X4),
+                    rhs_scale=h_scale[b, j][:],
+                    start=(b == 0),
+                    stop=(b == 1),
+                )
+            y2 = ring.tile([P, HALF], F32, name="y2")
+            nc.scalar.activation(y2[:], acc[:], ACT.Square)
+            nc.scalar.activation(logs[n][:, HALF * j : HALF * (j + 1)], y2[:], ACT.Ln, bias=1.0)
+
+        def place(n, halves):
+            lo, hi = halves[0], halves[-1] + 1
+            cols = slice(HALF * lo, HALF * hi)
+            nc.vector.tensor_tensor(
+                pages[n % 3][:].indirect(idx2[:, LIST_COLS * lo : LIST_COLS * hi]),
+                logs[n][:, cols],
+                gains[:, cols],
+                ALU.mult,
+            )
+
+        def store(n):
+            nc.sync.dma_start(out=out[P * n : P * (n + 1), :], in_=pages[n % 3][:])
+
+        def finish_h(b, j, after=None):
+            name = "h%d%d" % (b, j)
+            h_codes[b, j], h_scale[b, j] = quantise(weave(h_rows[b, j], name, after), name)
+
+        def new_page(after):
+            page = held([P, T2], F32, name="page%d" % len(pages), tag=after)
+            nc.gpsimd.memset(page[:], 0.0)
+            pages.append(page)
+
+        pick(0, (0, 1))
+        pick(1, (0, 1))
+        load_saved(3, "saved1")
+        pick(2, (0, 1))
+        load_saved(4, "tab0")
+        w1_bytes = order_w1()
+        load_w2(0, "tab1")
+        pick(3, (0, 1))
+        load_saved(5, "saved1")
+        back(0, 0)
+        back(0, 1)
+        load_saved(6, "picked00")
+        pick(4, (0, 1))
+        load_w2(1, "tab0")
+        back(1, 0)
+        back(1, 1)
+        load_saved(7, "picked10")
+        w2_woven0 = weave(w2_raw[0], "w20")
+        pick(5, (0,))
+        back(2, 0)
+        back(2, 1)
+        gains = held([P, S], F32, name="gains", tag="picked20")
+        nc.sync.dma_start(out=gains[:], in_=wgo)
+        pick(6, (0,))
+        back(3, 0)
+        back(3, 1)
+        w2_codes[0], w2_scale[0] = quantise(w2_woven0, "w20")
+        w2_woven1 = weave(w2_raw[1], "w21")
+        for u in range(4, 7):
+            back(u, 0)
+        pick(7, (0,))
+        pick(7, (1,))
+        finish_h(0, 0)
+        w2_codes[1], w2_scale[1] = quantise(w2_woven1, "w21")
+        back(7, 0)
+        finish_h(1, 0)
+        late = held([P, S], F32, name="late", tag="picked70")
+        pick(5, (1,), late[:, :HALF])
+        pick(6, (1,), late[:, HALF:])
+        back(4, 1)
+        new_page("picked40")
+        back(5, 1)
+        back(6, 1)
+        new_page("picked70")
+        back(7, 1)
+        forward(0, 0)
+        forward(1, 0)
+        place(0, (0,))
+        place(1, (0,))
+        finish_h(0, 1, "picked71")
+        finish_h(1, 1)
+        forward(2, 0)
+        place(2, (0,))
+        for n in range(3):
+            forward(n, 1)
+        forward(3, 0)
+        forward(3, 1)
+        for n in range(3):
+            place(n, (1,))
+            store(n)
+        place(3, (0, 1))
+        store(3)

@@ -39,56 +39,59 @@ def tile_list_hit_sensitivity_map_kernel(
         idx = keep.tile([P, S // 16], U16, name="idx")
         idx2 = keep.tile([P, S // 16], U16, name="idx2")
         tab_bytes = held([P, T], U8, name="tab_bytes")
-        w1_bytes_raw = held([P, 2, H // 4], I32, name="w1_bytes_raw")
-        v_planes = held([P, 2 * S // 4], I32, name="v_planes")
+        w1_bytes = held([P, H], U8, name="w1_bytes")
+        planes = held([P, 2, (S + H) // 4], I32, name="planes")
         pages = [held([P, T2], F32, name="page0")]
 
-        nc.vector.memset(tab_bytes[:].bitcast(I32)[32:64, :], 0)
-        nc.vector.memset(tab_bytes[:].bitcast(I32)[64:128, :], 0)
-        nc.vector.memset(w1_bytes_raw[:], 0)
-        nc.vector.memset(v_planes[:], 0)
+        for rows in (slice(32, 64), slice(64, 128)):
+            nc.vector.memset(tab_bytes[:].bitcast(I32)[rows, :], 0)
+            nc.vector.memset(w1_bytes[:].bitcast(I32)[rows, :], 0)
         nc.vector.memset(pages[0][:], 0.0)
 
-        def rows_of(x, b, t):
-            return x[PASS * b : PASS * (b + 1), :].rearrange("(g t i) c -> t g i c", t=PACK, i=8)[t]
+        def rows_of(x, b):
+            return x[PASS * b : PASS * (b + 1), :].rearrange("(p t) c -> p t c", t=PACK)
 
         saved = {}
         w2_raw = {}
 
         def load_saved(u, after):
             saved[u] = held([P, T], F32, name="saved%d" % u, tag=after)
-            nc.sync.dma_start(out=saved[u][:], in_=rows_of(sT, u // PACK, u % PACK))
+            nc.sync.dma_start(out=saved[u][:], in_=rows_of(sT, u // PACK)[:, u % PACK, :])
 
         def load_w2(b, after):
             w2_raw[b] = held([P, PACK, N], F32, name="w2_raw%d" % b, tag=after)
-            for t in range(PACK):
-                nc.sync.dma_start(out=w2_raw[b][:, t, :], in_=rows_of(w2, b, t))
+            nc.sync.dma_start(out=w2_raw[b][:], in_=rows_of(w2, b))
 
         nc.sync.dma_start(idx[:], offs)
         nc.sync.dma_start(
             out=tab_bytes[:].bitcast(I32)[0:32, :], in_=tab_scales.rearrange("a q t -> (a q) t").bitcast(I32)
         )
+        nc.sync.dma_start(
+            out=w1_bytes[:].bitcast(I32)[0:32, :], in_=w1_scales.rearrange("a q c -> (a q) c").bitcast(I32)
+        )
         tab = [held([P, T], I32, name="tab%d" % a) for a in range(2)]
         for a in range(2):
             nc.sync.dma_start(out=tab[a][:], in_=tab_words[a].rearrange("p t i -> p (t i)").bitcast(I32))
         nc.sync.dma_start(idx2[:], offs2)
-        for q in range(4):
-            nc.gpsimd.dma_start(
-                out=w1_bytes_raw[32 * q : 32 * q + 4, :, :],
-                in_=w1_scales[:, 4 * q : 4 * q + 4, :].bitcast(I32).rearrange("a r c -> r a c"),
-            )
         load_saved(0, "saved0")
         load_saved(1, "saved1")
 
         v_bytes = held([P, S], U8, name="v_bytes")
         nc.vector.tensor_copy(v_bytes[:], tab_bytes[:].indirect(idx[:]))
+        staged = held([P, S + H], U8, name="staged")
+        nc.vector.tensor_copy(
+            out=staged[:, S:].rearrange("p (b t g m) -> p b g t m", b=2, t=PACK, m=16),
+            in_=w1_bytes[:].rearrange("p (b g m t) -> p b g t m", b=2, t=PACK, m=16),
+        )
+        nc.vector.tensor_copy(staged[:].bitcast(I32)[0:32, : S // 4], v_bytes[:].bitcast(I32)[0:32, :])
         for a in range(2):
             for q in range(4):
-                nc.scalar.dma_start(
-                    out=v_planes[32 * q : 32 * q + 4, S // 4 * a : S // 4 * (a + 1)],
-                    in_=v_bytes[:].bitcast(I32)[16 * a + 4 * q : 16 * a + 4 * q + 4, :],
+                nc.sync.dma_start(
+                    out=planes[32 * q : 32 * q + 4, a, :],
+                    in_=staged[:].bitcast(I32)[16 * a + 4 * q : 16 * a + 4 * q + 4, :],
                 )
-        v_scale = [v_planes[:].bitcast(U8)[:, S * a : S * (a + 1)] for a in range(2)]
+        v_scale = [planes[:, a, :].bitcast(U8)[:, :S] for a in range(2)]
+        w1_scale = [planes[:, a, :].bitcast(U8)[:, S:] for a in range(2)]
         v_words = [held([P, S], U32, name="v_words%d" % a) for a in range(2)]
         for a in range(2):
             nc.vector.tensor_copy(v_words[a][:], tab[a][:].bitcast(U32).indirect(idx[:]))
@@ -100,16 +103,10 @@ def tile_list_hit_sensitivity_map_kernel(
         w1_cols = held([P, 2 * H], I32, name="w1_cols")
 
         def order_w1():
-            w1_bytes = held([P, 2 * H // 4], I32, name="w1_bytes", tag="saved0")
             nc.vector.tensor_copy(
-                out=w1_bytes[:].rearrange("p (ab t g i) -> p ab t g i", ab=4, t=PACK, i=2),
-                in_=w1_bytes_raw[:].rearrange("p a (b g t i) -> p (a b) t g i", b=2, t=PACK, i=2),
+                out=w1_cols[:].rearrange("p (ab t g m) -> p ab g t m", ab=4, t=PACK, m=4),
+                in_=w1_raw[:].rearrange("p a (b g m t) -> p (a b) g t m", b=2, t=PACK, m=4),
             )
-            nc.vector.tensor_copy(
-                out=w1_cols[:].rearrange("p (ab t g i) -> p ab t g i", ab=4, t=PACK, i=8),
-                in_=w1_raw[:].rearrange("p a (b g t i) -> p (a b) t g i", b=2, t=PACK, i=8),
-            )
-            return w1_bytes
 
         squares = {}
         h_rows = {}
@@ -131,18 +128,17 @@ def tile_list_hit_sensitivity_map_kernel(
             b, t = divmod(u, PACK)
             acc = psum1.tile([P, HALF], F32, name="acc1")
             for a in range(2):
-                cols = slice(H * a + P * u, H * a + P * (u + 1))
                 nc.tensor.matmul_mx(
                     out=acc[:],
-                    lhsT=w1_cols[:, cols].bitcast(E4M3X4),
-                    lhsT_scale=w1_bytes[:].bitcast(U8)[:, cols],
+                    lhsT=w1_cols[:, H * a + P * u : H * a + P * (u + 1)].bitcast(E4M3X4),
+                    lhsT_scale=w1_scale[a][:, P * u : P * (u + 1)],
                     rhs=v_words[a][:, HALF * j : HALF * (j + 1)].bitcast(E5M2X4),
                     rhs_scale=v_scale[a][:, HALF * j : HALF * (j + 1)],
                     start=(a == 0),
                     stop=(a == 1),
                 )
             if t == 0:
-                tag = "h_rows10" if b == 1 else "h_rows0%d" % j
+                tag = "picked10" if b == 1 else "h_rows0%d" % j
                 h_rows[b, j] = held([P, PACK, HALF], BF16, name="h_rows%d%d" % (b, j), tag=tag)
             nc.vector.scalar_tensor_tensor(
                 out=h_rows[b, j][:, t, :], in0=squares[u, j], scalar=1.0, in1=acc[:], op0=ALU.subtract, op1=ALU.mult
@@ -156,8 +152,8 @@ def tile_list_hit_sensitivity_map_kernel(
             )
             return woven
 
-        def quantise(woven, name):
-            codes = held([P, HALF], U32, name=name + "_codes")
+        def quantise(woven, name, after=""):
+            codes = held([P, HALF], U32, name=name + "_codes", tag=after)
             scale = held([P, HALF], U8, name=name + "_scale")
             nc.vector.quantize_mx(
                 out=codes[:].bitcast(E4M3X4), scales=scale[:], in_=woven[:].rearrange("p c t -> p (c t)")
@@ -202,54 +198,51 @@ def tile_list_hit_sensitivity_map_kernel(
 
         def new_page(after):
             page = held([P, T2], F32, name="page%d" % len(pages), tag=after)
-            nc.gpsimd.memset(page[:], 0.0)
+            nc.vector.memset(page[:], 0.0)
             pages.append(page)
 
         pick(0, (0, 1))
+        load_saved(3, "saved0")
         pick(1, (0, 1))
-        load_saved(3, "saved1")
+        load_w2(0, "saved1")
         pick(2, (0, 1))
-        load_saved(4, "tab0")
-        w1_bytes = order_w1()
-        load_w2(0, "tab1")
+        load_w2(1, "tab0")
+        order_w1()
+        load_saved(4, "tab1")
         pick(3, (0, 1))
-        load_saved(5, "saved1")
+        load_saved(5, "saved0")
+        w2_woven = [weave(w2_raw[b], "w2%d" % b) for b in range(2)]
         back(0, 0)
         back(0, 1)
         load_saved(6, "picked00")
-        pick(4, (0, 1))
-        load_w2(1, "tab0")
         back(1, 0)
         back(1, 1)
         load_saved(7, "picked10")
-        w2_woven0 = weave(w2_raw[0], "w20")
-        pick(5, (0,))
         back(2, 0)
         back(2, 1)
         gains = held([P, S], F32, name="gains", tag="picked20")
         nc.sync.dma_start(out=gains[:], in_=wgo)
-        pick(6, (0,))
         back(3, 0)
         back(3, 1)
-        w2_codes[0], w2_scale[0] = quantise(w2_woven0, "w20")
-        w2_woven1 = weave(w2_raw[1], "w21")
-        for u in range(4, 7):
-            back(u, 0)
+        pick(4, (0, 1))
+        for b in range(2):
+            w2_codes[b], w2_scale[b] = quantise(w2_woven[b], "w2%d" % b)
+        pick(5, (0,))
+        pick(6, (0,))
+        h00_woven = weave(h_rows[0, 0], "h00")
         pick(7, (0,))
         pick(7, (1,))
-        finish_h(0, 0)
-        w2_codes[1], w2_scale[1] = quantise(w2_woven1, "w21")
-        back(7, 0)
+        for u in range(4, 8):
+            back(u, 0)
         finish_h(1, 0)
         late = held([P, S], F32, name="late", tag="picked70")
         pick(5, (1,), late[:, :HALF])
         pick(6, (1,), late[:, HALF:])
-        back(4, 1)
-        new_page("picked40")
-        back(5, 1)
-        back(6, 1)
+        h_codes[0, 0], h_scale[0, 0] = quantise(h00_woven, "h00", "picked50")
+        new_page("picked60")
+        for u in range(4, 8):
+            back(u, 1)
         new_page("picked70")
-        back(7, 1)
         forward(0, 0)
         forward(1, 0)
         place(0, (0,))

@@ -40,13 +40,13 @@ def tile_list_hit_sensitivity_map_kernel(
         idx2 = keep.tile([P, S // 16], U16, name="idx2")
         tab_bytes = held([P, T], U8, name="tab_bytes")
         w1_bytes = held([P, H], U8, name="w1_bytes")
-        planes = held([P, 2, (S + H) // 4], I32, name="planes")
-        pages = [held([P, T2], F32, name="page0")]
+        pages = [held([P, T2], F32, name="page%d" % w) for w in range(2)]
 
         for rows in (slice(32, 64), slice(64, 128)):
             nc.vector.memset(tab_bytes[:].bitcast(I32)[rows, :], 0)
             nc.vector.memset(w1_bytes[:].bitcast(I32)[rows, :], 0)
-        nc.vector.memset(pages[0][:], 0.0)
+        for page in pages:
+            nc.vector.memset(page[:], 0.0)
 
         def rows_of(x, b):
             return x[PASS * b : PASS * (b + 1), :].rearrange("(p t) c -> p t c", t=PACK)
@@ -78,27 +78,35 @@ def tile_list_hit_sensitivity_map_kernel(
 
         v_bytes = held([P, S], U8, name="v_bytes")
         nc.vector.tensor_copy(v_bytes[:], tab_bytes[:].indirect(idx[:]))
+        load_saved(2, "tab_bytes")
         staged = held([P, S + H], U8, name="staged")
         nc.vector.tensor_copy(
             out=staged[:, S:].rearrange("p (b t g m) -> p b g t m", b=2, t=PACK, m=16),
             in_=w1_bytes[:].rearrange("p (b g m t) -> p b g t m", b=2, t=PACK, m=16),
         )
         nc.vector.tensor_copy(staged[:].bitcast(I32)[0:32, : S // 4], v_bytes[:].bitcast(I32)[0:32, :])
-        for a in range(2):
+
+        v_scale = []
+        w1_scale = []
+
+        def lay_plane(a, after):
+            plane = held([P, (S + H) // 4], I32, name="plane%d" % a, tag=after)
             for q in range(4):
-                nc.sync.dma_start(
-                    out=planes[32 * q : 32 * q + 4, a, :],
+                nc.scalar.dma_start(
+                    out=plane[32 * q : 32 * q + 4, :],
                     in_=staged[:].bitcast(I32)[16 * a + 4 * q : 16 * a + 4 * q + 4, :],
                 )
-        v_scale = [planes[:, a, :].bitcast(U8)[:, :S] for a in range(2)]
-        w1_scale = [planes[:, a, :].bitcast(U8)[:, S:] for a in range(2)]
+            v_scale.append(plane[:].bitcast(U8)[:, :S])
+            w1_scale.append(plane[:].bitcast(U8)[:, S:])
+
+        lay_plane(0, "plane0")
+        w1_raw = held([P, 2, H], I32, name="w1_raw", tag="v_bytes")
+        nc.sync.dma_start(out=w1_raw[:], in_=w1_words.rearrange("a p c i -> p a (c i)").bitcast(I32))
         v_words = [held([P, S], U32, name="v_words%d" % a) for a in range(2)]
         for a in range(2):
             nc.vector.tensor_copy(v_words[a][:], tab[a][:].bitcast(U32).indirect(idx[:]))
-
-        load_saved(2, "tab0")
-        w1_raw = held([P, 2, H], I32, name="w1_raw", tag="tab1")
-        nc.sync.dma_start(out=w1_raw[:], in_=w1_words.rearrange("a p c i -> p a (c i)").bitcast(I32))
+        load_saved(3, "tab0")
+        lay_plane(1, "tab1")
 
         w1_cols = held([P, 2 * H], I32, name="w1_cols")
 
@@ -138,7 +146,7 @@ def tile_list_hit_sensitivity_map_kernel(
                     stop=(a == 1),
                 )
             if t == 0:
-                tag = "picked10" if b == 1 else "h_rows0%d" % j
+                tag = "picked10" if b == 1 else ("tab0", "h_rows01")[j]
                 h_rows[b, j] = held([P, PACK, HALF], BF16, name="h_rows%d%d" % (b, j), tag=tag)
             nc.vector.scalar_tensor_tensor(
                 out=h_rows[b, j][:, t, :], in0=squares[u, j], scalar=1.0, in1=acc[:], op0=ALU.subtract, op1=ALU.mult
@@ -202,31 +210,30 @@ def tile_list_hit_sensitivity_map_kernel(
             pages.append(page)
 
         pick(0, (0, 1))
-        load_saved(3, "saved0")
+        load_w2(0, "saved0")
         pick(1, (0, 1))
-        load_w2(0, "saved1")
+        load_saved(4, "saved1")
         pick(2, (0, 1))
-        load_w2(1, "tab0")
+        load_w2(1, "tab_bytes")
         order_w1()
-        load_saved(4, "tab1")
+        load_saved(5, "v_bytes")
         pick(3, (0, 1))
-        load_saved(5, "saved0")
-        w2_woven = [weave(w2_raw[b], "w2%d" % b) for b in range(2)]
+        w2_woven = [weave(w2_raw[0], "w20")]
         back(0, 0)
         back(0, 1)
         load_saved(6, "picked00")
         back(1, 0)
         back(1, 1)
         load_saved(7, "picked10")
+        pick(4, (0, 1))
+        w2_woven.append(weave(w2_raw[1], "w21"))
         back(2, 0)
         back(2, 1)
         gains = held([P, S], F32, name="gains", tag="picked20")
         nc.sync.dma_start(out=gains[:], in_=wgo)
         back(3, 0)
         back(3, 1)
-        pick(4, (0, 1))
-        for b in range(2):
-            w2_codes[b], w2_scale[b] = quantise(w2_woven[b], "w2%d" % b)
+        w2_codes[0], w2_scale[0] = quantise(w2_woven[0], "w20", "picked30")
         pick(5, (0,))
         pick(6, (0,))
         h00_woven = weave(h_rows[0, 0], "h00")
@@ -235,14 +242,14 @@ def tile_list_hit_sensitivity_map_kernel(
         for u in range(4, 8):
             back(u, 0)
         finish_h(1, 0)
-        late = held([P, S], F32, name="late", tag="picked70")
-        pick(5, (1,), late[:, :HALF])
-        pick(6, (1,), late[:, HALF:])
+        late = held([P, 2, HALF], F32, name="late", tag="picked60")
+        for u in range(5, 7):
+            pick(u, (1,), late[:, u - 5, :])
         h_codes[0, 0], h_scale[0, 0] = quantise(h00_woven, "h00", "picked50")
-        new_page("picked60")
+        w2_codes[1], w2_scale[1] = quantise(w2_woven[1], "w21", "picked70")
         for u in range(4, 8):
             back(u, 1)
-        new_page("picked70")
+        new_page("picked60")
         forward(0, 0)
         forward(1, 0)
         place(0, (0,))

@@ -30,6 +30,7 @@ def tile_list_hit_sensitivity_map_kernel(
     with ExitStack() as ctx:
         keep = ctx.enter_context(tc.tile_pool(name="keep", bufs=1))
         ring = ctx.enter_context(tc.tile_pool(name="ring", bufs=2))
+        sums_ring = ctx.enter_context(tc.tile_pool(name="sums_ring", bufs=3))
         psum1 = ctx.enter_context(tc.psum_pool(name="psum1", bufs=5))
         psum2 = ctx.enter_context(tc.psum_pool(name="psum2", bufs=3))
 
@@ -40,13 +41,11 @@ def tile_list_hit_sensitivity_map_kernel(
         idx2 = keep.tile([P, S // 16], U16, name="idx2")
         tab_bytes = held([P, T], U8, name="tab_bytes")
         w1_bytes = held([P, H], U8, name="w1_bytes")
-        pages = [held([P, T2], F32, name="page%d" % w) for w in range(2)]
+        pages = []
 
         for rows in (slice(32, 64), slice(64, 128)):
             nc.vector.memset(tab_bytes[:].bitcast(I32)[rows, :], 0)
             nc.vector.memset(w1_bytes[:].bitcast(I32)[rows, :], 0)
-        for page in pages:
-            nc.vector.memset(page[:], 0.0)
 
         def rows_of(x, b):
             return x[PASS * b : PASS * (b + 1), :].rearrange("(p t) c -> p t c", t=PACK)
@@ -72,25 +71,37 @@ def tile_list_hit_sensitivity_map_kernel(
         tab = [held([P, T], I32, name="tab%d" % a) for a in range(2)]
         for a in range(2):
             nc.sync.dma_start(out=tab[a][:], in_=tab_words[a].rearrange("p t i -> p (t i)").bitcast(I32))
-        nc.sync.dma_start(idx2[:], offs2)
         load_saved(0, "saved0")
-        load_saved(1, "saved1")
+        w1_raw = held([P, 2, H], I32, name="w1_raw")
+        nc.sync.dma_start(out=w1_raw[:], in_=w1_words.rearrange("a p c i -> p a (c i)").bitcast(I32))
+        for u in range(1, 4):
+            load_saved(u, "saved%d" % u)
+        load_w2(0, "w2_raw0")
+        for u in range(4, 8):
+            load_saved(u, "saved%d" % u)
+        load_w2(1, "w2_raw1")
+        nc.sync.dma_start(idx2[:], offs2)
+
+        def new_page(after):
+            page = held([P, T2], F32, name="page%d" % len(pages), tag=after)
+            nc.gpsimd.memset(page[:], 0.0)
+            pages.append(page)
 
         v_bytes = held([P, S], U8, name="v_bytes")
         nc.vector.tensor_copy(v_bytes[:], tab_bytes[:].indirect(idx[:]))
-        load_saved(2, "tab_bytes")
         staged = held([P, S + H], U8, name="staged")
         nc.vector.tensor_copy(
             out=staged[:, S:].rearrange("p (b t g m) -> p b g t m", b=2, t=PACK, m=16),
             in_=w1_bytes[:].rearrange("p (b g m t) -> p b g t m", b=2, t=PACK, m=16),
         )
         nc.vector.tensor_copy(staged[:].bitcast(I32)[0:32, : S // 4], v_bytes[:].bitcast(I32)[0:32, :])
+        new_page("v_bytes")
 
         v_scale = []
         w1_scale = []
 
-        def lay_plane(a, after):
-            plane = held([P, (S + H) // 4], I32, name="plane%d" % a, tag=after)
+        def lay_plane(a):
+            plane = held([P, (S + H) // 4], I32, name="plane%d" % a)
             for q in range(4):
                 nc.scalar.dma_start(
                     out=plane[32 * q : 32 * q + 4, :],
@@ -99,14 +110,11 @@ def tile_list_hit_sensitivity_map_kernel(
             v_scale.append(plane[:].bitcast(U8)[:, :S])
             w1_scale.append(plane[:].bitcast(U8)[:, S:])
 
-        lay_plane(0, "plane0")
-        w1_raw = held([P, 2, H], I32, name="w1_raw", tag="v_bytes")
-        nc.sync.dma_start(out=w1_raw[:], in_=w1_words.rearrange("a p c i -> p a (c i)").bitcast(I32))
         v_words = [held([P, S], U32, name="v_words%d" % a) for a in range(2)]
         for a in range(2):
+            lay_plane(a)
             nc.vector.tensor_copy(v_words[a][:], tab[a][:].bitcast(U32).indirect(idx[:]))
-        load_saved(3, "tab0")
-        lay_plane(1, "tab1")
+            new_page("tab%d" % a)
 
         w1_cols = held([P, 2 * H], I32, name="w1_cols")
 
@@ -129,6 +137,8 @@ def tile_list_hit_sensitivity_map_kernel(
                 picked = held([P, HALF * len(halves)], F32, name="picked%d%d" % (u, lo))[:]
             nc.vector.tensor_copy(picked, saved[u][:].indirect(idx[:, LIST_COLS * lo : LIST_COLS * hi]))
             nc.scalar.activation(picked, picked, ACT.Square)
+            if u < PACK:
+                nc.gpsimd.tensor_scalar(picked, picked, 1.0, -1.0, ALU.mult, ALU.add)
             for j in halves:
                 squares[u, j] = picked[:, HALF * (j - lo) : HALF * (j - lo + 1)]
 
@@ -146,11 +156,16 @@ def tile_list_hit_sensitivity_map_kernel(
                     stop=(a == 1),
                 )
             if t == 0:
-                tag = "picked10" if b == 1 else ("tab0", "h_rows01")[j]
+                tag = "h_rows0%d" % j if b == 0 else ("saved7", "h_rows11")[j]
                 h_rows[b, j] = held([P, PACK, HALF], BF16, name="h_rows%d%d" % (b, j), tag=tag)
-            nc.vector.scalar_tensor_tensor(
-                out=h_rows[b, j][:, t, :], in0=squares[u, j], scalar=1.0, in1=acc[:], op0=ALU.subtract, op1=ALU.mult
-            )
+            if b == 0:
+                sums = sums_ring.tile([P, HALF], F32, name="sums")
+                nc.scalar.copy(out=sums[:], in_=acc[:])
+                nc.gpsimd.tensor_tensor(h_rows[b, j][:, t, :], squares[u, j], sums[:], ALU.mult)
+            else:
+                nc.vector.scalar_tensor_tensor(
+                    out=h_rows[b, j][:, t, :], in0=squares[u, j], scalar=1.0, in1=acc[:], op0=ALU.subtract, op1=ALU.mult
+                )
 
         def weave(rows, name, after=None):
             woven = held([P, HALF, PACK], BF16, name=name + "_woven", tag=after or name + "_woven")
@@ -168,7 +183,7 @@ def tile_list_hit_sensitivity_map_kernel(
             )
             return codes, scale
 
-        logs = [held([P, S], F32, name="logs%d" % n) for n in range(4)]
+        logs = [held([P, S], F32, name="logs%d" % n, tag="saved%d" % n) for n in range(4)]
 
         def forward(n, j):
             acc = psum2.tile([P, HALF], F32, name="acc2")
@@ -204,44 +219,26 @@ def tile_list_hit_sensitivity_map_kernel(
             name = "h%d%d" % (b, j)
             h_codes[b, j], h_scale[b, j] = quantise(weave(h_rows[b, j], name, after), name)
 
-        def new_page(after):
-            page = held([P, T2], F32, name="page%d" % len(pages), tag=after)
-            nc.vector.memset(page[:], 0.0)
-            pages.append(page)
-
         pick(0, (0, 1))
-        load_w2(0, "saved0")
-        pick(1, (0, 1))
-        load_saved(4, "saved1")
-        pick(2, (0, 1))
-        load_w2(1, "tab_bytes")
         order_w1()
-        load_saved(5, "v_bytes")
-        pick(3, (0, 1))
-        w2_woven = [weave(w2_raw[0], "w20")]
-        back(0, 0)
-        back(0, 1)
-        load_saved(6, "picked00")
-        back(1, 0)
-        back(1, 1)
-        load_saved(7, "picked10")
-        pick(4, (0, 1))
-        w2_woven.append(weave(w2_raw[1], "w21"))
-        back(2, 0)
-        back(2, 1)
-        gains = held([P, S], F32, name="gains", tag="picked20")
+        gains = held([P, S], F32, name="gains", tag="w1_raw")
         nc.sync.dma_start(out=gains[:], in_=wgo)
-        back(3, 0)
-        back(3, 1)
-        w2_codes[0], w2_scale[0] = quantise(w2_woven[0], "w20", "picked30")
+        for u in range(1, 5):
+            pick(u, (0, 1))
+            back(u - 1, 0)
+            back(u - 1, 1)
+        w2_woven = [weave(w2_raw[0], "w20")]
         pick(5, (0,))
         pick(6, (0,))
+        w2_codes[0], w2_scale[0] = quantise(w2_woven[0], "w20")
         h00_woven = weave(h_rows[0, 0], "h00")
+        h01_woven = weave(h_rows[0, 1], "h01")
         pick(7, (0,))
         pick(7, (1,))
+        w2_woven.append(weave(w2_raw[1], "w21"))
         for u in range(4, 8):
             back(u, 0)
-        finish_h(1, 0)
+        finish_h(1, 0, "picked00")
         late = held([P, 2, HALF], F32, name="late", tag="picked60")
         for u in range(5, 7):
             pick(u, (1,), late[:, u - 5, :])
@@ -249,13 +246,12 @@ def tile_list_hit_sensitivity_map_kernel(
         w2_codes[1], w2_scale[1] = quantise(w2_woven[1], "w21", "picked70")
         for u in range(4, 8):
             back(u, 1)
-        new_page("picked60")
+        h_codes[0, 1], h_scale[0, 1] = quantise(h01_woven, "h01", "picked71")
         forward(0, 0)
         forward(1, 0)
         place(0, (0,))
         place(1, (0,))
-        finish_h(0, 1, "picked71")
-        finish_h(1, 1)
+        finish_h(1, 1, "picked10")
         forward(2, 0)
         place(2, (0,))
         for n in range(3):

@@ -21,6 +21,7 @@ PACK = 4
 PASS = P * PACK
 HALF = 512
 LIST_COLS = HALF // 16
+ROW0 = 96
 
 
 def tile_list_hit_sensitivity_map_kernel(
@@ -30,7 +31,7 @@ def tile_list_hit_sensitivity_map_kernel(
     with ExitStack() as ctx:
         keep = ctx.enter_context(tc.tile_pool(name="keep", bufs=1))
         ring = ctx.enter_context(tc.tile_pool(name="ring", bufs=2))
-        sums_ring = ctx.enter_context(tc.tile_pool(name="sums_ring", bufs=3))
+        sums_ring = ctx.enter_context(tc.tile_pool(name="sums_ring", bufs=6))
         psum1 = ctx.enter_context(tc.psum_pool(name="psum1", bufs=5))
         psum2 = ctx.enter_context(tc.psum_pool(name="psum2", bufs=3))
 
@@ -43,9 +44,18 @@ def tile_list_hit_sensitivity_map_kernel(
         w1_bytes = held([P, H], U8, name="w1_bytes")
         pages = []
 
-        for rows in (slice(32, 64), slice(64, 128)):
-            nc.vector.memset(tab_bytes[:].bitcast(I32)[rows, :], 0)
-            nc.vector.memset(w1_bytes[:].bitcast(I32)[rows, :], 0)
+        nc.gpsimd.memset(tab_bytes[:].bitcast(I32)[:ROW0, :], 0)
+        nc.gpsimd.memset(w1_bytes[:].bitcast(I32)[:ROW0, :], 0)
+
+        def new_page(after):
+            page = held([P, T2], F32, name="page%d" % len(pages), tag=after)
+            nc.gpsimd.memset(page[:], 0.0)
+            pages.append(page)
+
+        new_page("page0")
+        warm = held([P, 1], F32, name="warm")
+        nc.scalar.activation(warm[:], pages[0][:, 0:1], ACT.Ln, bias=1.0)
+        new_page("page1")
 
         def rows_of(x, b):
             return x[PASS * b : PASS * (b + 1), :].rearrange("(p t) c -> p t c", t=PACK)
@@ -57,35 +67,28 @@ def tile_list_hit_sensitivity_map_kernel(
             saved[u] = held([P, T], F32, name="saved%d" % u, tag=after)
             nc.sync.dma_start(out=saved[u][:], in_=rows_of(sT, u // PACK)[:, u % PACK, :])
 
-        def load_w2(b, after):
-            w2_raw[b] = held([P, PACK, N], F32, name="w2_raw%d" % b, tag=after)
-            nc.sync.dma_start(out=w2_raw[b][:], in_=rows_of(w2, b))
+        def load_w2(half, after):
+            w2_raw[half] = held([P, 2, PACK, N // 2], F32, name="w2_raw%d" % half, tag=after)
+            for b in range(2):
+                nc.sync.dma_start(
+                    out=w2_raw[half][:, b], in_=rows_of(w2, b)[:, :, N // 2 * half : N // 2 * (half + 1)]
+                )
 
         nc.sync.dma_start(idx[:], offs)
         nc.sync.dma_start(
-            out=tab_bytes[:].bitcast(I32)[0:32, :], in_=tab_scales.rearrange("a q t -> (a q) t").bitcast(I32)
+            out=tab_bytes[:].bitcast(I32)[ROW0:, :], in_=tab_scales.rearrange("a q t -> (a q) t").bitcast(I32)
         )
         nc.sync.dma_start(
-            out=w1_bytes[:].bitcast(I32)[0:32, :], in_=w1_scales.rearrange("a q c -> (a q) c").bitcast(I32)
+            out=w1_bytes[:].bitcast(I32)[ROW0:, :], in_=w1_scales.rearrange("a q c -> (a q) c").bitcast(I32)
         )
         tab = [held([P, T], I32, name="tab%d" % a) for a in range(2)]
         for a in range(2):
             nc.sync.dma_start(out=tab[a][:], in_=tab_words[a].rearrange("p t i -> p (t i)").bitcast(I32))
+        nc.sync.dma_start(idx2[:], offs2)
         load_saved(0, "saved0")
         w1_raw = held([P, 2, H], I32, name="w1_raw")
         nc.sync.dma_start(out=w1_raw[:], in_=w1_words.rearrange("a p c i -> p a (c i)").bitcast(I32))
-        for u in range(1, 4):
-            load_saved(u, "saved%d" % u)
-        load_w2(0, "w2_raw0")
-        for u in range(4, 8):
-            load_saved(u, "saved%d" % u)
-        load_w2(1, "w2_raw1")
-        nc.sync.dma_start(idx2[:], offs2)
-
-        def new_page(after):
-            page = held([P, T2], F32, name="page%d" % len(pages), tag=after)
-            nc.gpsimd.memset(page[:], 0.0)
-            pages.append(page)
+        load_saved(1, "saved1")
 
         v_bytes = held([P, S], U8, name="v_bytes")
         nc.vector.tensor_copy(v_bytes[:], tab_bytes[:].indirect(idx[:]))
@@ -94,7 +97,7 @@ def tile_list_hit_sensitivity_map_kernel(
             out=staged[:, S:].rearrange("p (b t g m) -> p b g t m", b=2, t=PACK, m=16),
             in_=w1_bytes[:].rearrange("p (b g m t) -> p b g t m", b=2, t=PACK, m=16),
         )
-        nc.vector.tensor_copy(staged[:].bitcast(I32)[0:32, : S // 4], v_bytes[:].bitcast(I32)[0:32, :])
+        nc.vector.tensor_copy(staged[:].bitcast(I32)[ROW0:, : S // 4], v_bytes[:].bitcast(I32)[ROW0:, :])
         new_page("v_bytes")
 
         v_scale = []
@@ -105,7 +108,7 @@ def tile_list_hit_sensitivity_map_kernel(
             for q in range(4):
                 nc.scalar.dma_start(
                     out=plane[32 * q : 32 * q + 4, :],
-                    in_=staged[:].bitcast(I32)[16 * a + 4 * q : 16 * a + 4 * q + 4, :],
+                    in_=staged[:].bitcast(I32)[ROW0 + 16 * a + 4 * q : ROW0 + 16 * a + 4 * q + 4, :],
                 )
             v_scale.append(plane[:].bitcast(U8)[:, :S])
             w1_scale.append(plane[:].bitcast(U8)[:, S:])
@@ -114,7 +117,9 @@ def tile_list_hit_sensitivity_map_kernel(
         for a in range(2):
             lay_plane(a)
             nc.vector.tensor_copy(v_words[a][:], tab[a][:].bitcast(U32).indirect(idx[:]))
-            new_page("tab%d" % a)
+
+        load_saved(2, "tab0")
+        load_saved(3, "tab1")
 
         w1_cols = held([P, 2 * H], I32, name="w1_cols")
 
@@ -137,8 +142,6 @@ def tile_list_hit_sensitivity_map_kernel(
                 picked = held([P, HALF * len(halves)], F32, name="picked%d%d" % (u, lo))[:]
             nc.vector.tensor_copy(picked, saved[u][:].indirect(idx[:, LIST_COLS * lo : LIST_COLS * hi]))
             nc.scalar.activation(picked, picked, ACT.Square)
-            if u < PACK:
-                nc.gpsimd.tensor_scalar(picked, picked, 1.0, -1.0, ALU.mult, ALU.add)
             for j in halves:
                 squares[u, j] = picked[:, HALF * (j - lo) : HALF * (j - lo + 1)]
 
@@ -156,9 +159,10 @@ def tile_list_hit_sensitivity_map_kernel(
                     stop=(a == 1),
                 )
             if t == 0:
-                tag = "h_rows0%d" % j if b == 0 else ("saved7", "h_rows11")[j]
+                tag = ("tab1", "tab0")[b] if j == 0 else "h_rows%d1" % b
                 h_rows[b, j] = held([P, PACK, HALF], BF16, name="h_rows%d%d" % (b, j), tag=tag)
-            if b == 0:
+            if j == 1 and u < 6:
+                nc.gpsimd.tensor_scalar(squares[u, j], squares[u, j], 1.0, -1.0, ALU.mult, ALU.add)
                 sums = sums_ring.tile([P, HALF], F32, name="sums")
                 nc.scalar.copy(out=sums[:], in_=acc[:])
                 nc.gpsimd.tensor_tensor(h_rows[b, j][:, t, :], squares[u, j], sums[:], ALU.mult)
@@ -183,16 +187,30 @@ def tile_list_hit_sensitivity_map_kernel(
             )
             return codes, scale
 
-        logs = [held([P, S], F32, name="logs%d" % n, tag="saved%d" % n) for n in range(4)]
+        def ready_w2(n):
+            woven = held([P, 2, P, PACK], BF16, name="w2_woven%d" % n)
+            nc.scalar.copy(
+                out=woven[:].rearrange("p b (c i) t -> p b c t i", i=4),
+                in_=w2_raw[n // 2][:, :, :, P * (n % 2) : P * (n % 2 + 1)].rearrange("p b t (c i) -> p b c t i", i=4),
+            )
+            w2_codes[n] = held([P, 2 * P], U32, name="w2_codes%d" % n)
+            w2_scale[n] = held([P, 2 * P], U8, name="w2_scale%d" % n)
+            nc.vector.quantize_mx(
+                out=w2_codes[n][:].bitcast(E4M3X4),
+                scales=w2_scale[n][:],
+                in_=woven[:].rearrange("p b c t -> p (b c t)"),
+            )
+
+        logs = [held([P, S], F32, name="logs%d" % n) for n in range(4)]
 
         def forward(n, j):
             acc = psum2.tile([P, HALF], F32, name="acc2")
-            cols = slice(P * n, P * (n + 1))
             for b in range(2):
+                cols = slice(P * b, P * (b + 1))
                 nc.tensor.matmul_mx(
                     out=acc[:],
-                    lhsT=w2_codes[b][:, cols].bitcast(E4M3X4),
-                    lhsT_scale=w2_scale[b][:, cols],
+                    lhsT=w2_codes[n][:, cols].bitcast(E4M3X4),
+                    lhsT_scale=w2_scale[n][:, cols],
                     rhs=h_codes[b, j][:].bitcast(E4M3X4),
                     rhs_scale=h_scale[b, j][:],
                     start=(b == 0),
@@ -220,42 +238,54 @@ def tile_list_hit_sensitivity_map_kernel(
             h_codes[b, j], h_scale[b, j] = quantise(weave(h_rows[b, j], name, after), name)
 
         pick(0, (0, 1))
+        load_saved(4, "saved0")
         order_w1()
+        load_saved(5, "w1_raw")
+        back(0, 1)
+        pick(1, (0, 1))
+        load_saved(6, "saved1")
+        back(1, 1)
+        pick(2, (0, 1))
+        load_saved(7, "tab0")
+        back(2, 1)
+        pick(3, (0, 1))
+        back(3, 1)
+        pick(4, (0, 1))
+        load_w2(0, "saved0")
+        for u in range(4):
+            back(u, 0)
+        h00_woven = weave(h_rows[0, 0], "h00")
+        back(4, 1)
+        pick(5, (0, 1))
         gains = held([P, S], F32, name="gains", tag="w1_raw")
         nc.sync.dma_start(out=gains[:], in_=wgo)
-        for u in range(1, 5):
-            pick(u, (0, 1))
-            back(u - 1, 0)
-            back(u - 1, 1)
-        w2_woven = [weave(w2_raw[0], "w20")]
-        pick(5, (0,))
+        back(5, 1)
         pick(6, (0,))
-        w2_codes[0], w2_scale[0] = quantise(w2_woven[0], "w20")
-        h00_woven = weave(h_rows[0, 0], "h00")
-        h01_woven = weave(h_rows[0, 1], "h01")
         pick(7, (0,))
         pick(7, (1,))
-        w2_woven.append(weave(w2_raw[1], "w21"))
         for u in range(4, 8):
             back(u, 0)
+        ready_w2(0)
         finish_h(1, 0, "picked00")
-        late = held([P, 2, HALF], F32, name="late", tag="picked60")
-        for u in range(5, 7):
-            pick(u, (1,), late[:, u - 5, :])
-        h_codes[0, 0], h_scale[0, 0] = quantise(h00_woven, "h00", "picked50")
-        w2_codes[1], w2_scale[1] = quantise(w2_woven[1], "w21", "picked70")
-        for u in range(4, 8):
+        late = held([P, HALF], F32, name="late", tag="picked60")
+        pick(6, (1,), late[:])
+        load_w2(1, "picked40")
+        h_codes[0, 0], h_scale[0, 0] = quantise(h00_woven, "h00", "picked70")
+        for u in (7, 6):
             back(u, 1)
-        h_codes[0, 1], h_scale[0, 1] = quantise(h01_woven, "h01", "picked71")
+        h_codes[0, 1], h_scale[0, 1] = quantise(weave(h_rows[0, 1], "h01"), "h01", "picked71")
         forward(0, 0)
+        ready_w2(1)
         forward(1, 0)
         place(0, (0,))
-        place(1, (0,))
         finish_h(1, 1, "picked10")
+        place(1, (0,))
+        ready_w2(2)
         forward(2, 0)
         place(2, (0,))
         for n in range(3):
             forward(n, 1)
+        ready_w2(3)
         forward(3, 0)
         forward(3, 1)
         for n in range(3):

@@ -30,8 +30,6 @@ def tile_list_hit_sensitivity_map_kernel(
     nc = tc.nc
     with ExitStack() as ctx:
         keep = ctx.enter_context(tc.tile_pool(name="keep", bufs=1))
-        ring = ctx.enter_context(tc.tile_pool(name="ring", bufs=2))
-        sums_ring = ctx.enter_context(tc.tile_pool(name="sums_ring", bufs=6))
         psum1 = ctx.enter_context(tc.psum_pool(name="psum1", bufs=5))
         psum2 = ctx.enter_context(tc.psum_pool(name="psum2", bufs=3))
 
@@ -52,7 +50,11 @@ def tile_list_hit_sensitivity_map_kernel(
             nc.gpsimd.memset(page[:], 0.0)
             pages.append(page)
 
-        new_page("page0")
+        first_page = held([P, T2], F32, name="first_page")
+        nc.vector.memset(first_page[:, : T2 // 2 - 1], 0.0)
+        nc.vector.memset(first_page[:, T2 // 2 - 1 :], 0.0)
+        pages.append(first_page)
+        new_page("page2")
         warm = held([P, 1], F32, name="warm")
         nc.scalar.activation(warm[:], pages[0][:, 0:1], ACT.Ln, bias=1.0)
         new_page("page1")
@@ -159,11 +161,11 @@ def tile_list_hit_sensitivity_map_kernel(
                     stop=(a == 1),
                 )
             if t == 0:
-                tag = ("tab1", "tab0")[b] if j == 0 else "h_rows%d1" % b
+                tag = {(0, 1): "sums30", (1, 0): "tab0"}.get((b, j), "")
                 h_rows[b, j] = held([P, PACK, HALF], BF16, name="h_rows%d%d" % (b, j), tag=tag)
-            if j == 1 and u < 6:
+            if u < 4 or (u, j) == (4, 1):
                 nc.gpsimd.tensor_scalar(squares[u, j], squares[u, j], 1.0, -1.0, ALU.mult, ALU.add)
-                sums = sums_ring.tile([P, HALF], F32, name="sums")
+                sums = held([P, HALF], F32, name="sums%d%d" % (u, j))
                 nc.scalar.copy(out=sums[:], in_=acc[:])
                 nc.gpsimd.tensor_tensor(h_rows[b, j][:, t, :], squares[u, j], sums[:], ALU.mult)
             else:
@@ -185,53 +187,58 @@ def tile_list_hit_sensitivity_map_kernel(
             nc.vector.quantize_mx(
                 out=codes[:].bitcast(E4M3X4), scales=scale[:], in_=woven[:].rearrange("p c t -> p (c t)")
             )
-            return codes, scale
+            return codes[:], scale[:]
 
-        def ready_w2(n):
-            woven = held([P, 2, P, PACK], BF16, name="w2_woven%d" % n)
-            nc.scalar.copy(
-                out=woven[:].rearrange("p b (c i) t -> p b c t i", i=4),
-                in_=w2_raw[n // 2][:, :, :, P * (n % 2) : P * (n % 2 + 1)].rearrange("p b t (c i) -> p b c t i", i=4),
-            )
-            w2_codes[n] = held([P, 2 * P], U32, name="w2_codes%d" % n)
-            w2_scale[n] = held([P, 2 * P], U8, name="w2_scale%d" % n)
+        def weave_w2(tiles, after=""):
+            count = len(tiles)
+            woven = held([P, count, 2, P, PACK], BF16, name="w2_woven%d" % tiles[0], tag=after)
+            for m, n in enumerate(tiles):
+                nc.scalar.copy(
+                    out=woven[:, m].rearrange("p b (c i) t -> p b c t i", i=4),
+                    in_=w2_raw[n // 2][:, :, :, P * (n % 2) : P * (n % 2 + 1)].rearrange(
+                        "p b t (c i) -> p b c t i", i=4
+                    ),
+                )
+            return woven
+
+        def quantise_w2(tiles, woven, after=""):
+            count = len(tiles)
+            codes = held([P, count * 2 * P], U32, name="w2_codes%d" % tiles[0], tag=after)
+            scale = held([P, count * 2 * P], U8, name="w2_scale%d" % tiles[0])
             nc.vector.quantize_mx(
-                out=w2_codes[n][:].bitcast(E4M3X4),
-                scales=w2_scale[n][:],
-                in_=woven[:].rearrange("p b c t -> p (b c t)"),
+                out=codes[:].bitcast(E4M3X4), scales=scale[:], in_=woven[:].rearrange("p m b c t -> p (m b c t)")
             )
+            for m, n in enumerate(tiles):
+                w2_codes[n] = codes[:, 2 * P * m : 2 * P * (m + 1)]
+                w2_scale[n] = scale[:, 2 * P * m : 2 * P * (m + 1)]
 
-        logs = [held([P, S], F32, name="logs%d" % n) for n in range(4)]
+        logs = {}
 
-        def forward(n, j):
-            acc = psum2.tile([P, HALF], F32, name="acc2")
+        def forward(n, lo, hi, square_after="", log_after=""):
+            acc = psum2.tile([P, hi - lo], F32, name="acc2")
+            j, cols = lo // HALF, slice(lo % HALF, lo % HALF + hi - lo)
             for b in range(2):
-                cols = slice(P * b, P * (b + 1))
                 nc.tensor.matmul_mx(
                     out=acc[:],
-                    lhsT=w2_codes[n][:, cols].bitcast(E4M3X4),
-                    lhsT_scale=w2_scale[n][:, cols],
-                    rhs=h_codes[b, j][:].bitcast(E4M3X4),
-                    rhs_scale=h_scale[b, j][:],
+                    lhsT=w2_codes[n][:, P * b : P * (b + 1)].bitcast(E4M3X4),
+                    lhsT_scale=w2_scale[n][:, P * b : P * (b + 1)],
+                    rhs=h_codes[b, j][:, cols].bitcast(E4M3X4),
+                    rhs_scale=h_scale[b, j][:, cols],
                     start=(b == 0),
                     stop=(b == 1),
                 )
-            y2 = ring.tile([P, HALF], F32, name="y2")
+            y2 = held([P, hi - lo], F32, name="y2_%d_%d" % (n, lo), tag=square_after)
             nc.scalar.activation(y2[:], acc[:], ACT.Square)
-            nc.scalar.activation(logs[n][:, HALF * j : HALF * (j + 1)], y2[:], ACT.Ln, bias=1.0)
+            logs[n, lo] = held([P, hi - lo], F32, name="logs_%d_%d" % (n, lo), tag=log_after)
+            nc.scalar.activation(logs[n, lo][:], y2[:], ACT.Ln, bias=1.0)
 
-        def place(n, halves):
-            lo, hi = halves[0], halves[-1] + 1
-            cols = slice(HALF * lo, HALF * hi)
+        def place(n, lo, hi):
             nc.vector.tensor_tensor(
-                pages[n % 3][:].indirect(idx2[:, LIST_COLS * lo : LIST_COLS * hi]),
-                logs[n][:, cols],
-                gains[:, cols],
-                ALU.mult,
+                pages[n][:].indirect(idx2[:, lo // 16 : hi // 16]), logs[n, lo][:], gains[:, lo:hi], ALU.mult
             )
 
         def store(n):
-            nc.sync.dma_start(out=out[P * n : P * (n + 1), :], in_=pages[n % 3][:])
+            nc.sync.dma_start(out=out[P * n : P * (n + 1), :], in_=pages[n][:])
 
         def finish_h(b, j, after=None):
             name = "h%d%d" % (b, j)
@@ -241,55 +248,54 @@ def tile_list_hit_sensitivity_map_kernel(
         load_saved(4, "saved0")
         order_w1()
         load_saved(5, "w1_raw")
-        back(0, 1)
         pick(1, (0, 1))
         load_saved(6, "saved1")
-        back(1, 1)
         pick(2, (0, 1))
         load_saved(7, "tab0")
-        back(2, 1)
         pick(3, (0, 1))
-        back(3, 1)
+        load_w2(0, "tab1")
         pick(4, (0, 1))
-        load_w2(0, "saved0")
-        for u in range(4):
-            back(u, 0)
-        h00_woven = weave(h_rows[0, 0], "h00")
+        load_w2(1, "saved0")
+        for j in range(2):
+            for u in range(4):
+                back(u, j)
         back(4, 1)
-        pick(5, (0, 1))
-        gains = held([P, S], F32, name="gains", tag="w1_raw")
-        nc.sync.dma_start(out=gains[:], in_=wgo)
-        back(5, 1)
+        pick(5, (0,))
         pick(6, (0,))
         pick(7, (0,))
         pick(7, (1,))
+        gains = held([P, S], F32, name="gains", tag="picked10")
+        nc.sync.dma_start(out=gains[:], in_=wgo)
+        h00_woven = weave(h_rows[0, 0], "h00")
         for u in range(4, 8):
             back(u, 0)
-        ready_w2(0)
+        w2_woven = {tiles: weave_w2(tiles) for tiles in ((0,), (1,))}
+        quantise_w2((0,), w2_woven[0,])
         finish_h(1, 0, "picked00")
-        late = held([P, HALF], F32, name="late", tag="picked60")
-        pick(6, (1,), late[:])
-        load_w2(1, "picked40")
+        late5 = held([P, HALF], F32, name="late5", tag="picked60")
+        pick(5, (1,), late5[:])
         h_codes[0, 0], h_scale[0, 0] = quantise(h00_woven, "h00", "picked70")
-        for u in (7, 6):
-            back(u, 1)
-        h_codes[0, 1], h_scale[0, 1] = quantise(weave(h_rows[0, 1], "h01"), "h01", "picked71")
-        forward(0, 0)
-        ready_w2(1)
-        forward(1, 0)
-        place(0, (0,))
-        finish_h(1, 1, "picked10")
-        place(1, (0,))
-        ready_w2(2)
-        forward(2, 0)
-        place(2, (0,))
-        for n in range(3):
-            forward(n, 1)
-        ready_w2(3)
-        forward(3, 0)
-        forward(3, 1)
-        for n in range(3):
-            place(n, (1,))
+        quantise_w2((1,), w2_woven[1,])
+        late6 = held([P, HALF], F32, name="late6", tag="tab0")
+        pick(6, (1,), late6[:])
+        back(7, 1)
+        back(5, 1)
+        back(6, 1)
+        forward(0, 0, HALF // 2)
+        forward(0, HALF // 2, HALF)
+        place(0, 0, HALF // 2)
+        place(0, HALF // 2, HALF)
+        w2_late = weave_w2((2, 3), "y2_0_256")
+        forward(1, 0, HALF, square_after="y2_0_0", log_after="saved0")
+        quantise_w2((2, 3), w2_late)
+        place(1, 0, HALF)
+        finish_h(0, 1, "y2_0_0")
+        forward(2, 0, HALF)
+        place(2, 0, HALF)
+        finish_h(1, 1, "y2_2_0")
+        forward(3, 0, HALF, square_after="h_rows11")
+        place(3, 0, HALF)
+        for n in range(4):
+            forward(n, HALF, S)
+            place(n, HALF, S)
             store(n)
-        place(3, (0, 1))
-        store(3)

@@ -50,11 +50,7 @@ def tile_list_hit_sensitivity_map_kernel(
             nc.gpsimd.memset(page[:], 0.0)
             pages.append(page)
 
-        first_page = held([P, T2], F32, name="first_page")
-        nc.vector.memset(first_page[:, : T2 // 2 - 1], 0.0)
-        nc.vector.memset(first_page[:, T2 // 2 - 1 :], 0.0)
-        pages.append(first_page)
-        new_page("page2")
+        new_page("page0")
         warm = held([P, 1], F32, name="warm")
         nc.scalar.activation(warm[:], pages[0][:, 0:1], ACT.Ln, bias=1.0)
         new_page("page1")
@@ -86,11 +82,11 @@ def tile_list_hit_sensitivity_map_kernel(
         tab = [held([P, T], I32, name="tab%d" % a) for a in range(2)]
         for a in range(2):
             nc.sync.dma_start(out=tab[a][:], in_=tab_words[a].rearrange("p t i -> p (t i)").bitcast(I32))
-        nc.sync.dma_start(idx2[:], offs2)
         load_saved(0, "saved0")
         w1_raw = held([P, 2, H], I32, name="w1_raw")
         nc.sync.dma_start(out=w1_raw[:], in_=w1_words.rearrange("a p c i -> p a (c i)").bitcast(I32))
         load_saved(1, "saved1")
+        nc.sync.dma_start(idx2[:], offs2)
 
         v_bytes = held([P, S], U8, name="v_bytes")
         nc.vector.tensor_copy(v_bytes[:], tab_bytes[:].indirect(idx[:]))
@@ -120,8 +116,8 @@ def tile_list_hit_sensitivity_map_kernel(
             lay_plane(a)
             nc.vector.tensor_copy(v_words[a][:], tab[a][:].bitcast(U32).indirect(idx[:]))
 
-        load_saved(2, "tab0")
-        load_saved(3, "tab1")
+        new_page("tab0")
+        load_saved(2, "tab1")
 
         w1_cols = held([P, 2 * H], I32, name="w1_cols")
 
@@ -161,13 +157,18 @@ def tile_list_hit_sensitivity_map_kernel(
                     stop=(a == 1),
                 )
             if t == 0:
-                tag = {(0, 1): "sums30", (1, 0): "tab0"}.get((b, j), "")
+                tag = ("saved0", "picked70")[j] if b == 1 else ""
                 h_rows[b, j] = held([P, PACK, HALF], BF16, name="h_rows%d%d" % (b, j), tag=tag)
-            if u < 4 or (u, j) == (4, 1):
-                nc.gpsimd.tensor_scalar(squares[u, j], squares[u, j], 1.0, -1.0, ALU.mult, ALU.add)
+            if u < 4:
+                slope = squares[u, j]
+                if j == 1:
+                    slope = held([P, HALF], F32, name="slope%d" % u, tag=("sums30", "slope30")[u % 2])[:]
+                elif u == 3:
+                    slope = held([P, HALF], F32, name="slope30")[:]
+                nc.gpsimd.tensor_scalar(slope, squares[u, j], 1.0, -1.0, ALU.mult, ALU.add)
                 sums = held([P, HALF], F32, name="sums%d%d" % (u, j))
                 nc.scalar.copy(out=sums[:], in_=acc[:])
-                nc.gpsimd.tensor_tensor(h_rows[b, j][:, t, :], squares[u, j], sums[:], ALU.mult)
+                nc.gpsimd.tensor_tensor(h_rows[b, j][:, t, :], slope, sums[:], ALU.mult)
             else:
                 nc.vector.scalar_tensor_tensor(
                     out=h_rows[b, j][:, t, :], in0=squares[u, j], scalar=1.0, in1=acc[:], op0=ALU.subtract, op1=ALU.mult
@@ -245,38 +246,69 @@ def tile_list_hit_sensitivity_map_kernel(
             h_codes[b, j], h_scale[b, j] = quantise(weave(h_rows[b, j], name, after), name)
 
         pick(0, (0, 1))
-        load_saved(4, "saved0")
+        load_saved(3, "saved0")
         order_w1()
-        load_saved(5, "w1_raw")
+        load_saved(4, "w1_raw")
         pick(1, (0, 1))
-        load_saved(6, "saved1")
+        load_saved(5, "saved1")
         pick(2, (0, 1))
-        load_saved(7, "tab0")
+        load_saved(6, "tab1")
         pick(3, (0, 1))
-        load_w2(0, "tab1")
+        load_saved(7, "saved0")
         pick(4, (0, 1))
-        load_w2(1, "saved0")
+        load_w2(0, "w1_raw")
         for j in range(2):
             for u in range(4):
                 back(u, j)
-        back(4, 1)
         pick(5, (0,))
         pick(6, (0,))
         pick(7, (0,))
         pick(7, (1,))
         gains = held([P, S], F32, name="gains", tag="picked10")
         nc.sync.dma_start(out=gains[:], in_=wgo)
-        h00_woven = weave(h_rows[0, 0], "h00")
+        load_w2(1, "picked20")
+        early = held([P, 2, HALF, PACK], BF16, name="early_woven")
+        nc.scalar.copy(
+            out=early[:, 0].rearrange("p (c i) t -> p c t i", i=4),
+            in_=h_rows[0, 0][:].rearrange("p t (c i) -> p c t i", i=4),
+        )
         for u in range(4, 8):
             back(u, 0)
-        w2_woven = {tiles: weave_w2(tiles) for tiles in ((0,), (1,))}
-        quantise_w2((0,), w2_woven[0,])
-        finish_h(1, 0, "picked00")
+        for n in range(2):
+            nc.scalar.copy(
+                out=early[:, 1, 2 * P * n : 2 * P * (n + 1)].rearrange("p (b c i) t -> p b c t i", b=2, i=4),
+                in_=w2_raw[0][:, :, :, P * n : P * (n + 1)].rearrange("p b t (c i) -> p b c t i", i=4),
+            )
+        last_codes = held([P, HALF], U32, name="last_codes")
+        last_scale = held([P, HALF], U8, name="last_scale")
+        for part in range(2):
+            cols = slice(HALF // 2 * part, HALF // 2 * (part + 1))
+            woven = held([P, HALF // 2, PACK], BF16, name="last_woven%d" % part)
+            nc.scalar.copy(
+                out=woven[:].rearrange("p (c i) t -> p c t i", i=4),
+                in_=h_rows[1, 0][:, :, cols].rearrange("p t (c i) -> p c t i", i=4),
+            )
+            nc.vector.quantize_mx(
+                out=last_codes[:, cols].bitcast(E4M3X4),
+                scales=last_scale[:, cols],
+                in_=woven[:].rearrange("p c t -> p (c t)"),
+            )
+        h_codes[1, 0], h_scale[1, 0] = last_codes[:], last_scale[:]
+        early_codes = held([P, 2 * HALF], U32, name="early_codes", tag="picked50")
+        early_scale = held([P, 2 * HALF], U8, name="early_scale")
+        nc.vector.quantize_mx(
+            out=early_codes[:].bitcast(E4M3X4),
+            scales=early_scale[:],
+            in_=early[:].rearrange("p x c t -> p (x c t)"),
+        )
+        h_codes[0, 0], h_scale[0, 0] = early_codes[:, :HALF], early_scale[:, :HALF]
+        for n in range(2):
+            cols = slice(HALF + 2 * P * n, HALF + 2 * P * (n + 1))
+            w2_codes[n], w2_scale[n] = early_codes[:, cols], early_scale[:, cols]
         late5 = held([P, HALF], F32, name="late5", tag="picked60")
         pick(5, (1,), late5[:])
-        h_codes[0, 0], h_scale[0, 0] = quantise(h00_woven, "h00", "picked70")
-        quantise_w2((1,), w2_woven[1,])
-        late6 = held([P, HALF], F32, name="late6", tag="tab0")
+        back(4, 1)
+        late6 = held([P, HALF], F32, name="late6", tag="saved0")
         pick(6, (1,), late6[:])
         back(7, 1)
         back(5, 1)
@@ -286,14 +318,14 @@ def tile_list_hit_sensitivity_map_kernel(
         place(0, 0, HALF // 2)
         place(0, HALF // 2, HALF)
         w2_late = weave_w2((2, 3), "y2_0_256")
-        forward(1, 0, HALF, square_after="y2_0_0", log_after="saved0")
+        forward(1, 0, HALF, square_after="y2_0_0", log_after="picked20")
         quantise_w2((2, 3), w2_late)
         place(1, 0, HALF)
         finish_h(0, 1, "y2_0_0")
         forward(2, 0, HALF)
         place(2, 0, HALF)
         finish_h(1, 1, "y2_2_0")
-        forward(3, 0, HALF, square_after="h_rows11")
+        forward(3, 0, HALF, square_after="picked70")
         place(3, 0, HALF)
         for n in range(4):
             forward(n, HALF, S)

@@ -19,9 +19,12 @@ ACT = mybir.ActivationFunctionType
 P = 128
 PACK = 4
 PASS = P * PACK
-HALF = 512
-LIST_COLS = HALF // 16
+HALF = S // 2
+QUARTER = S // 4
+GROUP = 16
 ROW0 = 96
+GPSIMD_TILES = 4
+FIRST_BANKS, SECOND_BANKS = 5, 3
 
 
 def tile_list_hit_sensitivity_map_kernel(
@@ -30,30 +33,31 @@ def tile_list_hit_sensitivity_map_kernel(
     nc = tc.nc
     with ExitStack() as ctx:
         keep = ctx.enter_context(tc.tile_pool(name="keep", bufs=1))
-        psum1 = ctx.enter_context(tc.psum_pool(name="psum1", bufs=5))
-        psum2 = ctx.enter_context(tc.psum_pool(name="psum2", bufs=3))
+        psum1 = ctx.enter_context(tc.psum_pool(name="psum1", bufs=FIRST_BANKS))
+        psum2 = ctx.enter_context(tc.psum_pool(name="psum2", bufs=SECOND_BANKS))
 
-        def held(shape, dtype, name, tag=""):
-            return keep.tile(shape, dtype, name=name, tag=tag or name, align_bytes=64)
+        def held(shape, dtype, name, after=""):
+            return keep.tile(shape, dtype, name=name, tag=after or name, align_bytes=64)
 
-        idx = keep.tile([P, S // 16], U16, name="idx")
-        idx2 = keep.tile([P, S // 16], U16, name="idx2")
+        idx = keep.tile([P, S // GROUP], U16, name="idx")
+        idx2 = keep.tile([P, S // GROUP], U16, name="idx2")
+
         tab_bytes = held([P, T], U8, name="tab_bytes")
         w1_bytes = held([P, H], U8, name="w1_bytes")
-        pages = []
-
         nc.gpsimd.memset(tab_bytes[:].bitcast(I32)[:ROW0, :], 0)
         nc.gpsimd.memset(w1_bytes[:].bitcast(I32)[:ROW0, :], 0)
 
-        def new_page(after):
-            page = held([P, T2], F32, name="page%d" % len(pages), tag=after)
+        pages = []
+
+        def new_page(after=""):
+            page = held([P, T2], F32, name="page%d" % len(pages), after=after)
             nc.gpsimd.memset(page[:], 0.0)
             pages.append(page)
 
-        new_page("page0")
+        new_page()
         warm = held([P, 1], F32, name="warm")
         nc.scalar.activation(warm[:], pages[0][:, 0:1], ACT.Ln, bias=1.0)
-        new_page("page1")
+        new_page()
 
         def rows_of(x, b):
             return x[PASS * b : PASS * (b + 1), :].rearrange("(p t) c -> p t c", t=PACK)
@@ -61,15 +65,15 @@ def tile_list_hit_sensitivity_map_kernel(
         saved = {}
         w2_raw = {}
 
-        def load_saved(u, after):
-            saved[u] = held([P, T], F32, name="saved%d" % u, tag=after)
+        def load_saved(u, after=""):
+            saved[u] = held([P, T], F32, name="saved%d" % u, after=after)
             nc.sync.dma_start(out=saved[u][:], in_=rows_of(sT, u // PACK)[:, u % PACK, :])
 
-        def load_w2(half, after):
-            w2_raw[half] = held([P, 2, PACK, N // 2], F32, name="w2_raw%d" % half, tag=after)
+        def load_w2(side, after):
+            w2_raw[side] = held([P, 2, PACK, N // 2], F32, name="w2_raw%d" % side, after=after)
             for b in range(2):
                 nc.sync.dma_start(
-                    out=w2_raw[half][:, b], in_=rows_of(w2, b)[:, :, N // 2 * half : N // 2 * (half + 1)]
+                    out=w2_raw[side][:, b], in_=rows_of(w2, b)[:, :, N // 2 * side : N // 2 * (side + 1)]
                 )
 
         nc.sync.dma_start(idx[:], offs)
@@ -82,10 +86,10 @@ def tile_list_hit_sensitivity_map_kernel(
         tab = [held([P, T], I32, name="tab%d" % a) for a in range(2)]
         for a in range(2):
             nc.sync.dma_start(out=tab[a][:], in_=tab_words[a].rearrange("p t i -> p (t i)").bitcast(I32))
-        load_saved(0, "saved0")
+        load_saved(0)
         w1_raw = held([P, 2, H], I32, name="w1_raw")
         nc.sync.dma_start(out=w1_raw[:], in_=w1_words.rearrange("a p c i -> p a (c i)").bitcast(I32))
-        load_saved(1, "saved1")
+        load_saved(1)
         nc.sync.dma_start(idx2[:], offs2)
 
         v_bytes = held([P, S], U8, name="v_bytes")
@@ -96,28 +100,27 @@ def tile_list_hit_sensitivity_map_kernel(
             in_=w1_bytes[:].rearrange("p (b g m t) -> p b g t m", b=2, t=PACK, m=16),
         )
         nc.vector.tensor_copy(staged[:].bitcast(I32)[ROW0:, : S // 4], v_bytes[:].bitcast(I32)[ROW0:, :])
-        new_page("v_bytes")
+        new_page(after="v_bytes")
 
         v_scale = []
         w1_scale = []
 
-        def lay_plane(a):
-            plane = held([P, (S + H) // 4], I32, name="plane%d" % a)
-            for q in range(4):
+        def lay_scales(a):
+            rows = held([P, (S + H) // 4], I32, name="plane%d" % a)
+            for m in range(4):
                 nc.scalar.dma_start(
-                    out=plane[32 * q : 32 * q + 4, :],
-                    in_=staged[:].bitcast(I32)[ROW0 + 16 * a + 4 * q : ROW0 + 16 * a + 4 * q + 4, :],
+                    out=rows[m:P:32, :],
+                    in_=staged[:].bitcast(I32)[ROW0 + 16 * a + m : ROW0 + 16 * (a + 1) : 4, :],
                 )
-            v_scale.append(plane[:].bitcast(U8)[:, :S])
-            w1_scale.append(plane[:].bitcast(U8)[:, S:])
+            v_scale.append(rows[:].bitcast(U8)[:, :S])
+            w1_scale.append(rows[:].bitcast(U8)[:, S:])
 
         v_words = [held([P, S], U32, name="v_words%d" % a) for a in range(2)]
         for a in range(2):
-            lay_plane(a)
+            lay_scales(a)
             nc.vector.tensor_copy(v_words[a][:], tab[a][:].bitcast(U32).indirect(idx[:]))
-
-        new_page("tab0")
-        load_saved(2, "tab1")
+        new_page(after="tab0")
+        load_saved(2, after="tab1")
 
         w1_cols = held([P, 2 * H], I32, name="w1_cols")
 
@@ -133,17 +136,17 @@ def tile_list_hit_sensitivity_map_kernel(
         h_scale = {}
         w2_codes = {}
         w2_scale = {}
+        logs = {}
 
-        def pick(u, halves, picked=None):
+        def pick(u, halves, after=""):
             lo, hi = halves[0], halves[-1] + 1
-            if picked is None:
-                picked = held([P, HALF * len(halves)], F32, name="picked%d%d" % (u, lo))[:]
-            nc.vector.tensor_copy(picked, saved[u][:].indirect(idx[:, LIST_COLS * lo : LIST_COLS * hi]))
+            picked = held([P, HALF * len(halves)], F32, name="picked%d%d" % (u, lo), after=after)[:]
+            nc.vector.tensor_copy(picked, saved[u][:].indirect(idx[:, HALF * lo // GROUP : HALF * hi // GROUP]))
             nc.scalar.activation(picked, picked, ACT.Square)
             for j in halves:
                 squares[u, j] = picked[:, HALF * (j - lo) : HALF * (j - lo + 1)]
 
-        def back(u, j):
+        def back(u, j, rows_after=""):
             b, t = divmod(u, PACK)
             acc = psum1.tile([P, HALF], F32, name="acc1")
             for a in range(2):
@@ -157,63 +160,48 @@ def tile_list_hit_sensitivity_map_kernel(
                     stop=(a == 1),
                 )
             if t == 0:
-                tag = ("saved0", "picked70")[j] if b == 1 else ""
-                h_rows[b, j] = held([P, PACK, HALF], BF16, name="h_rows%d%d" % (b, j), tag=tag)
-            if u < 4:
-                slope = squares[u, j]
-                if j == 1:
-                    slope = held([P, HALF], F32, name="slope%d" % u, tag=("sums30", "slope30")[u % 2])[:]
-                elif u == 3:
-                    slope = held([P, HALF], F32, name="slope30")[:]
-                nc.gpsimd.tensor_scalar(slope, squares[u, j], 1.0, -1.0, ALU.mult, ALU.add)
-                sums = held([P, HALF], F32, name="sums%d%d" % (u, j))
-                nc.scalar.copy(out=sums[:], in_=acc[:])
-                nc.gpsimd.tensor_tensor(h_rows[b, j][:, t, :], slope, sums[:], ALU.mult)
-            else:
+                h_rows[b, j] = held([P, PACK, HALF], BF16, name="h_rows%d%d" % (b, j), after=rows_after)
+            if u >= GPSIMD_TILES:
                 nc.vector.scalar_tensor_tensor(
                     out=h_rows[b, j][:, t, :], in0=squares[u, j], scalar=1.0, in1=acc[:], op0=ALU.subtract, op1=ALU.mult
                 )
+                return
+            last = GPSIMD_TILES - 1
+            slope = squares[u, j]
+            if j == 1 and u > 0:
+                slope = held([P, HALF], F32, name="slope%d" % u, after=("sums%d0" % last, "slope%d0" % last)[u % 2])[:]
+            elif u == last:
+                slope = held([P, HALF], F32, name="slope%d0" % last)[:]
+            nc.gpsimd.tensor_scalar(slope, squares[u, j], 1.0, -1.0, ALU.mult, ALU.add)
+            sums = held([P, HALF], F32, name="sums%d%d" % (u, j))
+            nc.scalar.copy(out=sums[:], in_=acc[:])
+            nc.gpsimd.tensor_tensor(h_rows[b, j][:, t, :], slope, sums[:], ALU.mult)
 
-        def weave(rows, name, after=None):
-            woven = held([P, HALF, PACK], BF16, name=name + "_woven", tag=after or name + "_woven")
+        def weave_h(woven, rows):
             nc.scalar.copy(
-                out=woven[:].rearrange("p (c i) t -> p c t i", i=4),
-                in_=rows[:].rearrange("p t (c i) -> p c t i", i=4),
+                out=woven.rearrange("p (c i) t -> p c t i", i=4), in_=rows.rearrange("p t (c i) -> p c t i", i=4)
             )
-            return woven
 
-        def quantise(woven, name, after=""):
-            codes = held([P, HALF], U32, name=name + "_codes", tag=after)
-            scale = held([P, HALF], U8, name=name + "_scale")
-            nc.vector.quantize_mx(
-                out=codes[:].bitcast(E4M3X4), scales=scale[:], in_=woven[:].rearrange("p c t -> p (c t)")
+        def weave_w2(woven, n):
+            columns = w2_raw[n // 2][:, :, :, P * (n % 2) : P * (n % 2 + 1)]
+            nc.scalar.copy(
+                out=woven.rearrange("p (b c i) t -> p b c t i", b=2, i=4),
+                in_=columns.rearrange("p b t (c i) -> p b c t i", i=4),
             )
+
+        def quantise(woven, codes, scale):
+            nc.vector.quantize_mx(out=codes.bitcast(E4M3X4), scales=scale, in_=woven.rearrange("p c t -> p (c t)"))
+
+        def operand(width, name, after=""):
+            codes = held([P, width], U32, name=name + "_codes", after=after)
+            scale = held([P, width], U8, name=name + "_scale")
             return codes[:], scale[:]
 
-        def weave_w2(tiles, after=""):
-            count = len(tiles)
-            woven = held([P, count, 2, P, PACK], BF16, name="w2_woven%d" % tiles[0], tag=after)
-            for m, n in enumerate(tiles):
-                nc.scalar.copy(
-                    out=woven[:, m].rearrange("p b (c i) t -> p b c t i", i=4),
-                    in_=w2_raw[n // 2][:, :, :, P * (n % 2) : P * (n % 2 + 1)].rearrange(
-                        "p b t (c i) -> p b c t i", i=4
-                    ),
-                )
-            return woven
-
-        def quantise_w2(tiles, woven, after=""):
-            count = len(tiles)
-            codes = held([P, count * 2 * P], U32, name="w2_codes%d" % tiles[0], tag=after)
-            scale = held([P, count * 2 * P], U8, name="w2_scale%d" % tiles[0])
-            nc.vector.quantize_mx(
-                out=codes[:].bitcast(E4M3X4), scales=scale[:], in_=woven[:].rearrange("p m b c t -> p (m b c t)")
-            )
-            for m, n in enumerate(tiles):
-                w2_codes[n] = codes[:, 2 * P * m : 2 * P * (m + 1)]
-                w2_scale[n] = scale[:, 2 * P * m : 2 * P * (m + 1)]
-
-        logs = {}
+        def finish_h(b, j, after):
+            woven = held([P, HALF, PACK], BF16, name="h%d%d_woven" % (b, j), after=after)
+            weave_h(woven[:], h_rows[b, j][:])
+            h_codes[b, j], h_scale[b, j] = operand(HALF, "h%d%d" % (b, j))
+            quantise(woven[:], h_codes[b, j], h_scale[b, j])
 
         def forward(n, lo, hi, square_after="", log_after=""):
             acc = psum2.tile([P, hi - lo], F32, name="acc2")
@@ -228,106 +216,87 @@ def tile_list_hit_sensitivity_map_kernel(
                     start=(b == 0),
                     stop=(b == 1),
                 )
-            y2 = held([P, hi - lo], F32, name="y2_%d_%d" % (n, lo), tag=square_after)
+            y2 = held([P, hi - lo], F32, name="y2_%d_%d" % (n, lo), after=square_after)
             nc.scalar.activation(y2[:], acc[:], ACT.Square)
-            logs[n, lo] = held([P, hi - lo], F32, name="logs_%d_%d" % (n, lo), tag=log_after)
+            logs[n, lo] = held([P, hi - lo], F32, name="logs_%d_%d" % (n, lo), after=log_after)
             nc.scalar.activation(logs[n, lo][:], y2[:], ACT.Ln, bias=1.0)
 
         def place(n, lo, hi):
             nc.vector.tensor_tensor(
-                pages[n][:].indirect(idx2[:, lo // 16 : hi // 16]), logs[n, lo][:], gains[:, lo:hi], ALU.mult
+                pages[n][:].indirect(idx2[:, lo // GROUP : hi // GROUP]), logs[n, lo][:], gains[:, lo:hi], ALU.mult
             )
 
-        def store(n):
-            nc.sync.dma_start(out=out[P * n : P * (n + 1), :], in_=pages[n][:])
-
-        def finish_h(b, j, after=None):
-            name = "h%d%d" % (b, j)
-            h_codes[b, j], h_scale[b, j] = quantise(weave(h_rows[b, j], name, after), name)
-
         pick(0, (0, 1))
-        load_saved(3, "saved0")
+        load_saved(3, after="saved0")
         order_w1()
-        load_saved(4, "w1_raw")
+        load_saved(4, after="w1_raw")
         pick(1, (0, 1))
-        load_saved(5, "saved1")
+        load_saved(5, after="saved1")
         pick(2, (0, 1))
-        load_saved(6, "tab1")
+        load_saved(6, after="tab1")
         pick(3, (0, 1))
-        load_saved(7, "saved0")
+        load_saved(7, after="saved0")
         pick(4, (0, 1))
-        load_w2(0, "w1_raw")
+        load_w2(0, after="w1_raw")
         for j in range(2):
-            for u in range(4):
+            for u in range(GPSIMD_TILES):
                 back(u, j)
         pick(5, (0,))
         pick(6, (0,))
         pick(7, (0,))
         pick(7, (1,))
-        gains = held([P, S], F32, name="gains", tag="picked10")
+        gains = held([P, S], F32, name="gains", after="picked10")
         nc.sync.dma_start(out=gains[:], in_=wgo)
-        load_w2(1, "picked20")
-        early = held([P, 2, HALF, PACK], BF16, name="early_woven")
-        nc.scalar.copy(
-            out=early[:, 0].rearrange("p (c i) t -> p c t i", i=4),
-            in_=h_rows[0, 0][:].rearrange("p t (c i) -> p c t i", i=4),
-        )
-        for u in range(4, 8):
+        load_w2(1, after="picked20")
+
+        early = held([P, 2 * HALF, PACK], BF16, name="early_woven")
+        weave_h(early[:, :HALF], h_rows[0, 0][:])
+        back(4, 0, rows_after="saved0")
+        for u in range(5, 8):
             back(u, 0)
+        w2_cols = [slice(HALF + 2 * P * n, HALF + 2 * P * (n + 1)) for n in range(2)]
         for n in range(2):
-            nc.scalar.copy(
-                out=early[:, 1, 2 * P * n : 2 * P * (n + 1)].rearrange("p (b c i) t -> p b c t i", b=2, i=4),
-                in_=w2_raw[0][:, :, :, P * n : P * (n + 1)].rearrange("p b t (c i) -> p b c t i", i=4),
-            )
-        last_codes = held([P, HALF], U32, name="last_codes")
-        last_scale = held([P, HALF], U8, name="last_scale")
+            weave_w2(early[:, w2_cols[n]], n)
+        h_codes[1, 0], h_scale[1, 0] = operand(HALF, "last")
         for part in range(2):
-            cols = slice(HALF // 2 * part, HALF // 2 * (part + 1))
-            woven = held([P, HALF // 2, PACK], BF16, name="last_woven%d" % part)
-            nc.scalar.copy(
-                out=woven[:].rearrange("p (c i) t -> p c t i", i=4),
-                in_=h_rows[1, 0][:, :, cols].rearrange("p t (c i) -> p c t i", i=4),
-            )
-            nc.vector.quantize_mx(
-                out=last_codes[:, cols].bitcast(E4M3X4),
-                scales=last_scale[:, cols],
-                in_=woven[:].rearrange("p c t -> p (c t)"),
-            )
-        h_codes[1, 0], h_scale[1, 0] = last_codes[:], last_scale[:]
-        early_codes = held([P, 2 * HALF], U32, name="early_codes", tag="picked50")
-        early_scale = held([P, 2 * HALF], U8, name="early_scale")
-        nc.vector.quantize_mx(
-            out=early_codes[:].bitcast(E4M3X4),
-            scales=early_scale[:],
-            in_=early[:].rearrange("p x c t -> p (x c t)"),
-        )
+            cols = slice(QUARTER * part, QUARTER * (part + 1))
+            woven = held([P, QUARTER, PACK], BF16, name="last_woven%d" % part)
+            weave_h(woven[:], h_rows[1, 0][:, :, cols])
+            quantise(woven[:], h_codes[1, 0][:, cols], h_scale[1, 0][:, cols])
+        early_codes, early_scale = operand(2 * HALF, "early", after="picked50")
+        quantise(early[:], early_codes, early_scale)
         h_codes[0, 0], h_scale[0, 0] = early_codes[:, :HALF], early_scale[:, :HALF]
         for n in range(2):
-            cols = slice(HALF + 2 * P * n, HALF + 2 * P * (n + 1))
-            w2_codes[n], w2_scale[n] = early_codes[:, cols], early_scale[:, cols]
-        late5 = held([P, HALF], F32, name="late5", tag="picked60")
-        pick(5, (1,), late5[:])
-        back(4, 1)
-        late6 = held([P, HALF], F32, name="late6", tag="saved0")
-        pick(6, (1,), late6[:])
-        back(7, 1)
-        back(5, 1)
-        back(6, 1)
-        forward(0, 0, HALF // 2)
-        forward(0, HALF // 2, HALF)
-        place(0, 0, HALF // 2)
-        place(0, HALF // 2, HALF)
-        w2_late = weave_w2((2, 3), "y2_0_256")
+            w2_codes[n], w2_scale[n] = early_codes[:, w2_cols[n]], early_scale[:, w2_cols[n]]
+
+        pick(5, (1,), after="picked60")
+        back(4, 1, rows_after="picked70")
+        pick(6, (1,), after="saved0")
+        for u in (7, 5, 6):
+            back(u, 1)
+
+        for lo in (0, QUARTER):
+            forward(0, lo, lo + QUARTER)
+        for lo in (0, QUARTER):
+            place(0, lo, lo + QUARTER)
+        late = held([P, 4 * P, PACK], BF16, name="w2_woven2", after="y2_0_%d" % QUARTER)
+        late_cols = {n: slice(2 * P * (n - 2), 2 * P * (n - 1)) for n in (2, 3)}
+        for n in (2, 3):
+            weave_w2(late[:, late_cols[n]], n)
         forward(1, 0, HALF, square_after="y2_0_0", log_after="picked20")
-        quantise_w2((2, 3), w2_late)
+        late_codes, late_scale = operand(4 * P, "w2_late")
+        quantise(late[:], late_codes, late_scale)
+        for n in (2, 3):
+            w2_codes[n], w2_scale[n] = late_codes[:, late_cols[n]], late_scale[:, late_cols[n]]
         place(1, 0, HALF)
-        finish_h(0, 1, "y2_0_0")
+        finish_h(0, 1, after="y2_0_0")
         forward(2, 0, HALF)
         place(2, 0, HALF)
-        finish_h(1, 1, "y2_2_0")
+        finish_h(1, 1, after="y2_2_0")
         forward(3, 0, HALF, square_after="picked70")
         place(3, 0, HALF)
-        for n in range(4):
+
+        for n in range(N // P):
             forward(n, HALF, S)
             place(n, HALF, S)
-            store(n)
+            nc.sync.dma_start(out=out[P * n : P * (n + 1), :], in_=pages[n][:])

@@ -24,6 +24,12 @@ QUARTER = S // 4
 GROUP = 16
 ROW0 = 96
 GPSIMD_TILES = 4
+ROW = 8192
+PLACES = {
+    "saved2": 0, "saved6": 0, "tab1": 0, "early_codes": 0,
+    "saved1": ROW + 2048, "saved5": ROW + 2048, "tab0": ROW + 2048 + 64, "page3": 2 * ROW + 2048,
+    "page1": 3 * ROW + 2048, "v_bytes": 4 * ROW + 2048 - 512, "page2": 4 * ROW + 2048,
+}
 FIRST_BANKS, SECOND_BANKS = 5, 3
 
 
@@ -33,10 +39,13 @@ def tile_list_hit_sensitivity_map_kernel(
     nc = tc.nc
     with ExitStack() as ctx:
         keep = ctx.enter_context(tc.tile_pool(name="keep", bufs=1))
+        laid = ctx.enter_context(tc.tile_pool(name="laid", bufs=1))
         psum1 = ctx.enter_context(tc.psum_pool(name="psum1", bufs=FIRST_BANKS))
         psum2 = ctx.enter_context(tc.psum_pool(name="psum2", bufs=SECOND_BANKS))
 
         def held(shape, dtype, name, after=""):
+            if name in PLACES:
+                return laid.tile(shape, dtype, name=name, offset=PLACES[name], align_bytes=64)
             return keep.tile(shape, dtype, name=name, tag=after or name, align_bytes=64)
 
         idx = keep.tile([P, S // GROUP], U16, name="idx")
@@ -57,7 +66,6 @@ def tile_list_hit_sensitivity_map_kernel(
         new_page()
         warm = held([P, 1], F32, name="warm")
         nc.scalar.activation(warm[:], pages[0][:, 0:1], ACT.Ln, bias=1.0)
-        new_page()
 
         def rows_of(x, b):
             return x[PASS * b : PASS * (b + 1), :].rearrange("(p t) c -> p t c", t=PACK)
@@ -68,6 +76,13 @@ def tile_list_hit_sensitivity_map_kernel(
         def load_saved(u, after=""):
             saved[u] = held([P, T], F32, name="saved%d" % u, after=after)
             nc.sync.dma_start(out=saved[u][:], in_=rows_of(sT, u // PACK)[:, u % PACK, :])
+
+        w1_raw = {}
+
+        def load_w1(b):
+            w1_raw[b] = held([P, 2, PASS], I32, name="w1_raw%d" % b)
+            words = w1_words.rearrange("a p c i -> p a (c i)").bitcast(I32)
+            nc.sync.dma_start(out=w1_raw[b][:], in_=words[:, :, PASS * b : PASS * (b + 1)])
 
         def load_w2(side, after):
             w2_raw[side] = held([P, 2, PACK, N // 2], F32, name="w2_raw%d" % side, after=after)
@@ -83,24 +98,23 @@ def tile_list_hit_sensitivity_map_kernel(
         nc.sync.dma_start(
             out=w1_bytes[:].bitcast(I32)[ROW0:, :], in_=w1_scales.rearrange("a q c -> (a q) c").bitcast(I32)
         )
+        nc.sync.dma_start(idx2[:], offs2)
         tab = [held([P, T], I32, name="tab%d" % a) for a in range(2)]
         for a in range(2):
             nc.sync.dma_start(out=tab[a][:], in_=tab_words[a].rearrange("p t i -> p (t i)").bitcast(I32))
         load_saved(0)
-        w1_raw = held([P, 2, H], I32, name="w1_raw")
-        nc.sync.dma_start(out=w1_raw[:], in_=w1_words.rearrange("a p c i -> p a (c i)").bitcast(I32))
-        load_saved(1)
-        nc.sync.dma_start(idx2[:], offs2)
+
 
         v_bytes = held([P, S], U8, name="v_bytes")
         nc.vector.tensor_copy(v_bytes[:], tab_bytes[:].indirect(idx[:]))
         staged = held([P, S + H], U8, name="staged")
-        nc.vector.tensor_copy(
+        nc.gpsimd.tensor_copy(
             out=staged[:, S:].rearrange("p (b t g m) -> p b g t m", b=2, t=PACK, m=16),
             in_=w1_bytes[:].rearrange("p (b g m t) -> p b g t m", b=2, t=PACK, m=16),
         )
         nc.vector.tensor_copy(staged[:].bitcast(I32)[ROW0:, : S // 4], v_bytes[:].bitcast(I32)[ROW0:, :])
-        new_page(after="v_bytes")
+        new_page()
+        new_page()
 
         v_scale = []
         w1_scale = []
@@ -108,7 +122,7 @@ def tile_list_hit_sensitivity_map_kernel(
         def lay_scales(a):
             rows = held([P, (S + H) // 4], I32, name="plane%d" % a)
             for m in range(4):
-                nc.scalar.dma_start(
+                nc.sync.dma_start(
                     out=rows[m:P:32, :],
                     in_=staged[:].bitcast(I32)[ROW0 + 16 * a + m : ROW0 + 16 * (a + 1) : 4, :],
                 )
@@ -116,18 +130,22 @@ def tile_list_hit_sensitivity_map_kernel(
             w1_scale.append(rows[:].bitcast(U8)[:, S:])
 
         v_words = [held([P, S], U32, name="v_words%d" % a) for a in range(2)]
-        for a in range(2):
-            lay_scales(a)
-            nc.vector.tensor_copy(v_words[a][:], tab[a][:].bitcast(U32).indirect(idx[:]))
-        new_page(after="tab0")
-        load_saved(2, after="tab1")
+        lay_scales(0)
+        load_w1(0)
+        nc.vector.tensor_copy(v_words[0][:], tab[0][:].bitcast(U32).indirect(idx[:]))
+        load_saved(1)
+        lay_scales(1)
+        new_page()
+        nc.vector.tensor_copy(v_words[1][:], tab[1][:].bitcast(U32).indirect(idx[:]))
+        load_saved(2)
 
-        w1_cols = held([P, 2 * H], I32, name="w1_cols")
+        w1_cols = {}
 
-        def order_w1():
+        def order_w1(b):
+            w1_cols[b] = held([P, 2, PASS], I32, name="w1_cols%d" % b)
             nc.vector.tensor_copy(
-                out=w1_cols[:].rearrange("p (ab t g m) -> p ab g t m", ab=4, t=PACK, m=4),
-                in_=w1_raw[:].rearrange("p a (b g m t) -> p (a b) g t m", b=2, t=PACK, m=4),
+                out=w1_cols[b][:].rearrange("p a (t g m) -> p a g t m", t=PACK, m=4),
+                in_=w1_raw[b][:].rearrange("p a (g m t) -> p a g t m", t=PACK, m=4),
             )
 
         squares = {}
@@ -138,11 +156,16 @@ def tile_list_hit_sensitivity_map_kernel(
         w2_scale = {}
         logs = {}
 
-        def pick(u, halves, after=""):
+        def pick(u, halves, after="", square_after=""):
             lo, hi = halves[0], halves[-1] + 1
             picked = held([P, HALF * len(halves)], F32, name="picked%d%d" % (u, lo), after=after)[:]
             nc.vector.tensor_copy(picked, saved[u][:].indirect(idx[:, HALF * lo // GROUP : HALF * hi // GROUP]))
-            nc.scalar.activation(picked, picked, ACT.Square)
+            if square_after:
+                square = held([P, HALF * len(halves)], F32, name="square%d%d" % (u, lo), after=square_after)[:]
+                nc.scalar.activation(square, picked, ACT.Square)
+                picked = square
+            else:
+                nc.scalar.activation(picked, picked, ACT.Square)
             for j in halves:
                 squares[u, j] = picked[:, HALF * (j - lo) : HALF * (j - lo + 1)]
 
@@ -152,7 +175,7 @@ def tile_list_hit_sensitivity_map_kernel(
             for a in range(2):
                 nc.tensor.matmul_mx(
                     out=acc[:],
-                    lhsT=w1_cols[:, H * a + P * u : H * a + P * (u + 1)].bitcast(E4M3X4),
+                    lhsT=w1_cols[b][:, a, P * t : P * (t + 1)].bitcast(E4M3X4),
                     lhsT_scale=w1_scale[a][:, P * u : P * (u + 1)],
                     rhs=v_words[a][:, HALF * j : HALF * (j + 1)].bitcast(E5M2X4),
                     rhs_scale=v_scale[a][:, HALF * j : HALF * (j + 1)],
@@ -228,20 +251,22 @@ def tile_list_hit_sensitivity_map_kernel(
 
         pick(0, (0, 1))
         load_saved(3, after="saved0")
-        order_w1()
-        load_saved(4, after="w1_raw")
+        order_w1(0)
+        load_saved(4, after="w1_raw0")
+        load_w1(1)
         pick(1, (0, 1))
-        load_saved(5, after="saved1")
+        load_saved(5)
         pick(2, (0, 1))
-        load_saved(6, after="tab1")
+        load_saved(6)
         pick(3, (0, 1))
         load_saved(7, after="saved0")
         pick(4, (0, 1))
-        load_w2(0, after="w1_raw")
+        order_w1(1)
+        load_w2(0, after="w1_raw0")
         for j in range(2):
             for u in range(GPSIMD_TILES):
                 back(u, j)
-        pick(5, (0,))
+        pick(5, (0, 1))
         pick(6, (0,))
         pick(7, (0,))
         pick(7, (1,))
@@ -249,30 +274,31 @@ def tile_list_hit_sensitivity_map_kernel(
         nc.sync.dma_start(out=gains[:], in_=wgo)
         load_w2(1, after="picked20")
 
-        early = held([P, 2 * HALF, PACK], BF16, name="early_woven")
-        weave_h(early[:, :HALF], h_rows[0, 0][:])
         back(4, 0, rows_after="saved0")
         for u in range(5, 8):
             back(u, 0)
+        early = held([P, 2 * HALF, PACK], BF16, name="early_woven")
+        weave_h(early[:, :HALF], h_rows[0, 0][:])
         w2_cols = [slice(HALF + 2 * P * n, HALF + 2 * P * (n + 1)) for n in range(2)]
         for n in range(2):
             weave_w2(early[:, w2_cols[n]], n)
         h_codes[1, 0], h_scale[1, 0] = operand(HALF, "last")
+        quarters = []
         for part in range(2):
             cols = slice(QUARTER * part, QUARTER * (part + 1))
-            woven = held([P, QUARTER, PACK], BF16, name="last_woven%d" % part)
+            woven = held([P, QUARTER, PACK], BF16, name="last_woven%d" % part, after=("w1_raw0", "")[part])
             weave_h(woven[:], h_rows[1, 0][:, :, cols])
-            quantise(woven[:], h_codes[1, 0][:, cols], h_scale[1, 0][:, cols])
-        early_codes, early_scale = operand(2 * HALF, "early", after="picked50")
+            quarters.append((woven[:], h_codes[1, 0][:, cols], h_scale[1, 0][:, cols]))
+        pick(6, (1,), after="picked70", square_after="saved0")
+        early_codes, early_scale = operand(2 * HALF, "early")
         quantise(early[:], early_codes, early_scale)
         h_codes[0, 0], h_scale[0, 0] = early_codes[:, :HALF], early_scale[:, :HALF]
         for n in range(2):
             w2_codes[n], w2_scale[n] = early_codes[:, w2_cols[n]], early_scale[:, w2_cols[n]]
-
-        pick(5, (1,), after="picked60")
-        back(4, 1, rows_after="picked70")
-        pick(6, (1,), after="saved0")
-        for u in (7, 5, 6):
+        for part in range(2):
+            quantise(*quarters[part])
+        back(4, 1, rows_after="early_woven")
+        for u in (5, 7, 6):
             back(u, 1)
 
         for lo in (0, QUARTER):
@@ -293,7 +319,7 @@ def tile_list_hit_sensitivity_map_kernel(
         forward(2, 0, HALF)
         place(2, 0, HALF)
         finish_h(1, 1, after="y2_2_0")
-        forward(3, 0, HALF, square_after="picked70")
+        forward(3, 0, HALF, square_after="early_woven")
         place(3, 0, HALF)
 
         for n in range(N // P):

@@ -28,7 +28,6 @@ ROW = 8192
 PLACES = {
     "saved2": 0, "saved6": 0, "tab1": 0, "early_codes": 0,
     "saved1": ROW + 2048, "saved5": ROW + 2048, "tab0": ROW + 2048 + 64, "page3": 2 * ROW + 2048,
-    "page1": 3 * ROW + 2048, "v_bytes": 4 * ROW + 2048 - 512, "page2": 4 * ROW + 2048,
 }
 FIRST_BANKS, SECOND_BANKS = 5, 3
 
@@ -66,6 +65,7 @@ def tile_list_hit_sensitivity_map_kernel(
         new_page()
         warm = held([P, 1], F32, name="warm")
         nc.scalar.activation(warm[:], pages[0][:, 0:1], ACT.Ln, bias=1.0)
+        new_page()
 
         def rows_of(x, b):
             return x[PASS * b : PASS * (b + 1), :].rearrange("(p t) c -> p t c", t=PACK)
@@ -108,13 +108,12 @@ def tile_list_hit_sensitivity_map_kernel(
         v_bytes = held([P, S], U8, name="v_bytes")
         nc.vector.tensor_copy(v_bytes[:], tab_bytes[:].indirect(idx[:]))
         staged = held([P, S + H], U8, name="staged")
-        nc.gpsimd.tensor_copy(
+        nc.vector.tensor_copy(
             out=staged[:, S:].rearrange("p (b t g m) -> p b g t m", b=2, t=PACK, m=16),
             in_=w1_bytes[:].rearrange("p (b g m t) -> p b g t m", b=2, t=PACK, m=16),
         )
         nc.vector.tensor_copy(staged[:].bitcast(I32)[ROW0:, : S // 4], v_bytes[:].bitcast(I32)[ROW0:, :])
-        new_page()
-        new_page()
+        new_page(after="v_bytes")
 
         v_scale = []
         w1_scale = []
@@ -156,18 +155,23 @@ def tile_list_hit_sensitivity_map_kernel(
         w2_scale = {}
         logs = {}
 
-        def pick(u, halves, after="", square_after=""):
+        picks = {}
+
+        def pick(u, halves):
             lo, hi = halves[0], halves[-1] + 1
-            picked = held([P, HALF * len(halves)], F32, name="picked%d%d" % (u, lo), after=after)[:]
+            picked = held([P, HALF * len(halves)], F32, name="picked%d%d" % (u, lo))[:]
             nc.vector.tensor_copy(picked, saved[u][:].indirect(idx[:, HALF * lo // GROUP : HALF * hi // GROUP]))
-            if square_after:
-                square = held([P, HALF * len(halves)], F32, name="square%d%d" % (u, lo), after=square_after)[:]
-                nc.scalar.activation(square, picked, ACT.Square)
-                picked = square
-            else:
-                nc.scalar.activation(picked, picked, ACT.Square)
+            nc.scalar.activation(picked, picked, ACT.Square)
             for j in halves:
                 squares[u, j] = picked[:, HALF * (j - lo) : HALF * (j - lo + 1)]
+
+        def gather(u, j):
+            picks[u, j] = held([P, HALF], F32, name="picked%d%d" % (u, j))[:]
+            nc.vector.tensor_copy(picks[u, j], saved[u][:].indirect(idx[:, HALF * j // GROUP : HALF * (j + 1) // GROUP]))
+
+        def square(u, j, after):
+            squares[u, j] = held([P, HALF], F32, name="square%d%d" % (u, j), after=after)[:]
+            nc.scalar.activation(squares[u, j], picks[u, j], ACT.Square)
 
         def back(u, j, rows_after=""):
             b, t = divmod(u, PACK)
@@ -268,8 +272,9 @@ def tile_list_hit_sensitivity_map_kernel(
                 back(u, j)
         pick(5, (0, 1))
         pick(6, (0,))
+        gather(6, 1)
         pick(7, (0,))
-        pick(7, (1,))
+        gather(7, 1)
         gains = held([P, S], F32, name="gains", after="picked10")
         nc.sync.dma_start(out=gains[:], in_=wgo)
         load_w2(1, after="picked20")
@@ -289,7 +294,8 @@ def tile_list_hit_sensitivity_map_kernel(
             woven = held([P, QUARTER, PACK], BF16, name="last_woven%d" % part, after=("w1_raw0", "")[part])
             weave_h(woven[:], h_rows[1, 0][:, :, cols])
             quarters.append((woven[:], h_codes[1, 0][:, cols], h_scale[1, 0][:, cols]))
-        pick(6, (1,), after="picked70", square_after="saved0")
+        square(6, 1, after="saved0")
+        square(7, 1, after="picked61")
         early_codes, early_scale = operand(2 * HALF, "early")
         quantise(early[:], early_codes, early_scale)
         h_codes[0, 0], h_scale[0, 0] = early_codes[:, :HALF], early_scale[:, :HALF]
@@ -297,8 +303,8 @@ def tile_list_hit_sensitivity_map_kernel(
             w2_codes[n], w2_scale[n] = early_codes[:, w2_cols[n]], early_scale[:, w2_cols[n]]
         for part in range(2):
             quantise(*quarters[part])
-        back(4, 1, rows_after="early_woven")
-        for u in (5, 7, 6):
+        back(4, 1, rows_after="picked70")
+        for u in (5, 6, 7):
             back(u, 1)
 
         for lo in (0, QUARTER):
@@ -319,7 +325,7 @@ def tile_list_hit_sensitivity_map_kernel(
         forward(2, 0, HALF)
         place(2, 0, HALF)
         finish_h(1, 1, after="y2_2_0")
-        forward(3, 0, HALF, square_after="early_woven")
+        forward(3, 0, HALF, square_after="picked70")
         place(3, 0, HALF)
 
         for n in range(N // P):

@@ -25,10 +25,7 @@ GROUP = 16
 ROW0 = 96
 GPSIMD_TILES = 4
 ROW = 8192
-PLACES = {
-    "saved2": 0, "saved6": 0, "tab1": 0, "early_codes": 0,
-    "saved1": ROW + 2048, "saved5": ROW + 2048, "tab0": ROW + 2048 + 64, "page3": 2 * ROW + 2048,
-}
+PLACES = {"page2": 0, "v_bytes": ROW - 512, "page3": ROW}
 FIRST_BANKS, SECOND_BANKS = 5, 3
 
 
@@ -77,13 +74,6 @@ def tile_list_hit_sensitivity_map_kernel(
             saved[u] = held([P, T], F32, name="saved%d" % u, after=after)
             nc.sync.dma_start(out=saved[u][:], in_=rows_of(sT, u // PACK)[:, u % PACK, :])
 
-        w1_raw = {}
-
-        def load_w1(b):
-            w1_raw[b] = held([P, 2, PASS], I32, name="w1_raw%d" % b)
-            words = w1_words.rearrange("a p c i -> p a (c i)").bitcast(I32)
-            nc.sync.dma_start(out=w1_raw[b][:], in_=words[:, :, PASS * b : PASS * (b + 1)])
-
         def load_w2(side, after):
             w2_raw[side] = held([P, 2, PACK, N // 2], F32, name="w2_raw%d" % side, after=after)
             for b in range(2):
@@ -113,7 +103,8 @@ def tile_list_hit_sensitivity_map_kernel(
             in_=w1_bytes[:].rearrange("p (b g m t) -> p b g t m", b=2, t=PACK, m=16),
         )
         nc.vector.tensor_copy(staged[:].bitcast(I32)[ROW0:, : S // 4], v_bytes[:].bitcast(I32)[ROW0:, :])
-        new_page(after="v_bytes")
+        new_page()
+        new_page()
 
         v_scale = []
         w1_scale = []
@@ -130,13 +121,13 @@ def tile_list_hit_sensitivity_map_kernel(
 
         v_words = [held([P, S], U32, name="v_words%d" % a) for a in range(2)]
         lay_scales(0)
-        load_w1(0)
-        nc.vector.tensor_copy(v_words[0][:], tab[0][:].bitcast(U32).indirect(idx[:]))
         load_saved(1)
         lay_scales(1)
-        new_page()
-        nc.vector.tensor_copy(v_words[1][:], tab[1][:].bitcast(U32).indirect(idx[:]))
-        load_saved(2)
+        w1_raw = held([P, 2, H], I32, name="w1_raw")
+        nc.sync.dma_start(out=w1_raw[:], in_=w1_words.rearrange("a p c i -> p a (c i)").bitcast(I32))
+        for a in range(2):
+            nc.vector.tensor_copy(v_words[a][:], tab[a][:].bitcast(U32).indirect(idx[:]))
+            load_saved(2 + a, after="tab%d" % a)
 
         w1_cols = {}
 
@@ -144,7 +135,7 @@ def tile_list_hit_sensitivity_map_kernel(
             w1_cols[b] = held([P, 2, PASS], I32, name="w1_cols%d" % b)
             nc.vector.tensor_copy(
                 out=w1_cols[b][:].rearrange("p a (t g m) -> p a g t m", t=PACK, m=4),
-                in_=w1_raw[b][:].rearrange("p a (g m t) -> p a g t m", t=PACK, m=4),
+                in_=w1_raw[:, :, PASS * b : PASS * (b + 1)].rearrange("p a (g m t) -> p a g t m", t=PACK, m=4),
             )
 
         squares = {}
@@ -155,25 +146,18 @@ def tile_list_hit_sensitivity_map_kernel(
         w2_scale = {}
         logs = {}
 
-        picks = {}
+        def gather(picked, u, lo, hi):
+            nc.vector.tensor_copy(picked, saved[u][:].indirect(idx[:, lo // GROUP : hi // GROUP]))
+            nc.scalar.activation(picked, picked, ACT.Square)
 
         def pick(u, halves):
             lo, hi = halves[0], halves[-1] + 1
             picked = held([P, HALF * len(halves)], F32, name="picked%d%d" % (u, lo))[:]
-            nc.vector.tensor_copy(picked, saved[u][:].indirect(idx[:, HALF * lo // GROUP : HALF * hi // GROUP]))
-            nc.scalar.activation(picked, picked, ACT.Square)
+            gather(picked, u, HALF * lo, HALF * hi)
             for j in halves:
                 squares[u, j] = picked[:, HALF * (j - lo) : HALF * (j - lo + 1)]
 
-        def gather(u, j):
-            picks[u, j] = held([P, HALF], F32, name="picked%d%d" % (u, j))[:]
-            nc.vector.tensor_copy(picks[u, j], saved[u][:].indirect(idx[:, HALF * j // GROUP : HALF * (j + 1) // GROUP]))
-
-        def square(u, j, after):
-            squares[u, j] = held([P, HALF], F32, name="square%d%d" % (u, j), after=after)[:]
-            nc.scalar.activation(squares[u, j], picks[u, j], ACT.Square)
-
-        def back(u, j, rows_after=""):
+        def first_sum(u, j):
             b, t = divmod(u, PACK)
             acc = psum1.tile([P, HALF], F32, name="acc1")
             for a in range(2):
@@ -186,23 +170,29 @@ def tile_list_hit_sensitivity_map_kernel(
                     start=(a == 0),
                     stop=(a == 1),
                 )
+            return acc
+
+        def back(u, j, rows_after=""):
+            b, t = divmod(u, PACK)
+            acc = first_sum(u, j)
             if t == 0:
                 h_rows[b, j] = held([P, PACK, HALF], BF16, name="h_rows%d%d" % (b, j), after=rows_after)
-            if u >= GPSIMD_TILES:
-                nc.vector.scalar_tensor_tensor(
-                    out=h_rows[b, j][:, t, :], in0=squares[u, j], scalar=1.0, in1=acc[:], op0=ALU.subtract, op1=ALU.mult
-                )
-                return
-            last = GPSIMD_TILES - 1
-            slope = squares[u, j]
-            if j == 1 and u > 0:
-                slope = held([P, HALF], F32, name="slope%d" % u, after=("sums%d0" % last, "slope%d0" % last)[u % 2])[:]
-            elif u == last:
-                slope = held([P, HALF], F32, name="slope%d0" % last)[:]
-            nc.gpsimd.tensor_scalar(slope, squares[u, j], 1.0, -1.0, ALU.mult, ALU.add)
-            sums = held([P, HALF], F32, name="sums%d%d" % (u, j))
-            nc.scalar.copy(out=sums[:], in_=acc[:])
-            nc.gpsimd.tensor_tensor(h_rows[b, j][:, t, :], slope, sums[:], ALU.mult)
+            nc.vector.scalar_tensor_tensor(
+                out=h_rows[b, j][:, t, :], in0=squares[u, j], scalar=1.0, in1=acc[:], op0=ALU.subtract, op1=ALU.mult
+            )
+
+        slopes = [held([P, 2, S], F32, name="slopes%d" % q) for q in range(2)]
+
+        def back_pair(q, j, woven):
+            sums = held([P, 2, HALF], F32, name="sums%d%d" % (q, j))
+            for e in range(2):
+                nc.scalar.copy(out=sums[:, e, :], in_=first_sum(2 * q + e, j)[:])
+            nc.gpsimd.tensor_tensor(
+                woven[:, :, 2 * q : 2 * q + 2].rearrange("p (c i) t -> p c t i", i=4),
+                slopes[q][:, :, HALF * j : HALF * (j + 1)].rearrange("p t (c i) -> p c t i", i=4),
+                sums[:].rearrange("p t (c i) -> p c t i", i=4),
+                ALU.mult,
+            )
 
         def weave_h(woven, rows):
             nc.scalar.copy(
@@ -253,37 +243,36 @@ def tile_list_hit_sensitivity_map_kernel(
                 pages[n][:].indirect(idx2[:, lo // GROUP : hi // GROUP]), logs[n, lo][:], gains[:, lo:hi], ALU.mult
             )
 
-        pick(0, (0, 1))
-        load_saved(3, after="saved0")
+        for u in range(2):
+            gather(slopes[0][:, u, :], u, 0, S)
+            nc.scalar.activation(slopes[0][:, u, :], slopes[0][:, u, :], ACT.Identity, bias=-1.0)
+            load_saved(4 + u, after="saved%d" % u)
         order_w1(0)
-        load_saved(4, after="w1_raw0")
-        load_w1(1)
-        pick(1, (0, 1))
-        load_saved(5)
-        pick(2, (0, 1))
-        load_saved(6)
-        pick(3, (0, 1))
-        load_saved(7, after="saved0")
-        pick(4, (0, 1))
         order_w1(1)
-        load_w2(0, after="w1_raw0")
-        for j in range(2):
-            for u in range(GPSIMD_TILES):
-                back(u, j)
-        pick(5, (0, 1))
-        pick(6, (0,))
-        gather(6, 1)
-        pick(7, (0,))
-        gather(7, 1)
-        gains = held([P, S], F32, name="gains", after="picked10")
+        load_saved(6, after="w1_raw")
+        early = held([P, 2 * HALF, PACK], BF16, name="early_woven")
+        second = held([P, HALF, PACK], BF16, name="h01_woven")
+        back_pair(0, 0, early[:, :HALF])
+        back_pair(0, 1, second[:])
+        for u in range(2):
+            gather(slopes[1][:, u, :], 2 + u, 0, S)
+            nc.scalar.activation(slopes[1][:, u, :], slopes[1][:, u, :], ACT.Identity, bias=-1.0)
+        load_saved(7, after="tab0")
+        load_w2(0, after="tab1")
+        back_pair(1, 0, early[:, :HALF])
+        back_pair(1, 1, second[:])
+        pick(4, (0, 1))
+        gains = held([P, S], F32, name="gains", after="saved0")
         nc.sync.dma_start(out=gains[:], in_=wgo)
-        load_w2(1, after="picked20")
+        pick(5, (0, 1))
+        load_w2(1, after="saved1")
+        pick(6, (0, 1))
+        pick(7, (0,))
+        pick(7, (1,))
 
-        back(4, 0, rows_after="saved0")
+        back(4, 0, rows_after="tab0")
         for u in range(5, 8):
             back(u, 0)
-        early = held([P, 2 * HALF, PACK], BF16, name="early_woven")
-        weave_h(early[:, :HALF], h_rows[0, 0][:])
         w2_cols = [slice(HALF + 2 * P * n, HALF + 2 * P * (n + 1)) for n in range(2)]
         for n in range(2):
             weave_w2(early[:, w2_cols[n]], n)
@@ -291,21 +280,21 @@ def tile_list_hit_sensitivity_map_kernel(
         quarters = []
         for part in range(2):
             cols = slice(QUARTER * part, QUARTER * (part + 1))
-            woven = held([P, QUARTER, PACK], BF16, name="last_woven%d" % part, after=("w1_raw0", "")[part])
+            woven = held([P, QUARTER, PACK], BF16, name="last_woven%d" % part, after=("tab1", "")[part])
             weave_h(woven[:], h_rows[1, 0][:, :, cols])
             quarters.append((woven[:], h_codes[1, 0][:, cols], h_scale[1, 0][:, cols]))
-        square(6, 1, after="saved0")
-        square(7, 1, after="picked61")
-        early_codes, early_scale = operand(2 * HALF, "early")
+        early_codes, early_scale = operand(2 * HALF, "early", after="picked70")
         quantise(early[:], early_codes, early_scale)
         h_codes[0, 0], h_scale[0, 0] = early_codes[:, :HALF], early_scale[:, :HALF]
         for n in range(2):
             w2_codes[n], w2_scale[n] = early_codes[:, w2_cols[n]], early_scale[:, w2_cols[n]]
         for part in range(2):
             quantise(*quarters[part])
-        back(4, 1, rows_after="picked70")
+        back(4, 1, rows_after="tab1")
         for u in (5, 6, 7):
             back(u, 1)
+        h_codes[0, 1], h_scale[0, 1] = operand(HALF, "h01", after="last_woven1")
+        quantise(second[:], h_codes[0, 1], h_scale[0, 1])
 
         for lo in (0, QUARTER):
             forward(0, lo, lo + QUARTER)
@@ -315,18 +304,16 @@ def tile_list_hit_sensitivity_map_kernel(
         late_cols = {n: slice(2 * P * (n - 2), 2 * P * (n - 1)) for n in (2, 3)}
         for n in (2, 3):
             weave_w2(late[:, late_cols[n]], n)
-        forward(1, 0, HALF, square_after="y2_0_0", log_after="picked20")
+        forward(1, 0, HALF, square_after="y2_0_0", log_after="saved1")
         late_codes, late_scale = operand(4 * P, "w2_late")
         quantise(late[:], late_codes, late_scale)
         for n in (2, 3):
             w2_codes[n], w2_scale[n] = late_codes[:, late_cols[n]], late_scale[:, late_cols[n]]
         place(1, 0, HALF)
-        finish_h(0, 1, after="y2_0_0")
-        forward(2, 0, HALF)
-        place(2, 0, HALF)
-        finish_h(1, 1, after="y2_2_0")
-        forward(3, 0, HALF, square_after="picked70")
-        place(3, 0, HALF)
+        finish_h(1, 1, after="y2_0_0")
+        for n in (2, 3):
+            forward(n, 0, HALF)
+            place(n, 0, HALF)
 
         for n in range(N // P):
             forward(n, HALF, S)

@@ -121,22 +121,26 @@ def tile_list_hit_sensitivity_map_kernel(
 
         v_words = [held([P, S], U32, name="v_words%d" % a) for a in range(2)]
         lay_scales(0)
-        load_saved(1)
-        lay_scales(1)
-        w1_raw = held([P, 2, H], I32, name="w1_raw")
-        nc.sync.dma_start(out=w1_raw[:], in_=w1_words.rearrange("a p c i -> p a (c i)").bitcast(I32))
-        for a in range(2):
-            nc.vector.tensor_copy(v_words[a][:], tab[a][:].bitcast(U32).indirect(idx[:]))
-            load_saved(2 + a, after="tab%d" % a)
-
         w1_cols = {}
 
-        def order_w1(b):
+        def load_w1(b):
+            raw = held([P, 2, PASS], I32, name="w1_raw%d" % b)
+            words = w1_words.rearrange("a p c i -> p a (c i)").bitcast(I32)
+            nc.sync.dma_start(out=raw[:], in_=words[:, :, PASS * b : PASS * (b + 1)])
             w1_cols[b] = held([P, 2, PASS], I32, name="w1_cols%d" % b)
-            nc.vector.tensor_copy(
+            nc.gpsimd.tensor_copy(
                 out=w1_cols[b][:].rearrange("p a (t g m) -> p a g t m", t=PACK, m=4),
-                in_=w1_raw[:, :, PASS * b : PASS * (b + 1)].rearrange("p a (g m t) -> p a g t m", t=PACK, m=4),
+                in_=raw[:].rearrange("p a (g m t) -> p a g t m", t=PACK, m=4),
             )
+
+        load_w1(0)
+        load_saved(1)
+        lay_scales(1)
+        for a in range(2):
+            nc.vector.tensor_copy(v_words[a][:], tab[a][:].bitcast(U32).indirect(idx[:]))
+        load_saved(2, after="tab0")
+        load_saved(3, after="tab1")
+        load_w1(1)
 
         squares = {}
         h_rows = {}
@@ -181,12 +185,29 @@ def tile_list_hit_sensitivity_map_kernel(
                 out=h_rows[b, j][:, t, :], in0=squares[u, j], scalar=1.0, in1=acc[:], op0=ALU.subtract, op1=ALU.mult
             )
 
-        slopes = [held([P, 2, S], F32, name="slopes%d" % q) for q in range(2)]
+        slopes = [held([P, 2, S], F32, name="slopes%d" % q, after=("staged", "")[q]) for q in range(2)]
 
-        def back_pair(q, j, woven):
+        def slope(u):
+            row = slopes[u // 2][:, u % 2, :]
+            if u == 0:
+                picked = held([P, S], F32, name="picked00")[:]
+                gather(picked, u, 0, S)
+                nc.gpsimd.tensor_scalar(row, picked, 1.0, -1.0, ALU.mult, ALU.add)
+                return
+            nc.vector.tensor_copy(row, saved[u][:].indirect(idx[:]))
+
+        def finish_slope(u, j):
+            half = slopes[u // 2][:, u % 2, HALF * j : HALF * (j + 1)]
+            nc.scalar.activation(half, half, ACT.Square)
+            nc.scalar.activation(half, half, ACT.Identity, bias=-1.0)
+
+        def pair_sums(q, j):
             sums = held([P, 2, HALF], F32, name="sums%d%d" % (q, j))
             for e in range(2):
                 nc.scalar.copy(out=sums[:, e, :], in_=first_sum(2 * q + e, j)[:])
+            return sums
+
+        def back_pair(q, j, woven, sums):
             nc.gpsimd.tensor_tensor(
                 woven[:, :, 2 * q : 2 * q + 2].rearrange("p (c i) t -> p c t i", i=4),
                 slopes[q][:, :, HALF * j : HALF * (j + 1)].rearrange("p t (c i) -> p c t i", i=4),
@@ -243,24 +264,30 @@ def tile_list_hit_sensitivity_map_kernel(
                 pages[n][:].indirect(idx2[:, lo // GROUP : hi // GROUP]), logs[n, lo][:], gains[:, lo:hi], ALU.mult
             )
 
-        for u in range(2):
-            gather(slopes[0][:, u, :], u, 0, S)
-            nc.scalar.activation(slopes[0][:, u, :], slopes[0][:, u, :], ACT.Identity, bias=-1.0)
-            load_saved(4 + u, after="saved%d" % u)
-        order_w1(0)
-        order_w1(1)
-        load_saved(6, after="w1_raw")
-        early = held([P, 2 * HALF, PACK], BF16, name="early_woven")
-        second = held([P, HALF, PACK], BF16, name="h01_woven")
-        back_pair(0, 0, early[:, :HALF])
-        back_pair(0, 1, second[:])
-        for u in range(2):
-            gather(slopes[1][:, u, :], 2 + u, 0, S)
-            nc.scalar.activation(slopes[1][:, u, :], slopes[1][:, u, :], ACT.Identity, bias=-1.0)
+        slope(0)
+        load_saved(4, after="saved0")
+        slope(1)
+        sums = []
+        for j in range(2):
+            sums.append(pair_sums(0, j))
+            finish_slope(1, j)
+        load_saved(5, after="saved1")
+        load_saved(6, after="picked00")
+        early = held([P, HALF, PACK], BF16, name="early_woven")
+        second = held([P, HALF, PACK], BF16, name="h01_woven", after="w1_raw1")
+        back_pair(0, 0, early[:], sums[0])
+        back_pair(0, 1, second[:], sums[1])
+        slope(2)
+        slope(3)
+        sums = []
+        for j in range(2):
+            finish_slope(2, j)
+            sums.append(pair_sums(1, j))
+            finish_slope(3, j)
         load_saved(7, after="tab0")
         load_w2(0, after="tab1")
-        back_pair(1, 0, early[:, :HALF])
-        back_pair(1, 1, second[:])
+        back_pair(1, 0, early[:], sums[0])
+        back_pair(1, 1, second[:], sums[1])
         pick(4, (0, 1))
         gains = held([P, S], F32, name="gains", after="saved0")
         nc.sync.dma_start(out=gains[:], in_=wgo)
@@ -273,24 +300,23 @@ def tile_list_hit_sensitivity_map_kernel(
         back(4, 0, rows_after="tab0")
         for u in range(5, 8):
             back(u, 0)
-        w2_cols = [slice(HALF + 2 * P * n, HALF + 2 * P * (n + 1)) for n in range(2)]
-        for n in range(2):
-            weave_w2(early[:, w2_cols[n]], n)
-        h_codes[1, 0], h_scale[1, 0] = operand(HALF, "last")
-        quarters = []
+        h_codes[0, 0], h_scale[0, 0] = operand(HALF, "early", after="picked70")
+        quantise(early[:], h_codes[0, 0], h_scale[0, 0])
+        codes, scale = operand(2 * HALF, "last")
+        h_codes[1, 0], h_scale[1, 0] = codes[:, QUARTER : QUARTER + HALF], scale[:, QUARTER : QUARTER + HALF]
         for part in range(2):
-            cols = slice(QUARTER * part, QUARTER * (part + 1))
-            woven = held([P, QUARTER, PACK], BF16, name="last_woven%d" % part, after=("tab1", "")[part])
-            weave_h(woven[:], h_rows[1, 0][:, :, cols])
-            quarters.append((woven[:], h_codes[1, 0][:, cols], h_scale[1, 0][:, cols]))
-        early_codes, early_scale = operand(2 * HALF, "early", after="picked70")
-        quantise(early[:], early_codes, early_scale)
-        h_codes[0, 0], h_scale[0, 0] = early_codes[:, :HALF], early_scale[:, :HALF]
-        for n in range(2):
-            w2_codes[n], w2_scale[n] = early_codes[:, w2_cols[n]], early_scale[:, w2_cols[n]]
-        for part in range(2):
-            quantise(*quarters[part])
-        back(4, 1, rows_after="tab1")
+            woven = held([P, HALF, PACK], BF16, name="last_woven%d" % part)
+            w2_cols = slice(QUARTER * part, QUARTER * (part + 1))
+            h_cols = slice(QUARTER * (1 - part), QUARTER * (2 - part))
+            if part == 0:
+                weave_w2(woven[:, w2_cols], part)
+            weave_h(woven[:, h_cols], h_rows[1, 0][:, :, w2_cols])
+            if part == 1:
+                weave_w2(woven[:, w2_cols], part)
+            cols = slice(HALF * part, HALF * (part + 1))
+            quantise(woven[:], codes[:, cols], scale[:, cols])
+            w2_codes[part], w2_scale[part] = codes[:, cols][:, w2_cols], scale[:, cols][:, w2_cols]
+        back(4, 1, rows_after="early_woven")
         for u in (5, 6, 7):
             back(u, 1)
         h_codes[0, 1], h_scale[0, 1] = operand(HALF, "h01", after="last_woven1")

@@ -76,10 +76,13 @@ def tile_list_hit_sensitivity_map_kernel(
 
         def load_w2(side, after):
             w2_raw[side] = held([P, 2, PACK, N // 2], F32, name="w2_raw%d" % side, after=after)
-            for b in range(2):
-                nc.sync.dma_start(
-                    out=w2_raw[side][:, b], in_=rows_of(w2, b)[:, :, N // 2 * side : N // 2 * (side + 1)]
-                )
+            step = (P, 2 * P)[side]
+            for lo in range(0, 2 * P, step):
+                for b in range(2):
+                    nc.sync.dma_start(
+                        out=w2_raw[side][:, b, :, lo : lo + step],
+                        in_=rows_of(w2, b)[:, :, N // 2 * side + lo : N // 2 * side + lo + step],
+                    )
 
         nc.sync.dma_start(idx[:], offs)
         nc.sync.dma_start(
@@ -189,8 +192,8 @@ def tile_list_hit_sensitivity_map_kernel(
 
         def slope(u):
             row = slopes[u // 2][:, u % 2, :]
-            if u == 0:
-                picked = held([P, S], F32, name="picked00")[:]
+            if u < 2:
+                picked = held([P, S], F32, name="picked%d0" % u)[:]
                 gather(picked, u, 0, S)
                 nc.gpsimd.tensor_scalar(row, picked, 1.0, -1.0, ALU.mult, ALU.add)
                 return
@@ -266,11 +269,9 @@ def tile_list_hit_sensitivity_map_kernel(
 
         slope(0)
         load_saved(4, after="saved0")
+        sums = [pair_sums(0, 0)]
         slope(1)
-        sums = []
-        for j in range(2):
-            sums.append(pair_sums(0, j))
-            finish_slope(1, j)
+        sums.append(pair_sums(0, 1))
         load_saved(5, after="saved1")
         load_saved(6, after="picked00")
         early = held([P, HALF, PACK], BF16, name="early_woven")
@@ -326,20 +327,21 @@ def tile_list_hit_sensitivity_map_kernel(
             forward(0, lo, lo + QUARTER)
         for lo in (0, QUARTER):
             place(0, lo, lo + QUARTER)
-        late = held([P, 4 * P, PACK], BF16, name="w2_woven2", after="y2_0_%d" % QUARTER)
-        late_cols = {n: slice(2 * P * (n - 2), 2 * P * (n - 1)) for n in (2, 3)}
-        for n in (2, 3):
-            weave_w2(late[:, late_cols[n]], n)
-        forward(1, 0, HALF, square_after="y2_0_0", log_after="saved1")
-        late_codes, late_scale = operand(4 * P, "w2_late")
-        quantise(late[:], late_codes, late_scale)
-        for n in (2, 3):
-            w2_codes[n], w2_scale[n] = late_codes[:, late_cols[n]], late_scale[:, late_cols[n]]
+        def finish_w2(n, after):
+            woven = held([P, 2 * P, PACK], BF16, name="w2_woven%d" % n, after=after)
+            weave_w2(woven[:], n)
+            w2_codes[n], w2_scale[n] = operand(2 * P, "w2_late%d" % n)
+            quantise(woven[:], w2_codes[n], w2_scale[n])
+
+        forward(1, 0, HALF, square_after="y2_0_%d" % QUARTER)
+        finish_w2(2, after="y2_0_0")
         place(1, 0, HALF)
-        finish_h(1, 1, after="y2_0_0")
-        for n in (2, 3):
-            forward(n, 0, HALF)
-            place(n, 0, HALF)
+        finish_w2(3, after="y2_0_%d" % QUARTER)
+        forward(2, 0, HALF)
+        place(2, 0, HALF)
+        finish_h(1, 1, after="y2_2_0")
+        forward(3, 0, HALF, square_after="early_woven")
+        place(3, 0, HALF)
 
         for n in range(N // P):
             forward(n, HALF, S)

@@ -218,8 +218,8 @@ def tile_list_hit_sensitivity_map_kernel(
                 ALU.mult,
             )
 
-        def weave_h(woven, rows):
-            nc.scalar.copy(
+        def weave_h(woven, rows, copy=nc.scalar.copy):
+            copy(
                 out=woven.rearrange("p (c i) t -> p c t i", i=4), in_=rows.rearrange("p t (c i) -> p c t i", i=4)
             )
 
@@ -301,19 +301,17 @@ def tile_list_hit_sensitivity_map_kernel(
         back(4, 0, rows_after="tab0")
         for u in range(5, 8):
             back(u, 0)
-        h_codes[0, 0], h_scale[0, 0] = operand(HALF, "early", after="picked70")
-        quantise(early[:], h_codes[0, 0], h_scale[0, 0])
         codes, scale = operand(2 * HALF, "last")
         h_codes[1, 0], h_scale[1, 0] = codes[:, QUARTER : QUARTER + HALF], scale[:, QUARTER : QUARTER + HALF]
         for part in range(2):
             woven = held([P, HALF, PACK], BF16, name="last_woven%d" % part)
             w2_cols = slice(QUARTER * part, QUARTER * (part + 1))
             h_cols = slice(QUARTER * (1 - part), QUARTER * (2 - part))
+            weave_w2(woven[:, w2_cols], part)
+            weave_h(woven[:, h_cols], h_rows[1, 0][:, :, w2_cols], (nc.vector.tensor_copy, nc.scalar.copy)[part])
             if part == 0:
-                weave_w2(woven[:, w2_cols], part)
-            weave_h(woven[:, h_cols], h_rows[1, 0][:, :, w2_cols])
-            if part == 1:
-                weave_w2(woven[:, w2_cols], part)
+                h_codes[0, 0], h_scale[0, 0] = operand(HALF, "early", after="picked70")
+                quantise(early[:], h_codes[0, 0], h_scale[0, 0])
             cols = slice(HALF * part, HALF * (part + 1))
             quantise(woven[:], codes[:, cols], scale[:, cols])
             w2_codes[part], w2_scale[part] = codes[:, cols][:, w2_cols], scale[:, cols][:, w2_cols]
@@ -327,21 +325,20 @@ def tile_list_hit_sensitivity_map_kernel(
             forward(0, lo, lo + QUARTER)
         for lo in (0, QUARTER):
             place(0, lo, lo + QUARTER)
-        def finish_w2(n, after):
-            woven = held([P, 2 * P, PACK], BF16, name="w2_woven%d" % n, after=after)
-            weave_w2(woven[:], n)
-            w2_codes[n], w2_scale[n] = operand(2 * P, "w2_late%d" % n)
-            quantise(woven[:], w2_codes[n], w2_scale[n])
-
-        forward(1, 0, HALF, square_after="y2_0_%d" % QUARTER)
-        finish_w2(2, after="y2_0_0")
+        late = held([P, 4 * P, PACK], BF16, name="w2_woven2", after="y2_0_%d" % QUARTER)
+        late_cols = {n: slice(2 * P * (n - 2), 2 * P * (n - 1)) for n in (2, 3)}
+        for n in (2, 3):
+            weave_w2(late[:, late_cols[n]], n)
+        forward(1, 0, HALF, square_after="y2_0_0", log_after="saved1")
+        late_codes, late_scale = operand(4 * P, "w2_late")
+        quantise(late[:], late_codes, late_scale)
+        for n in (2, 3):
+            w2_codes[n], w2_scale[n] = late_codes[:, late_cols[n]], late_scale[:, late_cols[n]]
         place(1, 0, HALF)
-        finish_w2(3, after="y2_0_%d" % QUARTER)
-        forward(2, 0, HALF)
-        place(2, 0, HALF)
-        finish_h(1, 1, after="y2_2_0")
-        forward(3, 0, HALF, square_after="early_woven")
-        place(3, 0, HALF)
+        finish_h(1, 1, after="y2_0_0")
+        for n in (2, 3):
+            forward(n, 0, HALF)
+            place(n, 0, HALF)
 
         for n in range(N // P):
             forward(n, HALF, S)

@@ -294,13 +294,16 @@ def tile_list_hit_sensitivity_map_kernel(
         nc.sync.dma_start(out=gains[:], in_=wgo)
         pick(5, (0, 1))
         load_w2(1, after="saved1")
-        pick(6, (0, 1))
+        pick(6, (0,))
+        pick(6, (1,))
         pick(7, (0,))
         pick(7, (1,))
 
         back(4, 0, rows_after="tab0")
         for u in range(5, 8):
             back(u, 0)
+        h_codes[0, 0], h_scale[0, 0] = operand(HALF, "early", after="picked60")
+        quantise(early[:], h_codes[0, 0], h_scale[0, 0])
         codes, scale = operand(2 * HALF, "last")
         h_codes[1, 0], h_scale[1, 0] = codes[:, QUARTER : QUARTER + HALF], scale[:, QUARTER : QUARTER + HALF]
         for part in range(2):
@@ -310,12 +313,10 @@ def tile_list_hit_sensitivity_map_kernel(
             weave_w2(woven[:, w2_cols], part)
             weave_h(woven[:, h_cols], h_rows[1, 0][:, :, w2_cols], (nc.vector.tensor_copy, nc.scalar.copy)[part])
             if part == 0:
-                h_codes[0, 0], h_scale[0, 0] = operand(HALF, "early", after="picked70")
-                quantise(early[:], h_codes[0, 0], h_scale[0, 0])
+                back(4, 1, rows_after="early_woven")
             cols = slice(HALF * part, HALF * (part + 1))
             quantise(woven[:], codes[:, cols], scale[:, cols])
             w2_codes[part], w2_scale[part] = codes[:, cols][:, w2_cols], scale[:, cols][:, w2_cols]
-        back(4, 1, rows_after="early_woven")
         for u in (5, 6, 7):
             back(u, 1)
         h_codes[0, 1], h_scale[0, 1] = operand(HALF, "h01", after="last_woven1")
@@ -335,10 +336,11 @@ def tile_list_hit_sensitivity_map_kernel(
         for n in (2, 3):
             w2_codes[n], w2_scale[n] = late_codes[:, late_cols[n]], late_scale[:, late_cols[n]]
         place(1, 0, HALF)
-        finish_h(1, 1, after="y2_0_0")
-        for n in (2, 3):
-            forward(n, 0, HALF)
-            place(n, 0, HALF)
+        forward(2, 0, HALF)
+        place(2, 0, HALF)
+        finish_h(1, 1, after="y2_2_0")
+        forward(3, 0, HALF, square_after="early_woven")
+        place(3, 0, HALF)
 
         for n in range(N // P):
             forward(n, HALF, S)

@@ -23,9 +23,21 @@ HALF = S // 2
 QUARTER = S // 4
 GROUP = 16
 ROW0 = 96
-GPSIMD_TILES = 4
 ROW = 8192
-PLACES = {"page2": 0, "v_bytes": ROW - 512, "page3": ROW}
+
+PLACES = {
+    "page2": 0, "tab0": ROW - 64, "saved2": ROW, "saved6": ROW, "rows11": ROW, "y2_3_0": ROW,
+    "page3": 2 * ROW, "tab1": 3 * ROW - 64, "saved3": 3 * ROW, "saved7": 3 * ROW,
+    "h00_codes": 3 * ROW, "last_codes": 3 * ROW + 2048,
+    "saved0": 4 * ROW, "saved4": 4 * ROW, "w2_raw0": 4 * ROW, "w2_raw1": 4 * ROW + 4096,
+    "square71": 4 * ROW, "y2_0_256": 4 * ROW + 4096, "w2_woven2": 4 * ROW + 4096,
+    "v_bytes": 5 * ROW - 512,
+    "saved1": 5 * ROW, "saved5": 5 * ROW, "gains": 5 * ROW,
+    "w2_raw2": 6 * ROW - 64, "y2_2_0": 6 * ROW, "woven11": 6 * ROW,
+    "slopes00": 7 * ROW, "w1_cols0": 7 * ROW + 3072, "slopes01": 7 * ROW + 4096,
+    "slopes10": 8 * ROW, "picked1": 8 * ROW + 2048, "squares11": 8 * ROW + 4096, "slopes11": 8 * ROW,
+    "second_woven": 8 * ROW + 4096, "first_woven": 8 * ROW + 6144, "h01_codes": 8 * ROW + 6144,
+}
 FIRST_BANKS, SECOND_BANKS = 5, 3
 
 
@@ -54,8 +66,8 @@ def tile_list_hit_sensitivity_map_kernel(
 
         pages = []
 
-        def new_page(after=""):
-            page = held([P, T2], F32, name="page%d" % len(pages), after=after)
+        def new_page():
+            page = held([P, T2], F32, name="page%d" % len(pages))
             nc.gpsimd.memset(page[:], 0.0)
             pages.append(page)
 
@@ -69,20 +81,23 @@ def tile_list_hit_sensitivity_map_kernel(
 
         saved = {}
         w2_raw = {}
+        w1_raw = {}
 
-        def load_saved(u, after=""):
-            saved[u] = held([P, T], F32, name="saved%d" % u, after=after)
+        def load_saved(u):
+            saved[u] = held([P, T], F32, name="saved%d" % u)
             nc.sync.dma_start(out=saved[u][:], in_=rows_of(sT, u // PACK)[:, u % PACK, :])
 
-        def load_w2(side, after):
-            w2_raw[side] = held([P, 2, PACK, N // 2], F32, name="w2_raw%d" % side, after=after)
-            step = (P, 2 * P)[side]
-            for lo in range(0, 2 * P, step):
-                for b in range(2):
-                    nc.sync.dma_start(
-                        out=w2_raw[side][:, b, :, lo : lo + step],
-                        in_=rows_of(w2, b)[:, :, N // 2 * side + lo : N // 2 * side + lo + step],
-                    )
+        def load_w2(n, count):
+            raw = held([P, 2, PACK, P * count], F32, name="w2_raw%d" % n)
+            for b in range(2):
+                nc.sync.dma_start(out=raw[:, b], in_=rows_of(w2, b)[:, :, P * n : P * (n + count)])
+            for e in range(count):
+                w2_raw[n + e] = raw[:, :, :, P * e : P * (e + 1)]
+
+        def load_w1(b):
+            w1_raw[b] = held([P, 2, PASS], I32, name="w1_raw%d" % b, after="w1_raw0")
+            words = w1_words.rearrange("a p c i -> p a (c i)").bitcast(I32)
+            nc.sync.dma_start(out=w1_raw[b][:], in_=words[:, :, PASS * b : PASS * (b + 1)])
 
         nc.sync.dma_start(idx[:], offs)
         nc.sync.dma_start(
@@ -95,8 +110,7 @@ def tile_list_hit_sensitivity_map_kernel(
         tab = [held([P, T], I32, name="tab%d" % a) for a in range(2)]
         for a in range(2):
             nc.sync.dma_start(out=tab[a][:], in_=tab_words[a].rearrange("p t i -> p (t i)").bitcast(I32))
-        load_saved(0)
-
+        load_w1(0)
 
         v_bytes = held([P, S], U8, name="v_bytes")
         nc.vector.tensor_copy(v_bytes[:], tab_bytes[:].indirect(idx[:]))
@@ -106,8 +120,6 @@ def tile_list_hit_sensitivity_map_kernel(
             in_=w1_bytes[:].rearrange("p (b g m t) -> p b g t m", b=2, t=PACK, m=16),
         )
         nc.vector.tensor_copy(staged[:].bitcast(I32)[ROW0:, : S // 4], v_bytes[:].bitcast(I32)[ROW0:, :])
-        new_page()
-        new_page()
 
         v_scale = []
         w1_scale = []
@@ -122,144 +134,139 @@ def tile_list_hit_sensitivity_map_kernel(
             v_scale.append(rows[:].bitcast(U8)[:, :S])
             w1_scale.append(rows[:].bitcast(U8)[:, S:])
 
-        v_words = [held([P, S], U32, name="v_words%d" % a) for a in range(2)]
         lay_scales(0)
-        w1_cols = {}
-
-        def load_w1(b):
-            raw = held([P, 2, PASS], I32, name="w1_raw%d" % b)
-            words = w1_words.rearrange("a p c i -> p a (c i)").bitcast(I32)
-            nc.sync.dma_start(out=raw[:], in_=words[:, :, PASS * b : PASS * (b + 1)])
-            w1_cols[b] = held([P, 2, PASS], I32, name="w1_cols%d" % b)
-            nc.gpsimd.tensor_copy(
-                out=w1_cols[b][:].rearrange("p a (t g m) -> p a g t m", t=PACK, m=4),
-                in_=raw[:].rearrange("p a (g m t) -> p a g t m", t=PACK, m=4),
-            )
-
-        load_w1(0)
-        load_saved(1)
+        load_saved(0)
         lay_scales(1)
+        load_saved(1)
+        v_words = [held([P, S], U32, name="v_words%d" % a) for a in range(2)]
         for a in range(2):
             nc.vector.tensor_copy(v_words[a][:], tab[a][:].bitcast(U32).indirect(idx[:]))
-        load_saved(2, after="tab0")
-        load_saved(3, after="tab1")
+            new_page()
+            load_saved(2 + a)
+
+        w1_cols = {}
+
+        def order_w1(q):
+            w1_cols[q] = held([P, 2, 2 * P], U32, name="w1_cols%d" % q)
+            e = 2 * (q % 2)
+            nc.scalar.copy(
+                out=w1_cols[q][:].rearrange("p a (t g m) -> p a g t m", t=2, m=4),
+                in_=w1_raw[q // 2][:].bitcast(U32).rearrange("p a (g m t) -> p a g t m", t=PACK, m=4)[:, :, :, e : e + 2, :],
+            )
+
+        order_w1(0)
+        order_w1(1)
         load_w1(1)
 
-        squares = {}
-        h_rows = {}
-        h_codes = {}
-        h_scale = {}
+        banks = {}
+        sums = {}
+        slopes = {}
+        picked = {}
         w2_codes = {}
         w2_scale = {}
         logs = {}
 
-        def gather(picked, u, lo, hi):
-            nc.vector.tensor_copy(picked, saved[u][:].indirect(idx[:, lo // GROUP : hi // GROUP]))
-            nc.scalar.activation(picked, picked, ACT.Square)
-
-        def pick(u, halves):
-            lo, hi = halves[0], halves[-1] + 1
-            picked = held([P, HALF * len(halves)], F32, name="picked%d%d" % (u, lo))[:]
-            gather(picked, u, HALF * lo, HALF * hi)
-            for j in halves:
-                squares[u, j] = picked[:, HALF * (j - lo) : HALF * (j - lo + 1)]
-
         def first_sum(u, j):
-            b, t = divmod(u, PACK)
             acc = psum1.tile([P, HALF], F32, name="acc1")
             for a in range(2):
                 nc.tensor.matmul_mx(
                     out=acc[:],
-                    lhsT=w1_cols[b][:, a, P * t : P * (t + 1)].bitcast(E4M3X4),
+                    lhsT=w1_cols[u // 2][:, a, P * (u % 2) : P * (u % 2 + 1)].bitcast(E4M3X4),
                     lhsT_scale=w1_scale[a][:, P * u : P * (u + 1)],
                     rhs=v_words[a][:, HALF * j : HALF * (j + 1)].bitcast(E5M2X4),
                     rhs_scale=v_scale[a][:, HALF * j : HALF * (j + 1)],
                     start=(a == 0),
                     stop=(a == 1),
                 )
-            return acc
+            banks[u, j] = acc
 
-        def back(u, j, rows_after=""):
-            b, t = divmod(u, PACK)
-            acc = first_sum(u, j)
-            if t == 0:
-                h_rows[b, j] = held([P, PACK, HALF], BF16, name="h_rows%d%d" % (b, j), after=rows_after)
-            nc.vector.scalar_tensor_tensor(
-                out=h_rows[b, j][:, t, :], in0=squares[u, j], scalar=1.0, in1=acc[:], op0=ALU.subtract, op1=ALU.mult
-            )
+        def empty(u, j):
+            first_sum(u, j)
+            if u % 2 == 0:
+                sums[u // 2, j] = held([P, 2, HALF], F32, name="sums%d%d" % (u // 2, j))
+            nc.scalar.copy(out=sums[u // 2, j][:, u % 2, :], in_=banks[u, j][:])
 
-        slopes = [held([P, 2, S], F32, name="slopes%d" % q, after=("staged", "")[q]) for q in range(2)]
+        def pair_slot(u, j, after=""):
+            if (u // 2, j) not in slopes:
+                slopes[u // 2, j] = held([P, 2, HALF], F32, name="slopes%d%d" % (u // 2, j), after=after)
+            return slopes[u // 2, j][:, u % 2, :]
 
-        def slope(u):
-            row = slopes[u // 2][:, u % 2, :]
-            if u < 2:
-                picked = held([P, S], F32, name="picked%d0" % u)[:]
-                gather(picked, u, 0, S)
-                nc.gpsimd.tensor_scalar(row, picked, 1.0, -1.0, ALU.mult, ALU.add)
-                return
-            nc.vector.tensor_copy(row, saved[u][:].indirect(idx[:]))
+        def pick(u, pieces):
+            whole = held([P, S], F32, name="picked%d" % u)
+            width = S // pieces
+            for lo in range(0, S, width):
+                nc.vector.tensor_copy(
+                    whole[:, lo : lo + width], saved[u][:].indirect(idx[:, lo // GROUP : (lo + width) // GROUP])
+                )
+            for j in range(2):
+                picked[u, j] = whole[:, HALF * j : HALF * (j + 1)]
 
-        def finish_slope(u, j):
-            half = slopes[u // 2][:, u % 2, HALF * j : HALF * (j + 1)]
-            nc.scalar.activation(half, half, ACT.Square)
-            nc.scalar.activation(half, half, ACT.Identity, bias=-1.0)
+        def pick_half(u, j, into=None):
+            picked[u, j] = held([P, HALF], F32, name="picked%d%d" % (u, j))[:] if into is None else into
+            lo = HALF * j // GROUP
+            nc.vector.tensor_copy(picked[u, j], saved[u][:].indirect(idx[:, lo : lo + HALF // GROUP]))
 
-        def pair_sums(q, j):
-            sums = held([P, 2, HALF], F32, name="sums%d%d" % (q, j))
-            for e in range(2):
-                nc.scalar.copy(out=sums[:, e, :], in_=first_sum(2 * q + e, j)[:])
-            return sums
+        def square(u, j, into=None):
+            target = picked[u, j] if into is None else into
+            nc.scalar.activation(target, picked[u, j], ACT.Square)
+            picked[u, j] = target
 
-        def back_pair(q, j, woven, sums):
+        def less_one_gpsimd(x, into=None):
+            nc.gpsimd.tensor_scalar(x if into is None else into, x, 1.0, -1.0, ALU.mult, ALU.add)
+
+        def less_one_scalar(x):
+            nc.scalar.activation(x, x, ACT.Identity, bias=-1.0)
+
+        def by_fours(x, order):
+            return x.rearrange(order + " -> p c t i", i=4)
+
+        def back_pair(q, j, woven, cols=slice(0, HALF)):
+            e = 2 * (q % 2)
             nc.gpsimd.tensor_tensor(
-                woven[:, :, 2 * q : 2 * q + 2].rearrange("p (c i) t -> p c t i", i=4),
-                slopes[q][:, :, HALF * j : HALF * (j + 1)].rearrange("p t (c i) -> p c t i", i=4),
-                sums[:].rearrange("p t (c i) -> p c t i", i=4),
+                woven[:, :, e : e + 2],
+                slopes[q, j][:, :, cols].rearrange("p t c -> p c t"),
+                sums[q, j][:, :, cols].rearrange("p t c -> p c t"),
                 ALU.mult,
             )
 
-        def weave_h(woven, rows, copy=nc.scalar.copy):
-            copy(
-                out=woven.rearrange("p (c i) t -> p c t i", i=4), in_=rows.rearrange("p t (c i) -> p c t i", i=4)
+        def back(u, j, row):
+            nc.vector.scalar_tensor_tensor(
+                out=row, in0=picked[u, j], scalar=1.0, in1=banks[u, j][:], op0=ALU.subtract, op1=ALU.mult
             )
+
+        def weave_h(woven, rows):
+            nc.scalar.copy(out=by_fours(woven, "p (c i) t"), in_=by_fours(rows, "p t (c i)"))
 
         def weave_w2(woven, n):
-            columns = w2_raw[n // 2][:, :, :, P * (n % 2) : P * (n % 2 + 1)]
             nc.scalar.copy(
                 out=woven.rearrange("p (b c i) t -> p b c t i", b=2, i=4),
-                in_=columns.rearrange("p b t (c i) -> p b c t i", i=4),
+                in_=w2_raw[n].rearrange("p b t (c i) -> p b c t i", i=4),
             )
 
-        def quantise(woven, codes, scale):
-            nc.vector.quantize_mx(out=codes.bitcast(E4M3X4), scales=scale, in_=woven.rearrange("p c t -> p (c t)"))
-
-        def operand(width, name, after=""):
+        def quantise(woven, name, after=""):
+            width = woven.shape[1]
             codes = held([P, width], U32, name=name + "_codes", after=after)
             scale = held([P, width], U8, name=name + "_scale")
-            return codes[:], scale[:]
+            nc.vector.quantize_mx(
+                out=codes[:].bitcast(E4M3X4), scales=scale[:], in_=woven[:].rearrange("p c t -> p (c t)")
+            )
+            return codes, scale
 
-        def finish_h(b, j, after):
-            woven = held([P, HALF, PACK], BF16, name="h%d%d_woven" % (b, j), after=after)
-            weave_h(woven[:], h_rows[b, j][:])
-            h_codes[b, j], h_scale[b, j] = operand(HALF, "h%d%d" % (b, j))
-            quantise(woven[:], h_codes[b, j], h_scale[b, j])
-
-        def forward(n, lo, hi, square_after="", log_after=""):
+        def forward(n, lo, hi, operands, square_after=""):
             acc = psum2.tile([P, hi - lo], F32, name="acc2")
-            j, cols = lo // HALF, slice(lo % HALF, lo % HALF + hi - lo)
             for b in range(2):
                 nc.tensor.matmul_mx(
                     out=acc[:],
                     lhsT=w2_codes[n][:, P * b : P * (b + 1)].bitcast(E4M3X4),
                     lhsT_scale=w2_scale[n][:, P * b : P * (b + 1)],
-                    rhs=h_codes[b, j][:, cols].bitcast(E4M3X4),
-                    rhs_scale=h_scale[b, j][:, cols],
+                    rhs=operands[b][0].bitcast(E4M3X4),
+                    rhs_scale=operands[b][1],
                     start=(b == 0),
                     stop=(b == 1),
                 )
             y2 = held([P, hi - lo], F32, name="y2_%d_%d" % (n, lo), after=square_after)
             nc.scalar.activation(y2[:], acc[:], ACT.Square)
-            logs[n, lo] = held([P, hi - lo], F32, name="logs_%d_%d" % (n, lo), after=log_after)
+            logs[n, lo] = held([P, hi - lo], F32, name="logs_%d_%d" % (n, lo))
             nc.scalar.activation(logs[n, lo][:], y2[:], ACT.Ln, bias=1.0)
 
         def place(n, lo, hi):
@@ -267,82 +274,128 @@ def tile_list_hit_sensitivity_map_kernel(
                 pages[n][:].indirect(idx2[:, lo // GROUP : hi // GROUP]), logs[n, lo][:], gains[:, lo:hi], ALU.mult
             )
 
-        slope(0)
-        load_saved(4, after="saved0")
-        sums = [pair_sums(0, 0)]
-        slope(1)
-        sums.append(pair_sums(0, 1))
-        load_saved(5, after="saved1")
-        load_saved(6, after="picked00")
-        early = held([P, HALF, PACK], BF16, name="early_woven")
-        second = held([P, HALF, PACK], BF16, name="h01_woven", after="w1_raw1")
-        back_pair(0, 0, early[:], sums[0])
-        back_pair(0, 1, second[:], sums[1])
-        slope(2)
-        slope(3)
-        sums = []
-        for j in range(2):
-            finish_slope(2, j)
-            sums.append(pair_sums(1, j))
-            finish_slope(3, j)
-        load_saved(7, after="tab0")
-        load_w2(0, after="tab1")
-        back_pair(1, 0, early[:], sums[0])
-        back_pair(1, 1, second[:], sums[1])
-        pick(4, (0, 1))
-        gains = held([P, S], F32, name="gains", after="saved0")
-        nc.sync.dma_start(out=gains[:], in_=wgo)
-        pick(5, (0, 1))
-        load_w2(1, after="saved1")
-        pick(6, (0,))
-        pick(6, (1,))
-        pick(7, (0,))
-        pick(7, (1,))
+        woven0 = [held([P, HALF, PACK], BF16, name="woven0%d" % j) for j in range(2)]
 
-        back(4, 0, rows_after="tab0")
-        for u in range(5, 8):
-            back(u, 0)
-        h_codes[0, 0], h_scale[0, 0] = operand(HALF, "early", after="picked60")
-        quantise(early[:], h_codes[0, 0], h_scale[0, 0])
-        codes, scale = operand(2 * HALF, "last")
-        h_codes[1, 0], h_scale[1, 0] = codes[:, QUARTER : QUARTER + HALF], scale[:, QUARTER : QUARTER + HALF]
-        for part in range(2):
-            woven = held([P, HALF, PACK], BF16, name="last_woven%d" % part)
-            w2_cols = slice(QUARTER * part, QUARTER * (part + 1))
-            h_cols = slice(QUARTER * (1 - part), QUARTER * (2 - part))
-            weave_w2(woven[:, w2_cols], part)
-            weave_h(woven[:, h_cols], h_rows[1, 0][:, :, w2_cols], (nc.vector.tensor_copy, nc.scalar.copy)[part])
-            if part == 0:
-                back(4, 1, rows_after="early_woven")
-            cols = slice(HALF * part, HALF * (part + 1))
-            quantise(woven[:], codes[:, cols], scale[:, cols])
-            w2_codes[part], w2_scale[part] = codes[:, cols][:, w2_cols], scale[:, cols][:, w2_cols]
-        for u in (5, 6, 7):
-            back(u, 1)
-        h_codes[0, 1], h_scale[0, 1] = operand(HALF, "h01", after="last_woven1")
-        quantise(second[:], h_codes[0, 1], h_scale[0, 1])
+        for u, j in ((0, 0), (1, 0), (0, 1), (1, 1), (2, 0), (3, 0)):
+            empty(u, j)
+        pick(0, 1)
+        load_saved(4)
+        pick(1, 2)
+        load_saved(5)
+        for u, j in ((0, 0), (0, 1), (1, 0), (1, 1)):
+            square(u, j, pair_slot(u, j))
+        for u, j in ((0, 0), (0, 1), (1, 0)):
+            less_one_gpsimd(picked[u, j])
+        empty(2, 1)
+        empty(3, 1)
+        less_one_scalar(picked[1, 1])
+        back_pair(0, 0, woven0[0][:])
+        back_pair(0, 1, woven0[1][:])
+        pick(2, 1)
+        load_saved(6)
+        pick(3, 2)
+        load_saved(7)
+        squares11 = held([P, 2, HALF], F32, name="squares11")
+        square(2, 0, pair_slot(2, 0))
+        square(2, 1, squares11[:, 0, :])
+        square(3, 0, pair_slot(3, 0))
+        square(3, 1, squares11[:, 1, :])
+        less_one_gpsimd(picked[2, 0])
+        less_one_gpsimd(picked[3, 0])
+        back_pair(1, 0, woven0[0][:])
+        pair_slot(2, 1)
+        less_one_gpsimd(squares11[:].rearrange("p t c -> p (t c)"), slopes[1, 1][:].rearrange("p t c -> p (t c)"))
+        back_pair(1, 1, woven0[1][:])
+        order_w1(2)
+        order_w1(3)
+        pick(4, 1)
+        load_w2(0, 1)
+        load_w2(1, 1)
+        empty(4, 0)
+        square(4, 0, pair_slot(4, 0))
+        square(4, 1)
+        empty(5, 0)
+        pick_half(5, 0, pair_slot(5, 0))
+        pick_half(5, 1)
+        gains = held([P, S], F32, name="gains")
+        nc.sync.dma_start(out=gains[:, :HALF], in_=wgo[:, :HALF])
+        load_w2(2, 2)
+        nc.sync.dma_start(out=gains[:, HALF:], in_=wgo[:, HALF:])
+        square(5, 0)
+        square(5, 1)
+        less_one_scalar(slopes[2, 0][:].rearrange("p t c -> p (t c)"))
+        first = held([P, HALF, PACK], BF16, name="first_woven")
+        second = held([P, QUARTER, PACK], BF16, name="second_woven")
+        back_pair(2, 0, first[:, QUARTER:], slice(0, QUARTER))
+        back_pair(2, 0, second[:], slice(QUARTER, HALF))
+        pick_half(6, 0)
+        pick_half(6, 1)
+        square(6, 0)
+        square(6, 1)
+        rows11 = held([P, PACK, HALF], BF16, name="rows11")
+        rows10 = held([P, 2, HALF], BF16, name="rows10")
+        for u, j in ((4, 1), (5, 1), (6, 0), (7, 0), (6, 1), (7, 1)):
+            first_sum(u, j)
+            if u < 6:
+                back(u, j, rows11[:, u - PACK, :])
+        back(6, 0, rows10[:, 0, :])
+        pick_half(7, 0)
+        pick_half(7, 1)
+        square(7, 0)
+        back(7, 0, rows10[:, 1, :])
+        h00 = quantise(woven0[0], "h00")
+        back(6, 1, rows11[:, 2, :])
+        codes = held([P, 2 * HALF], U32, name="last_codes")
+        scale = held([P, 2 * HALF], U8, name="last_scale")
 
-        for lo in (0, QUARTER):
-            forward(0, lo, lo + QUARTER)
-        for lo in (0, QUARTER):
-            place(0, lo, lo + QUARTER)
-        late = held([P, 4 * P, PACK], BF16, name="w2_woven2", after="y2_0_%d" % QUARTER)
-        late_cols = {n: slice(2 * P * (n - 2), 2 * P * (n - 1)) for n in (2, 3)}
-        for n in (2, 3):
-            weave_w2(late[:, late_cols[n]], n)
-        forward(1, 0, HALF, square_after="y2_0_0", log_after="saved1")
-        late_codes, late_scale = operand(4 * P, "w2_late")
-        quantise(late[:], late_codes, late_scale)
-        for n in (2, 3):
-            w2_codes[n], w2_scale[n] = late_codes[:, late_cols[n]], late_scale[:, late_cols[n]]
+        def quantise_part(woven, lo):
+            cols = slice(lo, lo + woven.shape[1])
+            nc.vector.quantize_mx(
+                out=codes[:, cols].bitcast(E4M3X4), scales=scale[:, cols], in_=woven[:].rearrange("p c t -> p (c t)")
+            )
+
+        weave_w2(first[:, :QUARTER], 0)
+        weave_h(first[:, QUARTER:, 2:], rows10[:, :, :QUARTER])
+        quantise_part(first, 0)
+        h01 = quantise(woven0[1], "h01")
+        square(7, 1, held([P, HALF], F32, name="square71")[:])
+        back(7, 1, rows11[:, 3, :])
+        weave_h(second[:, :, 2:], rows10[:, :, QUARTER:])
+        quantise_part(second, HALF)
+        w2_codes[0], w2_scale[0] = codes[:, :QUARTER], scale[:, :QUARTER]
+        w2_codes[1], w2_scale[1] = codes[:, 3 * QUARTER :], scale[:, 3 * QUARTER :]
+
+        def first_half(lo, hi):
+            late = slice(QUARTER + lo, QUARTER + hi)
+            return [(h00[0][:, lo:hi], h00[1][:, lo:hi]), (codes[:, late], scale[:, late])]
+
+        def finish_w2(n, after=""):
+            woven = held([P, QUARTER, PACK], BF16, name="w2_woven%d" % n, after=after)
+            weave_w2(woven[:], n)
+            if n == 1:
+                quantise_part(woven, 3 * QUARTER)
+            else:
+                made = quantise(woven, "w2_%d" % n)
+                w2_codes[n], w2_scale[n] = made[0][:], made[1][:]
+
+        forward(0, 0, QUARTER, first_half(0, QUARTER), square_after="rows10")
+        place(0, 0, QUARTER)
+        finish_w2(1, after="rows10")
+        forward(0, QUARTER, HALF, first_half(QUARTER, HALF))
+        place(0, QUARTER, HALF)
+        finish_w2(2)
+        forward(1, 0, HALF, first_half(0, HALF))
         place(1, 0, HALF)
-        forward(2, 0, HALF)
+        finish_w2(3, after="y2_1_0")
+        forward(2, 0, HALF, first_half(0, HALF))
         place(2, 0, HALF)
-        finish_h(1, 1, after="y2_2_0")
-        forward(3, 0, HALF, square_after="early_woven")
+        woven11 = held([P, HALF, PACK], BF16, name="woven11")
+        weave_h(woven11[:], rows11[:])
+        h11 = quantise(woven11, "h11")
+        forward(3, 0, HALF, first_half(0, HALF))
         place(3, 0, HALF)
 
         for n in range(N // P):
-            forward(n, HALF, S)
+            forward(n, HALF, S, [(h01[0][:], h01[1][:]), (h11[0][:], h11[1][:])])
             place(n, HALF, S)
             nc.sync.dma_start(out=out[P * n : P * (n + 1), :], in_=pages[n][:])

@@ -26,17 +26,13 @@ ROW0 = 96
 ROW = 8192
 
 PLACES = {
-    "page2": 0, "tab0": ROW - 64, "saved2": ROW, "saved6": ROW, "rows11": ROW, "y2_3_0": ROW,
-    "page3": 2 * ROW, "tab1": 3 * ROW - 64, "saved3": 3 * ROW, "saved7": 3 * ROW,
-    "h00_codes": 3 * ROW, "last_codes": 3 * ROW + 2048,
-    "saved0": 4 * ROW, "saved4": 4 * ROW, "w2_raw0": 4 * ROW, "w2_raw1": 4 * ROW + 4096,
-    "square71": 4 * ROW, "y2_0_256": 4 * ROW + 4096, "w2_woven2": 4 * ROW + 4096,
+    "page2": 0, "tab0": ROW - 64, "saved2": ROW, "saved6": ROW, "w2_raw2": ROW, "y2_2_0": ROW, "woven11": ROW,
+    "page3": 2 * ROW, "tab1": 3 * ROW - 64, "saved3": 3 * ROW, "saved7": 3 * ROW, "h00_codes": 3 * ROW, "h01_codes": 3 * ROW + 2048,
+    "saved0": 4 * ROW, "saved4": 4 * ROW, "w1_raw1": 4 * ROW, "squares7": 4 * ROW,
     "v_bytes": 5 * ROW - 512,
-    "saved1": 5 * ROW, "saved5": 5 * ROW, "gains": 5 * ROW,
-    "w2_raw2": 6 * ROW - 64, "y2_2_0": 6 * ROW, "woven11": 6 * ROW,
+    "saved1": 5 * ROW + 64, "saved5": 5 * ROW + 64, "w2_raw0": 5 * ROW - 0, "w2_raw1": 5 * ROW + 4096, "gains": 6 * ROW,
     "slopes00": 7 * ROW, "w1_cols0": 7 * ROW + 3072, "slopes01": 7 * ROW + 4096,
-    "slopes10": 8 * ROW, "picked1": 8 * ROW + 2048, "squares11": 8 * ROW + 4096, "slopes11": 8 * ROW,
-    "second_woven": 8 * ROW + 4096, "first_woven": 8 * ROW + 6144, "h01_codes": 8 * ROW + 6144,
+    "slopes10": 8 * ROW, "picked1": 8 * ROW + 2048, "squares11": 8 * ROW + 4096, "squares4": 8 * ROW + 4096,
 }
 FIRST_BANKS, SECOND_BANKS = 5, 3
 
@@ -95,7 +91,7 @@ def tile_list_hit_sensitivity_map_kernel(
                 w2_raw[n + e] = raw[:, :, :, P * e : P * (e + 1)]
 
         def load_w1(b):
-            w1_raw[b] = held([P, 2, PASS], I32, name="w1_raw%d" % b, after="w1_raw0")
+            w1_raw[b] = held([P, 2, PASS], I32, name="w1_raw%d" % b)
             words = w1_words.rearrange("a p c i -> p a (c i)").bitcast(I32)
             nc.sync.dma_start(out=w1_raw[b][:], in_=words[:, :, PASS * b : PASS * (b + 1)])
 
@@ -156,7 +152,6 @@ def tile_list_hit_sensitivity_map_kernel(
 
         order_w1(0)
         order_w1(1)
-        load_w1(1)
 
         banks = {}
         sums = {}
@@ -198,24 +193,25 @@ def tile_list_hit_sensitivity_map_kernel(
                 nc.vector.tensor_copy(
                     whole[:, lo : lo + width], saved[u][:].indirect(idx[:, lo // GROUP : (lo + width) // GROUP])
                 )
+            picked[u] = whole[:]
             for j in range(2):
                 picked[u, j] = whole[:, HALF * j : HALF * (j + 1)]
-
-        def pick_half(u, j, into=None):
-            picked[u, j] = held([P, HALF], F32, name="picked%d%d" % (u, j))[:] if into is None else into
-            lo = HALF * j // GROUP
-            nc.vector.tensor_copy(picked[u, j], saved[u][:].indirect(idx[:, lo : lo + HALF // GROUP]))
 
         def square(u, j, into=None):
             target = picked[u, j] if into is None else into
             nc.scalar.activation(target, picked[u, j], ACT.Square)
             picked[u, j] = target
 
+        def square_whole(u, into):
+            nc.scalar.activation(into, picked[u], ACT.Square)
+            for j in range(2):
+                picked[u, j] = into[:, HALF * j : HALF * (j + 1)]
+
         def less_one_gpsimd(x, into=None):
             nc.gpsimd.tensor_scalar(x if into is None else into, x, 1.0, -1.0, ALU.mult, ALU.add)
 
-        def less_one_scalar(x):
-            nc.scalar.activation(x, x, ACT.Identity, bias=-1.0)
+        def less_one_scalar(x, into=None):
+            nc.scalar.activation(x if into is None else into, x, ACT.Identity, bias=-1.0)
 
         def by_fours(x, order):
             return x.rearrange(order + " -> p c t i", i=4)
@@ -234,8 +230,8 @@ def tile_list_hit_sensitivity_map_kernel(
                 out=row, in0=picked[u, j], scalar=1.0, in1=banks[u, j][:], op0=ALU.subtract, op1=ALU.mult
             )
 
-        def weave_h(woven, rows):
-            nc.scalar.copy(out=by_fours(woven, "p (c i) t"), in_=by_fours(rows, "p t (c i)"))
+        def weave_h(woven, rows, copy=nc.scalar.copy):
+            copy(out=by_fours(woven, "p (c i) t"), in_=by_fours(rows, "p t (c i)"))
 
         def weave_w2(woven, n):
             nc.scalar.copy(
@@ -300,99 +296,74 @@ def tile_list_hit_sensitivity_map_kernel(
         square(2, 1, squares11[:, 0, :])
         square(3, 0, pair_slot(3, 0))
         square(3, 1, squares11[:, 1, :])
-        less_one_gpsimd(picked[2, 0])
-        less_one_gpsimd(picked[3, 0])
+        less_one_scalar(slopes[1, 0][:].rearrange("p t c -> p (t c)"))
         back_pair(1, 0, woven0[0][:])
         pair_slot(2, 1)
-        less_one_gpsimd(squares11[:].rearrange("p t c -> p (t c)"), slopes[1, 1][:].rearrange("p t c -> p (t c)"))
+        less_one_scalar(squares11[:].rearrange("p t c -> p (t c)"), slopes[1, 1][:].rearrange("p t c -> p (t c)"))
         back_pair(1, 1, woven0[1][:])
-        order_w1(2)
-        order_w1(3)
         pick(4, 1)
+        load_w1(1)
+        square_whole(4, held([P, S], F32, name="squares4")[:])
+        pick(5, 1)
         load_w2(0, 1)
         load_w2(1, 1)
-        empty(4, 0)
-        square(4, 0, pair_slot(4, 0))
-        square(4, 1)
-        empty(5, 0)
-        pick_half(5, 0, pair_slot(5, 0))
-        pick_half(5, 1)
         gains = held([P, S], F32, name="gains")
-        nc.sync.dma_start(out=gains[:, :HALF], in_=wgo[:, :HALF])
+        nc.sync.dma_start(out=gains[:], in_=wgo)
+        square_whole(5, picked[5])
+        pick(6, 1)
         load_w2(2, 2)
-        nc.sync.dma_start(out=gains[:, HALF:], in_=wgo[:, HALF:])
-        square(5, 0)
-        square(5, 1)
-        less_one_scalar(slopes[2, 0][:].rearrange("p t c -> p (t c)"))
-        first = held([P, HALF, PACK], BF16, name="first_woven")
-        second = held([P, QUARTER, PACK], BF16, name="second_woven")
-        back_pair(2, 0, first[:, QUARTER:], slice(0, QUARTER))
-        back_pair(2, 0, second[:], slice(QUARTER, HALF))
-        pick_half(6, 0)
-        pick_half(6, 1)
-        square(6, 0)
-        square(6, 1)
-        rows11 = held([P, PACK, HALF], BF16, name="rows11")
-        rows10 = held([P, 2, HALF], BF16, name="rows10")
-        for u, j in ((4, 1), (5, 1), (6, 0), (7, 0), (6, 1), (7, 1)):
-            first_sum(u, j)
-            if u < 6:
-                back(u, j, rows11[:, u - PACK, :])
-        back(6, 0, rows10[:, 0, :])
-        pick_half(7, 0)
-        pick_half(7, 1)
-        square(7, 0)
-        back(7, 0, rows10[:, 1, :])
+        square_whole(6, picked[6])
+        pick(7, 1)
+        order_w1(2)
+        order_w1(3)
+        square_whole(7, held([P, S], F32, name="squares7")[:])
         h00 = quantise(woven0[0], "h00")
-        back(6, 1, rows11[:, 2, :])
+        h01 = quantise(woven0[1], "h01")
+        rows10 = held([P, PACK, HALF], BF16, name="rows10")
+        rows11 = held([P, PACK, HALF], BF16, name="rows11")
+        for u in range(PACK, 2 * PACK):
+            first_sum(u, 0)
+            back(u, 0, rows10[:, u - PACK, :])
         codes = held([P, 2 * HALF], U32, name="last_codes")
         scale = held([P, 2 * HALF], U8, name="last_scale")
-
-        def quantise_part(woven, lo):
-            cols = slice(lo, lo + woven.shape[1])
+        for part in range(2):
+            woven = held([P, HALF, PACK], BF16, name="last_woven%d" % part)
+            w2_cols = slice(QUARTER * part, QUARTER * (part + 1))
+            h_cols = slice(QUARTER * (1 - part), QUARTER * (2 - part))
+            weave_w2(woven[:, w2_cols], part)
+            weave_h(woven[:, h_cols], rows10[:, :, w2_cols], (nc.vector.tensor_copy, nc.scalar.copy)[part])
+            cols = slice(HALF * part, HALF * (part + 1))
             nc.vector.quantize_mx(
                 out=codes[:, cols].bitcast(E4M3X4), scales=scale[:, cols], in_=woven[:].rearrange("p c t -> p (c t)")
             )
-
-        weave_w2(first[:, :QUARTER], 0)
-        weave_h(first[:, QUARTER:, 2:], rows10[:, :, :QUARTER])
-        quantise_part(first, 0)
-        h01 = quantise(woven0[1], "h01")
-        square(7, 1, held([P, HALF], F32, name="square71")[:])
-        back(7, 1, rows11[:, 3, :])
-        weave_h(second[:, :, 2:], rows10[:, :, QUARTER:])
-        quantise_part(second, HALF)
-        w2_codes[0], w2_scale[0] = codes[:, :QUARTER], scale[:, :QUARTER]
-        w2_codes[1], w2_scale[1] = codes[:, 3 * QUARTER :], scale[:, 3 * QUARTER :]
+            w2_codes[part], w2_scale[part] = codes[:, cols][:, w2_cols], scale[:, cols][:, w2_cols]
+        for u in range(PACK, 2 * PACK):
+            first_sum(u, 1)
+            back(u, 1, rows11[:, u - PACK, :])
 
         def first_half(lo, hi):
             late = slice(QUARTER + lo, QUARTER + hi)
             return [(h00[0][:, lo:hi], h00[1][:, lo:hi]), (codes[:, late], scale[:, late])]
 
-        def finish_w2(n, after=""):
-            woven = held([P, QUARTER, PACK], BF16, name="w2_woven%d" % n, after=after)
-            weave_w2(woven[:], n)
-            if n == 1:
-                quantise_part(woven, 3 * QUARTER)
-            else:
-                made = quantise(woven, "w2_%d" % n)
-                w2_codes[n], w2_scale[n] = made[0][:], made[1][:]
-
-        forward(0, 0, QUARTER, first_half(0, QUARTER), square_after="rows10")
-        place(0, 0, QUARTER)
-        finish_w2(1, after="rows10")
-        forward(0, QUARTER, HALF, first_half(QUARTER, HALF))
-        place(0, QUARTER, HALF)
-        finish_w2(2)
-        forward(1, 0, HALF, first_half(0, HALF))
+        for lo in (0, QUARTER):
+            forward(0, lo, lo + QUARTER, first_half(lo, lo + QUARTER))
+        for lo in (0, QUARTER):
+            place(0, lo, lo + QUARTER)
+        late = held([P, 4 * P, PACK], BF16, name="w2_woven2", after="y2_0_%d" % QUARTER)
+        late_cols = {n: slice(2 * P * (n - 2), 2 * P * (n - 1)) for n in (2, 3)}
+        for n in (2, 3):
+            weave_w2(late[:, late_cols[n]], n)
+        forward(1, 0, HALF, first_half(0, HALF), square_after="y2_0_0")
+        late_codes, late_scale = quantise(late, "w2_late")
+        for n in (2, 3):
+            w2_codes[n], w2_scale[n] = late_codes[:, late_cols[n]], late_scale[:, late_cols[n]]
         place(1, 0, HALF)
-        finish_w2(3, after="y2_1_0")
         forward(2, 0, HALF, first_half(0, HALF))
         place(2, 0, HALF)
         woven11 = held([P, HALF, PACK], BF16, name="woven11")
         weave_h(woven11[:], rows11[:])
         h11 = quantise(woven11, "h11")
-        forward(3, 0, HALF, first_half(0, HALF))
+        forward(3, 0, HALF, first_half(0, HALF), square_after="rows11")
         place(3, 0, HALF)
 
         for n in range(N // P):

@@ -26,11 +26,12 @@ ROW0 = 96
 ROW = 8192
 
 PLACES = {
-    "page2": 0, "tab0": ROW - 64, "saved2": ROW, "saved6": ROW, "w2_raw2": ROW, "y2_2_0": ROW, "woven11": ROW,
-    "page3": 2 * ROW, "tab1": 3 * ROW - 64, "saved3": 3 * ROW, "saved7": 3 * ROW, "h00_codes": 3 * ROW, "h01_codes": 3 * ROW + 2048,
-    "saved0": 4 * ROW, "saved4": 4 * ROW, "w1_raw1": 4 * ROW, "squares7": 4 * ROW,
+    "page2": 0, "tab0": ROW - 64, "saved2": ROW, "saved6": ROW,
+    "page3": 2 * ROW, "tab1": 3 * ROW - 64, "saved3": 3 * ROW, "saved7": 3 * ROW,
+    "saved0": 4 * ROW, "saved4": 4 * ROW, "w2_raw0": 4 * ROW, "w2_raw1": 4 * ROW + 4096,
     "v_bytes": 5 * ROW - 512,
-    "saved1": 5 * ROW + 64, "saved5": 5 * ROW + 64, "w2_raw0": 5 * ROW - 0, "w2_raw1": 5 * ROW + 4096, "gains": 6 * ROW,
+    "saved1": 5 * ROW + 64, "saved5": 5 * ROW + 64,  "gains": 5 * ROW,
+    "w2_raw2": 6 * ROW, "y2_2_0": 6 * ROW, "woven11": 6 * ROW,
     "slopes00": 7 * ROW, "w1_cols0": 7 * ROW + 3072, "slopes01": 7 * ROW + 4096,
     "slopes10": 8 * ROW, "picked1": 8 * ROW + 2048, "squares11": 8 * ROW + 4096, "squares4": 8 * ROW + 4096,
 }
@@ -91,7 +92,7 @@ def tile_list_hit_sensitivity_map_kernel(
                 w2_raw[n + e] = raw[:, :, :, P * e : P * (e + 1)]
 
         def load_w1(b):
-            w1_raw[b] = held([P, 2, PASS], I32, name="w1_raw%d" % b)
+            w1_raw[b] = held([P, 2, PASS], I32, name="w1_raw%d" % b, after="w1_raw0")
             words = w1_words.rearrange("a p c i -> p a (c i)").bitcast(I32)
             nc.sync.dma_start(out=w1_raw[b][:], in_=words[:, :, PASS * b : PASS * (b + 1)])
 
@@ -152,6 +153,7 @@ def tile_list_hit_sensitivity_map_kernel(
 
         order_w1(0)
         order_w1(1)
+        load_w1(1)
 
         banks = {}
         sums = {}
@@ -196,6 +198,11 @@ def tile_list_hit_sensitivity_map_kernel(
             picked[u] = whole[:]
             for j in range(2):
                 picked[u, j] = whole[:, HALF * j : HALF * (j + 1)]
+
+        def pick_half(u, j):
+            picked[u, j] = held([P, HALF], F32, name="picked%d%d" % (u, j))[:]
+            lo = HALF * j // GROUP
+            nc.vector.tensor_copy(picked[u, j], saved[u][:].indirect(idx[:, lo : lo + HALF // GROUP]))
 
         def square(u, j, into=None):
             target = picked[u, j] if into is None else into
@@ -301,29 +308,32 @@ def tile_list_hit_sensitivity_map_kernel(
         pair_slot(2, 1)
         less_one_scalar(squares11[:].rearrange("p t c -> p (t c)"), slopes[1, 1][:].rearrange("p t c -> p (t c)"))
         back_pair(1, 1, woven0[1][:])
-        pick(4, 1)
-        load_w1(1)
-        square_whole(4, held([P, S], F32, name="squares4")[:])
-        pick(5, 1)
-        load_w2(0, 1)
-        load_w2(1, 1)
-        gains = held([P, S], F32, name="gains")
-        nc.sync.dma_start(out=gains[:], in_=wgo)
-        square_whole(5, picked[5])
-        pick(6, 1)
-        load_w2(2, 2)
-        square_whole(6, picked[6])
-        pick(7, 1)
         order_w1(2)
         order_w1(3)
-        square_whole(7, held([P, S], F32, name="squares7")[:])
-        h00 = quantise(woven0[0], "h00")
-        h01 = quantise(woven0[1], "h01")
-        rows10 = held([P, PACK, HALF], BF16, name="rows10")
-        rows11 = held([P, PACK, HALF], BF16, name="rows11")
-        for u in range(PACK, 2 * PACK):
+        pick(4, 1)
+        load_w2(0, 1)
+        load_w2(1, 1)
+        square_whole(4, held([P, S], F32, name="squares4")[:])
+        pick(5, 1)
+        gains = held([P, S], F32, name="gains")
+        nc.sync.dma_start(out=gains[:], in_=wgo)
+        load_w2(2, 2)
+        square_whole(5, picked[5])
+        pick_half(6, 0)
+        pick_half(6, 1)
+        square(6, 0, held([P, HALF], F32, name="square60")[:])
+        square(6, 1)
+        rows10 = held([P, PACK, HALF], BF16, name="rows10", after="picked60")
+        for u in range(PACK, 2 * PACK - 1):
             first_sum(u, 0)
             back(u, 0, rows10[:, u - PACK, :])
+        pick_half(7, 0)
+        pick_half(7, 1)
+        square(7, 0, held([P, HALF], F32, name="square70")[:])
+        square(7, 1)
+        first_sum(7, 0)
+        back(7, 0, rows10[:, PACK - 1, :])
+        h00 = quantise(woven0[0], "h00", after="picked70")
         codes = held([P, 2 * HALF], U32, name="last_codes")
         scale = held([P, 2 * HALF], U8, name="last_scale")
         for part in range(2):
@@ -332,11 +342,14 @@ def tile_list_hit_sensitivity_map_kernel(
             h_cols = slice(QUARTER * (1 - part), QUARTER * (2 - part))
             weave_w2(woven[:, w2_cols], part)
             weave_h(woven[:, h_cols], rows10[:, :, w2_cols], (nc.vector.tensor_copy, nc.scalar.copy)[part])
+            if part == 0:
+                h01 = quantise(woven0[1], "h01", after="square70")
             cols = slice(HALF * part, HALF * (part + 1))
             nc.vector.quantize_mx(
                 out=codes[:, cols].bitcast(E4M3X4), scales=scale[:, cols], in_=woven[:].rearrange("p c t -> p (c t)")
             )
             w2_codes[part], w2_scale[part] = codes[:, cols][:, w2_cols], scale[:, cols][:, w2_cols]
+        rows11 = held([P, PACK, HALF], BF16, name="rows11", after="woven01")
         for u in range(PACK, 2 * PACK):
             first_sum(u, 1)
             back(u, 1, rows11[:, u - PACK, :])
@@ -363,7 +376,7 @@ def tile_list_hit_sensitivity_map_kernel(
         woven11 = held([P, HALF, PACK], BF16, name="woven11")
         weave_h(woven11[:], rows11[:])
         h11 = quantise(woven11, "h11")
-        forward(3, 0, HALF, first_half(0, HALF), square_after="rows11")
+        forward(3, 0, HALF, first_half(0, HALF), square_after="woven01")
         place(3, 0, HALF)
 
         for n in range(N // P):

@@ -27,10 +27,11 @@ ROW = 8192
 
 PLACES = {
     "page2": 0, "tab0": ROW - 64, "saved2": ROW, "saved6": ROW,
-    "page3": 2 * ROW, "tab1": 3 * ROW - 64, "saved3": 3 * ROW, "saved7": 3 * ROW,
-    "saved0": 4 * ROW, "saved4": 4 * ROW, "w2_raw0": 4 * ROW, "w2_raw1": 4 * ROW + 4096,
+    "page3": 2 * ROW, "tab1": 3 * ROW - 64, "saved3": 3 * ROW, "w2_raw0": 3 * ROW, "square70": 3 * ROW, "h01_codes": 3 * ROW,
+    "saved0": 4 * ROW, "saved4": 4 * ROW, "saved7": 4 * ROW,
     "v_bytes": 5 * ROW - 512,
-    "saved1": 5 * ROW + 64, "saved5": 5 * ROW + 64,  "gains": 5 * ROW,
+    "saved1": 5 * ROW + 64, "saved5": 5 * ROW + 64,
+    "w2_raw1": 5 * ROW, "gains": 5 * ROW + 4096,
     "w2_raw2": 6 * ROW, "y2_2_0": 6 * ROW, "woven11": 6 * ROW,
     "slopes00": 7 * ROW, "w1_cols0": 7 * ROW + 3072, "slopes01": 7 * ROW + 4096,
     "slopes10": 8 * ROW, "picked1": 8 * ROW + 2048, "squares11": 8 * ROW + 4096, "squares4": 8 * ROW + 4096,
@@ -297,7 +298,7 @@ def tile_list_hit_sensitivity_map_kernel(
         pick(2, 1)
         load_saved(6)
         pick(3, 2)
-        load_saved(7)
+        load_w2(0, 1)
         squares11 = held([P, 2, HALF], F32, name="squares11")
         square(2, 0, pair_slot(2, 0))
         square(2, 1, squares11[:, 0, :])
@@ -311,10 +312,10 @@ def tile_list_hit_sensitivity_map_kernel(
         order_w1(2)
         order_w1(3)
         pick(4, 1)
-        load_w2(0, 1)
-        load_w2(1, 1)
+        load_saved(7)
         square_whole(4, held([P, S], F32, name="squares4")[:])
         pick(5, 1)
+        load_w2(1, 1)
         gains = held([P, S], F32, name="gains")
         nc.sync.dma_start(out=gains[:], in_=wgo)
         load_w2(2, 2)
@@ -327,29 +328,34 @@ def tile_list_hit_sensitivity_map_kernel(
         for u in range(PACK, 2 * PACK - 1):
             first_sum(u, 0)
             back(u, 0, rows10[:, u - PACK, :])
+        first = held([P, HALF, PACK], BF16, name="first_woven")
+        weave_w2(first[:, :QUARTER], 0)
         pick_half(7, 0)
         pick_half(7, 1)
         square(7, 0, held([P, HALF], F32, name="square70")[:])
-        square(7, 1)
         first_sum(7, 0)
         back(7, 0, rows10[:, PACK - 1, :])
         h00 = quantise(woven0[0], "h00", after="picked70")
         codes = held([P, 2 * HALF], U32, name="last_codes")
         scale = held([P, 2 * HALF], U8, name="last_scale")
-        for part in range(2):
-            woven = held([P, HALF, PACK], BF16, name="last_woven%d" % part)
-            w2_cols = slice(QUARTER * part, QUARTER * (part + 1))
-            h_cols = slice(QUARTER * (1 - part), QUARTER * (2 - part))
-            weave_w2(woven[:, w2_cols], part)
-            weave_h(woven[:, h_cols], rows10[:, :, w2_cols], (nc.vector.tensor_copy, nc.scalar.copy)[part])
-            if part == 0:
-                h01 = quantise(woven0[1], "h01", after="square70")
-            cols = slice(HALF * part, HALF * (part + 1))
+        w2_codes[0], w2_scale[0] = codes[:, :QUARTER], scale[:, :QUARTER]
+        w2_codes[1], w2_scale[1] = codes[:, 3 * QUARTER :], scale[:, 3 * QUARTER :]
+
+        def quantise_part(woven, lo):
+            cols = slice(lo, lo + woven.shape[1])
             nc.vector.quantize_mx(
                 out=codes[:, cols].bitcast(E4M3X4), scales=scale[:, cols], in_=woven[:].rearrange("p c t -> p (c t)")
             )
-            w2_codes[part], w2_scale[part] = codes[:, cols][:, w2_cols], scale[:, cols][:, w2_cols]
-        rows11 = held([P, PACK, HALF], BF16, name="rows11", after="woven01")
+
+        h01 = quantise(woven0[1], "h01")
+        second = held([P, HALF, PACK], BF16, name="second_woven")
+        weave_w2(second[:, QUARTER:], 1)
+        weave_h(first[:, QUARTER:], rows10[:, :, :QUARTER])
+        quantise_part(first, 0)
+        weave_h(second[:, :QUARTER], rows10[:, :, QUARTER:])
+        quantise_part(second, HALF)
+        square(7, 1, held([P, HALF], F32, name="square71", after="picked60")[:])
+        rows11 = held([P, PACK, HALF], BF16, name="rows11", after="first_woven")
         for u in range(PACK, 2 * PACK):
             first_sum(u, 1)
             back(u, 1, rows11[:, u - PACK, :])
@@ -358,25 +364,26 @@ def tile_list_hit_sensitivity_map_kernel(
             late = slice(QUARTER + lo, QUARTER + hi)
             return [(h00[0][:, lo:hi], h00[1][:, lo:hi]), (codes[:, late], scale[:, late])]
 
-        for lo in (0, QUARTER):
-            forward(0, lo, lo + QUARTER, first_half(lo, lo + QUARTER))
-        for lo in (0, QUARTER):
-            place(0, lo, lo + QUARTER)
-        late = held([P, 4 * P, PACK], BF16, name="w2_woven2", after="y2_0_%d" % QUARTER)
-        late_cols = {n: slice(2 * P * (n - 2), 2 * P * (n - 1)) for n in (2, 3)}
-        for n in (2, 3):
-            weave_w2(late[:, late_cols[n]], n)
-        forward(1, 0, HALF, first_half(0, HALF), square_after="y2_0_0")
-        late_codes, late_scale = quantise(late, "w2_late")
-        for n in (2, 3):
-            w2_codes[n], w2_scale[n] = late_codes[:, late_cols[n]], late_scale[:, late_cols[n]]
+        def finish_w2(n, after):
+            woven = held([P, QUARTER, PACK], BF16, name="w2_woven%d" % n, after=after)
+            weave_w2(woven[:], n)
+            made = quantise(woven, "w2_%d" % n)
+            w2_codes[n], w2_scale[n] = made[0][:], made[1][:]
+
+        forward(0, 0, QUARTER, first_half(0, QUARTER), square_after="picked71")
+        forward(0, QUARTER, HALF, first_half(QUARTER, HALF))
+        place(0, 0, QUARTER)
+        place(0, QUARTER, HALF)
+        finish_w2(2, after="y2_0_256")
+        forward(1, 0, HALF, first_half(0, HALF), square_after="picked71")
         place(1, 0, HALF)
+        finish_w2(3, after="picked71")
         forward(2, 0, HALF, first_half(0, HALF))
         place(2, 0, HALF)
         woven11 = held([P, HALF, PACK], BF16, name="woven11")
         weave_h(woven11[:], rows11[:])
         h11 = quantise(woven11, "h11")
-        forward(3, 0, HALF, first_half(0, HALF), square_after="woven01")
+        forward(3, 0, HALF, first_half(0, HALF), square_after="first_woven")
         place(3, 0, HALF)
 
         for n in range(N // P):

@@ -26,15 +26,17 @@ ROW0 = 96
 ROW = 8192
 
 PLACES = {
-    "page2": 0, "tab0": ROW - 64, "saved2": ROW, "saved6": ROW,
-    "page3": 2 * ROW, "tab1": 3 * ROW - 64, "saved3": 3 * ROW, "w2_raw0": 3 * ROW, "square70": 3 * ROW, "h01_codes": 3 * ROW,
+    "page2": 0, "tab0": ROW - 64, "saved2": ROW, "saved6": ROW, "w2_raw2": ROW, "y2_2_0": ROW, "woven11": ROW,
+    "page3": 2 * ROW, "tab1": 3 * ROW - 64, "saved3": 3 * ROW, "w1_raw1": 3 * ROW, "square60": 3 * ROW, "h00_codes": 3 * ROW,
+    "square70": 3 * ROW + 5120, "h01_codes": 3 * ROW + 4096, "square71": 3 * ROW + 6144,
     "saved0": 4 * ROW, "saved4": 4 * ROW, "saved7": 4 * ROW,
     "v_bytes": 5 * ROW - 512,
     "saved1": 5 * ROW + 64, "saved5": 5 * ROW + 64,
-    "w2_raw1": 5 * ROW, "gains": 5 * ROW + 4096,
-    "w2_raw2": 6 * ROW, "y2_2_0": 6 * ROW, "woven11": 6 * ROW,
+    "w2_raw0": 5 * ROW, "w2_raw1": 5 * ROW + 4096, "gains": 6 * ROW,
     "slopes00": 7 * ROW, "w1_cols0": 7 * ROW + 3072, "slopes01": 7 * ROW + 4096,
     "slopes10": 8 * ROW, "picked1": 8 * ROW + 2048, "squares11": 8 * ROW + 4096, "squares4": 8 * ROW + 4096,
+    "picked70": 9 * ROW + 3072, "rows10": 9 * ROW, "square61": 9 * ROW + 4096, "y2_0_0": 9 * ROW + 1536,
+    "w2_woven2": 9 * ROW, "y2_0_256": 9 * ROW + 2048, "y2_1_0": 9 * ROW + 2048, "w2_woven3": 9 * ROW + 2048,
 }
 FIRST_BANKS, SECOND_BANKS = 5, 3
 
@@ -93,7 +95,7 @@ def tile_list_hit_sensitivity_map_kernel(
                 w2_raw[n + e] = raw[:, :, :, P * e : P * (e + 1)]
 
         def load_w1(b):
-            w1_raw[b] = held([P, 2, PASS], I32, name="w1_raw%d" % b, after="w1_raw0")
+            w1_raw[b] = held([P, 2, PASS], I32, name="w1_raw%d" % b)
             words = w1_words.rearrange("a p c i -> p a (c i)").bitcast(I32)
             nc.sync.dma_start(out=w1_raw[b][:], in_=words[:, :, PASS * b : PASS * (b + 1)])
 
@@ -154,7 +156,6 @@ def tile_list_hit_sensitivity_map_kernel(
 
         order_w1(0)
         order_w1(1)
-        load_w1(1)
 
         banks = {}
         sums = {}
@@ -298,7 +299,7 @@ def tile_list_hit_sensitivity_map_kernel(
         pick(2, 1)
         load_saved(6)
         pick(3, 2)
-        load_w2(0, 1)
+        load_w1(1)
         squares11 = held([P, 2, HALF], F32, name="squares11")
         square(2, 0, pair_slot(2, 0))
         square(2, 1, squares11[:, 0, :])
@@ -309,33 +310,32 @@ def tile_list_hit_sensitivity_map_kernel(
         pair_slot(2, 1)
         less_one_scalar(squares11[:].rearrange("p t c -> p (t c)"), slopes[1, 1][:].rearrange("p t c -> p (t c)"))
         back_pair(1, 1, woven0[1][:])
-        order_w1(2)
-        order_w1(3)
         pick(4, 1)
         load_saved(7)
         square_whole(4, held([P, S], F32, name="squares4")[:])
         pick(5, 1)
+        load_w2(0, 1)
         load_w2(1, 1)
         gains = held([P, S], F32, name="gains")
         nc.sync.dma_start(out=gains[:], in_=wgo)
-        load_w2(2, 2)
         square_whole(5, picked[5])
         pick_half(6, 0)
         pick_half(6, 1)
+        load_w2(2, 2)
+        order_w1(2)
+        order_w1(3)
         square(6, 0, held([P, HALF], F32, name="square60")[:])
-        square(6, 1)
-        rows10 = held([P, PACK, HALF], BF16, name="rows10", after="picked60")
-        for u in range(PACK, 2 * PACK - 1):
-            first_sum(u, 0)
-            back(u, 0, rows10[:, u - PACK, :])
-        first = held([P, HALF, PACK], BF16, name="first_woven")
-        weave_w2(first[:, :QUARTER], 0)
         pick_half(7, 0)
         pick_half(7, 1)
         square(7, 0, held([P, HALF], F32, name="square70")[:])
-        first_sum(7, 0)
-        back(7, 0, rows10[:, PACK - 1, :])
-        h00 = quantise(woven0[0], "h00", after="picked70")
+        square(6, 1, held([P, HALF], F32, name="square61")[:])
+        rows10 = held([P, PACK, HALF], BF16, name="rows10")
+        for u in range(PACK, 2 * PACK):
+            first_sum(u, 0)
+            back(u, 0, rows10[:, u - PACK, :])
+        h00 = quantise(woven0[0], "h00")
+        first = held([P, HALF, PACK], BF16, name="first_woven")
+        weave_w2(first[:, :QUARTER], 0)
         codes = held([P, 2 * HALF], U32, name="last_codes")
         scale = held([P, 2 * HALF], U8, name="last_scale")
         w2_codes[0], w2_scale[0] = codes[:, :QUARTER], scale[:, :QUARTER]
@@ -352,10 +352,10 @@ def tile_list_hit_sensitivity_map_kernel(
         weave_w2(second[:, QUARTER:], 1)
         weave_h(first[:, QUARTER:], rows10[:, :, :QUARTER])
         quantise_part(first, 0)
+        square(7, 1, held([P, HALF], F32, name="square71")[:])
         weave_h(second[:, :QUARTER], rows10[:, :, QUARTER:])
         quantise_part(second, HALF)
-        square(7, 1, held([P, HALF], F32, name="square71", after="picked60")[:])
-        rows11 = held([P, PACK, HALF], BF16, name="rows11", after="first_woven")
+        rows11 = held([P, PACK, HALF], BF16, name="rows11", after="picked71")
         for u in range(PACK, 2 * PACK):
             first_sum(u, 1)
             back(u, 1, rows11[:, u - PACK, :])
@@ -364,26 +364,26 @@ def tile_list_hit_sensitivity_map_kernel(
             late = slice(QUARTER + lo, QUARTER + hi)
             return [(h00[0][:, lo:hi], h00[1][:, lo:hi]), (codes[:, late], scale[:, late])]
 
-        def finish_w2(n, after):
-            woven = held([P, QUARTER, PACK], BF16, name="w2_woven%d" % n, after=after)
+        def finish_w2(n):
+            woven = held([P, QUARTER, PACK], BF16, name="w2_woven%d" % n)
             weave_w2(woven[:], n)
             made = quantise(woven, "w2_%d" % n)
             w2_codes[n], w2_scale[n] = made[0][:], made[1][:]
 
-        forward(0, 0, QUARTER, first_half(0, QUARTER), square_after="picked71")
-        forward(0, QUARTER, HALF, first_half(QUARTER, HALF))
+        forward(0, 0, QUARTER, first_half(0, QUARTER))
         place(0, 0, QUARTER)
+        finish_w2(2)
+        forward(0, QUARTER, HALF, first_half(QUARTER, HALF))
         place(0, QUARTER, HALF)
-        finish_w2(2, after="y2_0_256")
-        forward(1, 0, HALF, first_half(0, HALF), square_after="picked71")
+        forward(1, 0, HALF, first_half(0, HALF))
         place(1, 0, HALF)
-        finish_w2(3, after="picked71")
+        finish_w2(3)
         forward(2, 0, HALF, first_half(0, HALF))
         place(2, 0, HALF)
         woven11 = held([P, HALF, PACK], BF16, name="woven11")
         weave_h(woven11[:], rows11[:])
         h11 = quantise(woven11, "h11")
-        forward(3, 0, HALF, first_half(0, HALF), square_after="first_woven")
+        forward(3, 0, HALF, first_half(0, HALF), square_after="picked71")
         place(3, 0, HALF)
 
         for n in range(N // P):

@@ -26,13 +26,14 @@ ROW0 = 96
 ROW = 8192
 
 PLACES = {
-    "page2": 0, "tab0": ROW - 64, "saved2": ROW, "saved6": ROW, "w2_raw2": ROW, "y2_2_0": ROW, "woven11": ROW,
-    "page3": 2 * ROW, "tab1": 3 * ROW - 64, "saved3": 3 * ROW, "w1_raw1": 3 * ROW, "square60": 3 * ROW, "h00_codes": 3 * ROW,
-    "square70": 3 * ROW + 5120, "h01_codes": 3 * ROW + 4096, "square71": 3 * ROW + 6144,
-    "saved0": 4 * ROW, "saved4": 4 * ROW, "saved7": 4 * ROW,
-    "v_bytes": 5 * ROW - 512,
-    "saved1": 5 * ROW + 64, "saved5": 5 * ROW + 64,
-    "w2_raw0": 5 * ROW, "w2_raw1": 5 * ROW + 4096, "gains": 6 * ROW,
+    "page2": 0, "tab0": ROW - 64, "saved1": ROW + 64, "saved5": ROW + 64,
+    "w2_raw0": ROW, "w2_raw1": ROW + 4096, "gains": 2 * ROW,
+    "page3": 2 * ROW + 4096, "tab1": 3 * ROW + 4096 - 64, "saved2": 3 * ROW + 4096, "saved6": 3 * ROW + 4096,
+    "w2_raw2": 3 * ROW + 4096, "y2_2_0": 3 * ROW + 4096, "woven11": 3 * ROW + 4096,
+    "saved0": 4 * ROW + 4096, "w1_bytes": 5 * ROW, "saved4": 4 * ROW + 4096, "saved7": 4 * ROW + 4096,
+    "v_bytes": 5 * ROW + 4096 - 512, "page1": 5 * ROW + 4096,
+    "w1_raw0": 10 * ROW, "saved3": 10 * ROW, "w1_raw1": 10 * ROW, "square60": 10 * ROW, "h00_codes": 10 * ROW,
+    "square70": 10 * ROW + 5120, "h01_codes": 10 * ROW + 4096, "square71": 10 * ROW + 6144,
     "slopes00": 7 * ROW, "w1_cols0": 7 * ROW + 3072, "slopes01": 7 * ROW + 4096,
     "slopes10": 8 * ROW, "picked1": 8 * ROW + 2048, "squares11": 8 * ROW + 4096, "squares4": 8 * ROW + 4096,
     "picked70": 9 * ROW + 3072, "rows10": 9 * ROW, "square61": 9 * ROW + 4096, "y2_0_0": 9 * ROW + 1536,
@@ -74,7 +75,6 @@ def tile_list_hit_sensitivity_map_kernel(
         new_page()
         warm = held([P, 1], F32, name="warm")
         nc.scalar.activation(warm[:], pages[0][:, 0:1], ACT.Ln, bias=1.0)
-        new_page()
 
         def rows_of(x, b):
             return x[PASS * b : PASS * (b + 1), :].rearrange("(p t) c -> p t c", t=PACK)
@@ -115,11 +115,12 @@ def tile_list_hit_sensitivity_map_kernel(
         v_bytes = held([P, S], U8, name="v_bytes")
         nc.vector.tensor_copy(v_bytes[:], tab_bytes[:].indirect(idx[:]))
         staged = held([P, S + H], U8, name="staged")
-        nc.vector.tensor_copy(
+        nc.gpsimd.tensor_copy(
             out=staged[:, S:].rearrange("p (b t g m) -> p b g t m", b=2, t=PACK, m=16),
             in_=w1_bytes[:].rearrange("p (b g m t) -> p b g t m", b=2, t=PACK, m=16),
         )
         nc.vector.tensor_copy(staged[:].bitcast(I32)[ROW0:, : S // 4], v_bytes[:].bitcast(I32)[ROW0:, :])
+        new_page()
 
         v_scale = []
         w1_scale = []
@@ -137,12 +138,11 @@ def tile_list_hit_sensitivity_map_kernel(
         lay_scales(0)
         load_saved(0)
         lay_scales(1)
-        load_saved(1)
         v_words = [held([P, S], U32, name="v_words%d" % a) for a in range(2)]
         for a in range(2):
             nc.vector.tensor_copy(v_words[a][:], tab[a][:].bitcast(U32).indirect(idx[:]))
             new_page()
-            load_saved(2 + a)
+            load_saved(1 + a)
 
         w1_cols = {}
 
@@ -156,6 +156,7 @@ def tile_list_hit_sensitivity_map_kernel(
 
         order_w1(0)
         order_w1(1)
+        load_saved(3)
 
         banks = {}
         sums = {}

@@ -33,13 +33,13 @@ PLACES = {
     "saved0": 4 * ROW + 4096, "w1_bytes": 5 * ROW, "saved4": 4 * ROW + 4096, "saved7": 4 * ROW + 4096,
     "v_bytes": 5 * ROW + 4096 - 512, "page1": 5 * ROW + 4096,
     "w1_raw0": 10 * ROW, "saved3": 10 * ROW, "w1_raw1": 10 * ROW, "square60": 10 * ROW, "h00_codes": 10 * ROW,
-    "square70": 10 * ROW + 5120, "h01_codes": 10 * ROW + 4096, "square71": 10 * ROW + 6144,
+    "square70": 10 * ROW + 5120, "square71": 10 * ROW + 6144,
     "slopes00": 7 * ROW, "w1_cols0": 7 * ROW + 3072, "slopes01": 7 * ROW + 4096,
     "slopes10": 8 * ROW, "picked1": 8 * ROW + 2048, "squares11": 8 * ROW + 4096, "squares4": 8 * ROW + 4096,
     "picked70": 9 * ROW + 3072, "rows10": 9 * ROW, "square61": 9 * ROW + 4096, "y2_0_0": 9 * ROW + 1536,
     "w2_woven2": 9 * ROW, "y2_0_256": 9 * ROW + 2048, "y2_1_0": 9 * ROW + 2048, "w2_woven3": 9 * ROW + 2048,
 }
-FIRST_BANKS, SECOND_BANKS = 5, 3
+FIRST_BANKS, SECOND_BANKS = 3, 4
 
 
 def tile_list_hit_sensitivity_map_kernel(
@@ -50,6 +50,7 @@ def tile_list_hit_sensitivity_map_kernel(
         keep = ctx.enter_context(tc.tile_pool(name="keep", bufs=1))
         laid = ctx.enter_context(tc.tile_pool(name="laid", bufs=1))
         psum1 = ctx.enter_context(tc.psum_pool(name="psum1", bufs=FIRST_BANKS))
+        psum_late = ctx.enter_context(tc.psum_pool(name="psum_late", bufs=1))
         psum2 = ctx.enter_context(tc.psum_pool(name="psum2", bufs=SECOND_BANKS))
 
         def held(shape, dtype, name, after=""):
@@ -166,8 +167,8 @@ def tile_list_hit_sensitivity_map_kernel(
         w2_scale = {}
         logs = {}
 
-        def first_sum(u, j):
-            acc = psum1.tile([P, HALF], F32, name="acc1")
+        def first_sum(u, j, pool=psum1):
+            acc = pool.tile([P, HALF], F32, name="acc1")
             for a in range(2):
                 nc.tensor.matmul_mx(
                     out=acc[:],
@@ -332,7 +333,7 @@ def tile_list_hit_sensitivity_map_kernel(
         square(6, 1, held([P, HALF], F32, name="square61")[:])
         rows10 = held([P, PACK, HALF], BF16, name="rows10")
         for u in range(PACK, 2 * PACK):
-            first_sum(u, 0)
+            first_sum(u, 0, psum_late if u == PACK else psum1)
             back(u, 0, rows10[:, u - PACK, :])
         h00 = quantise(woven0[0], "h00")
         first = held([P, HALF, PACK], BF16, name="first_woven")
@@ -348,7 +349,6 @@ def tile_list_hit_sensitivity_map_kernel(
                 out=codes[:, cols].bitcast(E4M3X4), scales=scale[:, cols], in_=woven[:].rearrange("p c t -> p (c t)")
             )
 
-        h01 = quantise(woven0[1], "h01")
         second = held([P, HALF, PACK], BF16, name="second_woven")
         weave_w2(second[:, QUARTER:], 1)
         weave_h(first[:, QUARTER:], rows10[:, :, :QUARTER])
@@ -356,9 +356,10 @@ def tile_list_hit_sensitivity_map_kernel(
         square(7, 1, held([P, HALF], F32, name="square71")[:])
         weave_h(second[:, :QUARTER], rows10[:, :, QUARTER:])
         quantise_part(second, HALF)
-        rows11 = held([P, PACK, HALF], BF16, name="rows11", after="picked71")
+        h01 = quantise(woven0[1], "h01", after="picked71")
+        rows11 = held([P, PACK, HALF], BF16, name="rows11")
         for u in range(PACK, 2 * PACK):
-            first_sum(u, 1)
+            first_sum(u, 1, psum1 if u % 2 else psum_late)
             back(u, 1, rows11[:, u - PACK, :])
 
         def first_half(lo, hi):
@@ -384,7 +385,7 @@ def tile_list_hit_sensitivity_map_kernel(
         woven11 = held([P, HALF, PACK], BF16, name="woven11")
         weave_h(woven11[:], rows11[:])
         h11 = quantise(woven11, "h11")
-        forward(3, 0, HALF, first_half(0, HALF), square_after="picked71")
+        forward(3, 0, HALF, first_half(0, HALF), square_after="rows11")
         place(3, 0, HALF)
 
         for n in range(N // P):

from contextlib import ExitStack

import concourse.mybir as mybir

K, H, N, T, S, T2 = 1024, 1024, 512, 2048, 1024, 2048
FLOPS = 2 * K * H * S + 2 * H * N * S

F32 = mybir.dt.float32
BF16 = mybir.dt.bfloat16
I32 = mybir.dt.int32
U32 = mybir.dt.uint32
U16 = mybir.dt.uint16
U8 = mybir.dt.uint8
E4M3X4 = mybir.dt.float8_e4m3fn_x4
E5M2X4 = mybir.dt.float8_e5m2_x4
ALU = mybir.AluOpType
ACT = mybir.ActivationFunctionType

P = 128
PACK = 4
PASS = P * PACK
HALF = S // 2
QUARTER = S // 4
GROUP = 16
ROW0 = 96
ROW = 8192

PLACES = {
    "page2": 0, "tab0": ROW - 64, "saved1": ROW + 64, "saved5": ROW + 64,
    "w2_raw0": ROW, "w2_raw1": ROW + 4096, "gains": 2 * ROW,
    "page3": 2 * ROW + 4096, "tab1": 3 * ROW + 4096 - 64, "saved2": 3 * ROW + 4096, "saved6": 3 * ROW + 4096,
    "w2_raw2": 3 * ROW + 4096, "y2_2_0": 3 * ROW + 4096, "woven11": 3 * ROW + 4096,
    "saved0": 4 * ROW + 4096, "w1_bytes": 5 * ROW, "saved4": 4 * ROW + 4096, "saved7": 4 * ROW + 4096,
    "v_bytes": 5 * ROW + 4096 - 512, "page1": 5 * ROW + 4096,
    "w1_raw0": 10 * ROW, "saved3": 10 * ROW, "w1_raw1": 10 * ROW, "square60": 10 * ROW, "h00_codes": 10 * ROW,
    "square70": 10 * ROW + 5120, "square71": 10 * ROW + 6144,
    "slopes00": 7 * ROW, "w1_cols0": 7 * ROW + 3072, "slopes01": 7 * ROW + 4096,
    "slopes10": 8 * ROW, "picked1": 8 * ROW + 2048, "squares11": 8 * ROW + 4096, "squares4": 8 * ROW + 4096,
    "picked70": 9 * ROW + 3072, "rows10": 9 * ROW, "square61": 9 * ROW + 4096, "y2_0_0": 9 * ROW + 1536,
    "w2_woven2": 9 * ROW, "y2_0_256": 9 * ROW + 2048, "y2_1_0": 9 * ROW + 2048, "w2_woven3": 9 * ROW + 2048,
}
FIRST_BANKS, SECOND_BANKS = 3, 4


def tile_list_hit_sensitivity_map_kernel(
    tc, tab_words, tab_scales, offs, w1_words, w1_scales, sT, w2, wgo, offs2, out
):
    nc = tc.nc
    with ExitStack() as ctx:
        keep = ctx.enter_context(tc.tile_pool(name="keep", bufs=1))
        laid = ctx.enter_context(tc.tile_pool(name="laid", bufs=1))
        psum1 = ctx.enter_context(tc.psum_pool(name="psum1", bufs=FIRST_BANKS))
        psum_late = ctx.enter_context(tc.psum_pool(name="psum_late", bufs=1))
        psum2 = ctx.enter_context(tc.psum_pool(name="psum2", bufs=SECOND_BANKS))

        def held(shape, dtype, name, after=""):
            if name in PLACES:
                return laid.tile(shape, dtype, name=name, offset=PLACES[name], align_bytes=64)
            return keep.tile(shape, dtype, name=name, tag=after or name, align_bytes=64)

        idx = keep.tile([P, S // GROUP], U16, name="idx")
        idx2 = keep.tile([P, S // GROUP], U16, name="idx2")

        tab_bytes = held([P, T], U8, name="tab_bytes")
        w1_bytes = held([P, H], U8, name="w1_bytes")
        nc.gpsimd.memset(tab_bytes[:].bitcast(I32)[:ROW0, :], 0)
        nc.gpsimd.memset(w1_bytes[:].bitcast(I32)[:ROW0, :], 0)

        pages = []

        def new_page():
            page = held([P, T2], F32, name="page%d" % len(pages))
            nc.gpsimd.memset(page[:], 0.0)
            pages.append(page)

        new_page()
        warm = held([P, 1], F32, name="warm")
        nc.scalar.activation(warm[:], pages[0][:, 0:1], ACT.Ln, bias=1.0)

        def rows_of(x, b):
            return x[PASS * b : PASS * (b + 1), :].rearrange("(p t) c -> p t c", t=PACK)

        saved = {}
        w2_raw = {}
        w1_raw = {}

        def load_saved(u):
            saved[u] = held([P, T], F32, name="saved%d" % u)
            nc.sync.dma_start(out=saved[u][:], in_=rows_of(sT, u // PACK)[:, u % PACK, :])

        def load_w2(n, count):
            raw = held([P, 2, PACK, P * count], F32, name="w2_raw%d" % n)
            for b in range(2):
                nc.sync.dma_start(out=raw[:, b], in_=rows_of(w2, b)[:, :, P * n : P * (n + count)])
            for e in range(count):
                w2_raw[n + e] = raw[:, :, :, P * e : P * (e + 1)]

        def load_w1(b):
            w1_raw[b] = held([P, 2, PASS], I32, name="w1_raw%d" % b)
            words = w1_words.rearrange("a p c i -> p a (c i)").bitcast(I32)
            nc.sync.dma_start(out=w1_raw[b][:], in_=words[:, :, PASS * b : PASS * (b + 1)])

        nc.sync.dma_start(idx[:], offs)
        nc.sync.dma_start(
            out=tab_bytes[:].bitcast(I32)[ROW0:, :], in_=tab_scales.rearrange("a q t -> (a q) t").bitcast(I32)
        )
        nc.sync.dma_start(
            out=w1_bytes[:].bitcast(I32)[ROW0:, :], in_=w1_scales.rearrange("a q c -> (a q) c").bitcast(I32)
        )
        nc.sync.dma_start(idx2[:], offs2)
        tab = [held([P, T], I32, name="tab%d" % a) for a in range(2)]
        for a in range(2):
            nc.sync.dma_start(out=tab[a][:], in_=tab_words[a].rearrange("p t i -> p (t i)").bitcast(I32))
        load_w1(0)

        v_bytes = held([P, S], U8, name="v_bytes")
        nc.vector.tensor_copy(v_bytes[:], tab_bytes[:].indirect(idx[:]))
        staged = held([P, S + H], U8, name="staged")
        nc.gpsimd.tensor_copy(
            out=staged[:, S:].rearrange("p (b t g m) -> p b g t m", b=2, t=PACK, m=16),
            in_=w1_bytes[:].rearrange("p (b g m t) -> p b g t m", b=2, t=PACK, m=16),
        )
        nc.vector.tensor_copy(staged[:].bitcast(I32)[ROW0:, : S // 4], v_bytes[:].bitcast(I32)[ROW0:, :])
        new_page()

        v_scale = []
        w1_scale = []

        def lay_scales(a):
            rows = held([P, (S + H) // 4], I32, name="plane%d" % a)
            for m in range(4):
                nc.sync.dma_start(
                    out=rows[m:P:32, :],
                    in_=staged[:].bitcast(I32)[ROW0 + 16 * a + m : ROW0 + 16 * (a + 1) : 4, :],
                )
            v_scale.append(rows[:].bitcast(U8)[:, :S])
            w1_scale.append(rows[:].bitcast(U8)[:, S:])

        lay_scales(0)
        load_saved(0)
        lay_scales(1)
        v_words = [held([P, S], U32, name="v_words%d" % a) for a in range(2)]
        for a in range(2):
            nc.vector.tensor_copy(v_words[a][:], tab[a][:].bitcast(U32).indirect(idx[:]))
            new_page()
            load_saved(1 + a)

        w1_cols = {}

        def order_w1(q):
            w1_cols[q] = held([P, 2, 2 * P], U32, name="w1_cols%d" % q)
            e = 2 * (q % 2)
            nc.scalar.copy(
                out=w1_cols[q][:].rearrange("p a (t g m) -> p a g t m", t=2, m=4),
                in_=w1_raw[q // 2][:].bitcast(U32).rearrange("p a (g m t) -> p a g t m", t=PACK, m=4)[:, :, :, e : e + 2, :],
            )

        order_w1(0)
        order_w1(1)
        load_saved(3)

        banks = {}
        sums = {}
        slopes = {}
        picked = {}
        w2_codes = {}
        w2_scale = {}
        logs = {}

        def first_sum(u, j, pool=psum1):
            acc = pool.tile([P, HALF], F32, name="acc1")
            for a in range(2):
                nc.tensor.matmul_mx(
                    out=acc[:],
                    lhsT=w1_cols[u // 2][:, a, P * (u % 2) : P * (u % 2 + 1)].bitcast(E4M3X4),
                    lhsT_scale=w1_scale[a][:, P * u : P * (u + 1)],
                    rhs=v_words[a][:, HALF * j : HALF * (j + 1)].bitcast(E5M2X4),
                    rhs_scale=v_scale[a][:, HALF * j : HALF * (j + 1)],
                    start=(a == 0),
                    stop=(a == 1),
                )
            banks[u, j] = acc

        def empty(u, j):
            first_sum(u, j)
            if u % 2 == 0:
                sums[u // 2, j] = held([P, 2, HALF], F32, name="sums%d%d" % (u // 2, j))
            nc.scalar.copy(out=sums[u // 2, j][:, u % 2, :], in_=banks[u, j][:])

        def pair_slot(u, j, after=""):
            if (u // 2, j) not in slopes:
                slopes[u // 2, j] = held([P, 2, HALF], F32, name="slopes%d%d" % (u // 2, j), after=after)
            return slopes[u // 2, j][:, u % 2, :]

        def pick(u, pieces):
            whole = held([P, S], F32, name="picked%d" % u)
            width = S // pieces
            for lo in range(0, S, width):
                nc.vector.tensor_copy(
                    whole[:, lo : lo + width], saved[u][:].indirect(idx[:, lo // GROUP : (lo + width) // GROUP])
                )
            picked[u] = whole[:]
            for j in range(2):
                picked[u, j] = whole[:, HALF * j : HALF * (j + 1)]

        def pick_half(u, j):
            picked[u, j] = held([P, HALF], F32, name="picked%d%d" % (u, j))[:]
            lo = HALF * j // GROUP
            nc.vector.tensor_copy(picked[u, j], saved[u][:].indirect(idx[:, lo : lo + HALF // GROUP]))

        def square(u, j, into=None):
            target = picked[u, j] if into is None else into
            nc.scalar.activation(target, picked[u, j], ACT.Square)
            picked[u, j] = target

        def square_whole(u, into):
            nc.scalar.activation(into, picked[u], ACT.Square)
            for j in range(2):
                picked[u, j] = into[:, HALF * j : HALF * (j + 1)]

        def less_one_gpsimd(x, into=None):
            nc.gpsimd.tensor_scalar(x if into is None else into, x, 1.0, -1.0, ALU.mult, ALU.add)

        def less_one_scalar(x, into=None):
            nc.scalar.activation(x if into is None else into, x, ACT.Identity, bias=-1.0)

        def by_fours(x, order):
            return x.rearrange(order + " -> p c t i", i=4)

        def back_pair(q, j, woven, cols=slice(0, HALF)):
            e = 2 * (q % 2)
            nc.gpsimd.tensor_tensor(
                woven[:, :, e : e + 2],
                slopes[q, j][:, :, cols].rearrange("p t c -> p c t"),
                sums[q, j][:, :, cols].rearrange("p t c -> p c t"),
                ALU.mult,
            )

        def back(u, j, row):
            nc.vector.scalar_tensor_tensor(
                out=row, in0=picked[u, j], scalar=1.0, in1=banks[u, j][:], op0=ALU.subtract, op1=ALU.mult
            )

        def weave_h(woven, rows, copy=nc.scalar.copy):
            copy(out=by_fours(woven, "p (c i) t"), in_=by_fours(rows, "p t (c i)"))

        def weave_w2(woven, n):
            nc.scalar.copy(
                out=woven.rearrange("p (b c i) t -> p b c t i", b=2, i=4),
                in_=w2_raw[n].rearrange("p b t (c i) -> p b c t i", i=4),
            )

        def quantise(woven, name, after=""):
            width = woven.shape[1]
            codes = held([P, width], U32, name=name + "_codes", after=after)
            scale = held([P, width], U8, name=name + "_scale")
            nc.vector.quantize_mx(
                out=codes[:].bitcast(E4M3X4), scales=scale[:], in_=woven[:].rearrange("p c t -> p (c t)")
            )
            return codes, scale

        def forward(n, lo, hi, operands, square_after=""):
            acc = psum2.tile([P, hi - lo], F32, name="acc2")
            for b in range(2):
                nc.tensor.matmul_mx(
                    out=acc[:],
                    lhsT=w2_codes[n][:, P * b : P * (b + 1)].bitcast(E4M3X4),
                    lhsT_scale=w2_scale[n][:, P * b : P * (b + 1)],
                    rhs=operands[b][0].bitcast(E4M3X4),
                    rhs_scale=operands[b][1],
                    start=(b == 0),
                    stop=(b == 1),
                )
            y2 = held([P, hi - lo], F32, name="y2_%d_%d" % (n, lo), after=square_after)
            nc.scalar.activation(y2[:], acc[:], ACT.Square)
            logs[n, lo] = held([P, hi - lo], F32, name="logs_%d_%d" % (n, lo))
            nc.scalar.activation(logs[n, lo][:], y2[:], ACT.Ln, bias=1.0)

        def place(n, lo, hi):
            nc.vector.tensor_tensor(
                pages[n][:].indirect(idx2[:, lo // GROUP : hi // GROUP]), logs[n, lo][:], gains[:, lo:hi], ALU.mult
            )

        woven0 = [held([P, HALF, PACK], BF16, name="woven0%d" % j) for j in range(2)]

        for u, j in ((0, 0), (1, 0), (0, 1), (1, 1), (2, 0), (3, 0)):
            empty(u, j)
        pick(0, 1)
        load_saved(4)
        pick(1, 2)
        load_saved(5)
        for u, j in ((0, 0), (0, 1), (1, 0), (1, 1)):
            square(u, j, pair_slot(u, j))
        for u, j in ((0, 0), (0, 1), (1, 0)):
            less_one_gpsimd(picked[u, j])
        empty(2, 1)
        empty(3, 1)
        less_one_scalar(picked[1, 1])
        back_pair(0, 0, woven0[0][:])
        back_pair(0, 1, woven0[1][:])
        pick(2, 1)
        load_saved(6)
        pick(3, 2)
        load_w1(1)
        squares11 = held([P, 2, HALF], F32, name="squares11")
        square(2, 0, pair_slot(2, 0))
        square(2, 1, squares11[:, 0, :])
        square(3, 0, pair_slot(3, 0))
        square(3, 1, squares11[:, 1, :])
        less_one_scalar(slopes[1, 0][:].rearrange("p t c -> p (t c)"))
        back_pair(1, 0, woven0[0][:])
        pair_slot(2, 1)
        less_one_scalar(squares11[:].rearrange("p t c -> p (t c)"), slopes[1, 1][:].rearrange("p t c -> p (t c)"))
        back_pair(1, 1, woven0[1][:])
        pick(4, 1)
        load_saved(7)
        square_whole(4, held([P, S], F32, name="squares4")[:])
        pick(5, 1)
        load_w2(0, 1)
        load_w2(1, 1)
        gains = held([P, S], F32, name="gains")
        nc.sync.dma_start(out=gains[:], in_=wgo)
        square_whole(5, picked[5])
        pick_half(6, 0)
        pick_half(6, 1)
        load_w2(2, 2)
        order_w1(2)
        order_w1(3)
        square(6, 0, held([P, HALF], F32, name="square60")[:])
        pick_half(7, 0)
        pick_half(7, 1)
        square(7, 0, held([P, HALF], F32, name="square70")[:])
        square(6, 1, held([P, HALF], F32, name="square61")[:])
        rows10 = held([P, PACK, HALF], BF16, name="rows10")
        for u in range(PACK, 2 * PACK):
            first_sum(u, 0, psum_late if u == PACK else psum1)
            back(u, 0, rows10[:, u - PACK, :])
        h00 = quantise(woven0[0], "h00")
        first = held([P, HALF, PACK], BF16, name="first_woven")
        weave_w2(first[:, :QUARTER], 0)
        codes = held([P, 2 * HALF], U32, name="last_codes")
        scale = held([P, 2 * HALF], U8, name="last_scale")
        w2_codes[0], w2_scale[0] = codes[:, :QUARTER], scale[:, :QUARTER]
        w2_codes[1], w2_scale[1] = codes[:, 3 * QUARTER :], scale[:, 3 * QUARTER :]

        def quantise_part(woven, lo):
            cols = slice(lo, lo + woven.shape[1])
            nc.vector.quantize_mx(
                out=codes[:, cols].bitcast(E4M3X4), scales=scale[:, cols], in_=woven[:].rearrange("p c t -> p (c t)")
            )

        second = held([P, HALF, PACK], BF16, name="second_woven")
        weave_w2(second[:, QUARTER:], 1)
        weave_h(first[:, QUARTER:], rows10[:, :, :QUARTER])
        quantise_part(first, 0)
        square(7, 1, held([P, HALF], F32, name="square71")[:])
        weave_h(second[:, :QUARTER], rows10[:, :, QUARTER:])
        quantise_part(second, HALF)
        h01 = quantise(woven0[1], "h01", after="picked71")
        rows11 = held([P, PACK, HALF], BF16, name="rows11")
        for u in range(PACK, 2 * PACK):
            first_sum(u, 1, psum1 if u % 2 else psum_late)
            back(u, 1, rows11[:, u - PACK, :])

        def first_half(lo, hi):
            late = slice(QUARTER + lo, QUARTER + hi)
            return [(h00[0][:, lo:hi], h00[1][:, lo:hi]), (codes[:, late], scale[:, late])]

        def finish_w2(n):
            woven = held([P, QUARTER, PACK], BF16, name="w2_woven%d" % n)
            weave_w2(woven[:], n)
            made = quantise(woven, "w2_%d" % n)
            w2_codes[n], w2_scale[n] = made[0][:], made[1][:]

        forward(0, 0, QUARTER, first_half(0, QUARTER))
        place(0, 0, QUARTER)
        finish_w2(2)
        forward(0, QUARTER, HALF, first_half(QUARTER, HALF))
        place(0, QUARTER, HALF)
        forward(1, 0, HALF, first_half(0, HALF))
        place(1, 0, HALF)
        finish_w2(3)
        forward(2, 0, HALF, first_half(0, HALF))
        place(2, 0, HALF)
        woven11 = held([P, HALF, PACK], BF16, name="woven11")
        weave_h(woven11[:], rows11[:])
        h11 = quantise(woven11, "h11")
        forward(3, 0, HALF, first_half(0, HALF), square_after="rows11")
        place(3, 0, HALF)

        for n in range(N // P):
            forward(n, HALF, S, [(h01[0][:], h01[1][:]), (h11[0][:], h11[1][:])])
            place(n, HALF, S)
            nc.sync.dma_start(out=out[P * n : P * (n + 1), :], in_=pages[n][:])
